import numpy as np
import ml_dtypes


def mxq(x, axis, fmt="e4m3"):
    dtype, down = {"e4m3": (ml_dtypes.float8_e4m3fn, 7), "e5m2": (ml_dtypes.float8_e5m2, 14)}[fmt]
    v = np.moveaxis(np.asarray(x, np.float32).astype(ml_dtypes.bfloat16).astype(np.float64), axis, -1)
    blocks = v.reshape(v.shape[:-1] + (-1, 32))
    amax = np.abs(blocks).max(-1, keepdims=True)
    byte = np.maximum(np.where(amax > 0, np.frexp(amax)[1] - 1 + 127, 0) - down, 1)
    scale = np.exp2(byte - 127.0)
    codes = (blocks / scale).astype(np.float32).astype(dtype).astype(np.float64)
    return np.moveaxis((codes * scale).reshape(v.shape), -1, axis)


WIDE = False


def mx_kscale(k):
    if not WIDE:
        return np.ones(k)
    levels = np.array([10, -10, 5, -5, 0])
    if k % 512:
        return np.exp2(np.random.permutation(np.resize(levels, k // 32))).repeat(32)
    a = np.empty((k // 512, 16))
    for p in range(k // 512):
        a[p, :8] = np.random.permutation(np.resize(levels, 8))
        for g in range(8):
            far = levels[np.abs(levels - a[p, g]) >= 10]
            a[p, g + 8] = far[np.random.randint(len(far))]
    return np.exp2(a.ravel()).repeat(32)


def f64(x):
    return np.asarray(x).astype(np.float64)


def striped(idx):
    return np.tile(idx.reshape(-1, 16).T, (8, 1)).astype(np.uint16)


def unstriped(offs):
    return offs[:16].T.reshape(-1).astype(np.int64)


E2M1 = np.array([0.0, 0.5, 1.0, 1.5, 2.0, 3.0, 4.0, 6.0, -0.0, -0.5, -1.0, -1.5, -2.0, -3.0, -4.0, -6.0])


def pack_fp4(w):
    k, n = w.shape
    w = f64(np.asarray(w, np.float32).astype(ml_dtypes.bfloat16)).reshape(k // 32, 32, n)
    amax = np.abs(w).max(1)
    mant, ex = np.frexp(amax / 6.0)
    byte = np.clip(np.where(amax > 0, np.where(mant > 0.5, ex, ex - 1) + 127, 1), 1, 254)
    scaled = (w * np.exp2(127.0 - byte)[:, None, :]).reshape(k, n).astype(np.float32)
    c = np.ascontiguousarray(scaled.reshape(k // 512, 128, 4, n).transpose(0, 1, 3, 2)).astype(ml_dtypes.float4_e2m1fn).view(np.uint8) & 0xF
    words = (c[..., 0::2] | (c[..., 1::2] << 4)).reshape(k // 512, 128, 2 * n)
    return np.ascontiguousarray(words), np.ascontiguousarray(byte.astype(np.uint8).reshape(k // 512, 16, n))


def unpack_fp4(words, scales):
    g, _, n = scales.shape
    words = np.ascontiguousarray(words).reshape(g, 128, n, 2)
    nib = np.empty((g, 128, n, 4), np.uint8)
    nib[..., 0::2] = words & 0xF
    nib[..., 1::2] = words >> 4
    vals = E2M1[nib] * np.repeat(np.exp2(scales.astype(np.float64) - 127.0), 8, axis=1)[..., None]
    return vals.transpose(0, 1, 3, 2).reshape(g * 512, n)


def relu(v):
    return np.maximum(v, 0.0)


K, T, S, H, N = 1024, 2048, 1024, 512, 128


def setup_inputs():
    n = np.random.standard_normal
    s = mx_kscale(K)[:, None]
    u = mx_kscale(H)
    packed_w2 = pack_fp4(n((H, N)) / np.sqrt(H) / u[:, None])
    return {
        "xT": (n((K, T)) * s).astype(np.float32),
        "w1": (n((K, H)) / np.sqrt(K) / s * u).astype(np.float32),
        "w2_words": packed_w2[0],
        "w2_scales": packed_w2[1],
        "offs": striped(np.random.permutation(T)[:S]),
    }


def reference(xT, w1, w2_words, w2_scales, offs):
    xq = mxq(f64(xT)[:, unstriped(offs)], 0, "e4m3")
    h = relu(mxq(f64(w1), 0, "e4m3").T @ xq)
    z = h - h.mean(axis=1, keepdims=True)
    return unpack_fp4(w2_words, w2_scales).T @ mxq(z, 0, "e4m3")

@@ -1,0 +1,247 @@
+from contextlib import ExitStack
+
+import concourse.mybir as mybir
+
+K, T, S, H, N = 1024, 2048, 1024, 512, 128
+FLOPS = 2 * S * H * (K + N)
+
+F32 = mybir.dt.float32
+BF16 = mybir.dt.bfloat16
+I32 = mybir.dt.int32
+U32 = mybir.dt.uint32
+U16 = mybir.dt.uint16
+U8 = mybir.dt.uint8
+FP8X4 = mybir.dt.float8_e4m3fn_x4
+FP4X4 = mybir.dt.float4_e2m1fn_x4
+ACT = mybir.ActivationFunctionType
+ALU = mybir.AluOpType
+
+P = 128
+PACK = 4
+K_PASS = P * PACK
+PASSES = K // K_PASS
+HALF = S // 2
+X_CHUNKS = (((512, 192),) * 4, ((512, 128), (512, 128), (512, 256), (256, 96), (256, 96)))
+W_PARTS = 2
+Z_WIDTH = 256
+
+
+def tile_picked_deepset_relu_e_kernel(tc, xT, w1, w2_words, w2_scales, offs, out):
+    nc = tc.nc
+    with ExitStack() as ctx:
+        keep = ctx.enter_context(tc.tile_pool(name="keep", bufs=1))
+        psum = ctx.enter_context(tc.psum_pool(name="psum", bufs=1))
+
+        offsets = keep.tile([P, S // 16], U16, name="offsets")
+        x_scales = keep.tile([P, T], U8, name="x_scales", align_bytes=64)
+        nc.vector.memset(x_scales[:].bitcast(I32), 0)
+        w2_plane = keep.tile([P, N], U8, name="w2_plane", align_bytes=64)
+        w2_codes = keep.tile([P, 2 * N], U8, name="w2_codes", align_bytes=64)
+        nc.vector.memset(w2_plane[:].bitcast(I32), 0)
+        inv_count = keep.tile([P, HALF], F32, name="inv_count")
+        nc.vector.memset(inv_count[:], 1.0 / S)
+
+        x_raw = {}
+        for g in range(PASSES):
+            rows = xT[g * K_PASS : (g + 1) * K_PASS, :].rearrange("(p j) c -> p j c", j=PACK)
+            c0 = 0
+            for width, share in X_CHUNKS[g]:
+                raw = keep.tile([P, PACK, width], F32, name="x_raw_%d_%d" % (g, c0))
+                nc.sync.dma_start(out=raw[:], in_=rows[:, :, c0 : c0 + width])
+                x_raw[g, c0] = raw
+                if g == 0 and c0 == 0:
+                    nc.sync.dma_start(offsets[:], offs)
+                c0 = c0 + width
+        w_raw = {}
+        part = H // W_PARTS
+        for g in range(PASSES):
+            rows = w1[g * K_PASS : (g + 1) * K_PASS, :].rearrange("(p j) c -> p j c", j=PACK)
+            for a in range(W_PARTS):
+                raw = keep.tile([P, PACK, part], F32, name="w_raw_%d_%d" % (g, a))
+                nc.sync.dma_start(out=raw[:], in_=rows[:, :, a * part : (a + 1) * part])
+                w_raw[g, a] = raw
+        nc.sync.dma_start(out=w2_codes[:].bitcast(I32), in_=w2_words[0].bitcast(I32))
+        for q in range(4):
+            nc.sync.dma_start(out=w2_plane[32 * q : 32 * q + 4, :].bitcast(I32), in_=w2_scales[0, 4 * q : 4 * q + 4, :].bitcast(I32))
+
+        def interleave(engine, dst, src):
+            dst = dst.rearrange("p (c i) j -> p c j i", i=4)
+            src = src.rearrange("p j (c i) -> p c j i", i=4)
+            if engine == "vector":
+                nc.vector.tensor_copy(out=dst, in_=src)
+            else:
+                nc.scalar.activation(out=dst, in_=src, func=ACT.Copy)
+
+        x_words = [keep.tile([P, T], U32, name="x_words_%d" % g, align_bytes=64) for g in range(PASSES)]
+        got_words = {}
+        got_scales = {}
+
+        def gather_words(g, half, tag):
+            got = keep.tile([P, HALF], U32, name="got_words_%d_%d" % (g, half), tag=tag, align_bytes=64)
+            nc.vector.tensor_copy(got[:], x_words[g][:].indirect(offsets[:, half * 32 : (half + 1) * 32]))
+            got_words[g, half] = got
+
+        def gather_scales(half):
+            got = keep.tile([P, HALF], U8, name="got_scales_%d" % half, align_bytes=64)
+            nc.vector.tensor_copy(got[:], x_scales[:].indirect(offsets[:, half * 32 : (half + 1) * 32]))
+            got_scales[half] = got
+
+        for g in range(PASSES):
+            c0 = 0
+            for width, share in X_CHUNKS[g]:
+                raw = x_raw[g, c0]
+                grouped = keep.tile([P, width, PACK], BF16, name="x_bf_%d_%d" % (g, c0), align_bytes=64)
+                interleave("vector", grouped[:, :share, :], raw[:, :, :share])
+                interleave("scalar", grouped[:, share:, :], raw[:, :, share:])
+                step = min(width, 512)
+                for s0 in range(0, width, step):
+                    cols = slice(c0 + s0, c0 + s0 + step)
+                    nc.vector.quantize_mx(
+                        out=x_words[g][:, cols].bitcast(FP8X4),
+                        scales=x_scales[4 * g :, cols],
+                        in_=grouped[:, s0 : s0 + step, :].rearrange("p c j -> p (c j)"),
+                    )
+                c0 = c0 + width
+            if g == 0:
+                gather_words(0, 0, "got_0_0")
+                gather_words(0, 1, "got_0_1")
+
+        w_words = {}
+        w_scales = {}
+
+        def round_w(g):
+            grouped = keep.tile([P, PACK, P, PACK], BF16, name="w_bf_%d" % g, tag="w_bf_%d" % g, align_bytes=64)
+            m_part = P // W_PARTS
+            for a in range(W_PARTS):
+                nc.scalar.activation(
+                    out=grouped[:, :, a * m_part : (a + 1) * m_part, :].rearrange("p t m j -> p m j t"),
+                    in_=w_raw[g, a][:].rearrange("p j (m t) -> p m j t", t=PACK),
+                    func=ACT.Copy,
+                )
+            return grouped
+
+        def quantize_w(g, grouped):
+            w_words[g] = keep.tile([P, H], U32, name="w_words_%d" % g, align_bytes=64)
+            w_scales[g] = keep.tile([P, H], U8, name="w_scales_%d" % g, align_bytes=64)
+            for t in range(PACK):
+                cols = slice(t * P, (t + 1) * P)
+                nc.vector.quantize_mx(
+                    out=w_words[g][:, cols].bitcast(FP8X4),
+                    scales=w_scales[g][:, cols],
+                    in_=grouped[:, t, :, :].rearrange("p m j -> p (m j)"),
+                )
+
+        w_bf = [round_w(g) for g in range(PASSES)]
+        gather_scales(0)
+        gather_scales(1)
+        quantize_w(0, w_bf[0])
+        gather_words(1, 0, "w_bf_0")
+        quantize_w(1, w_bf[1])
+        gather_words(1, 1, "w_bf_1")
+
+        banks = {}
+        for half in range(2):
+            for t in range(PACK):
+                banks[t, half] = psum.tile([P, HALF], F32, name="bank_%d" % (2 * t + half))
+
+        def product(g, t, half):
+            cols = slice(t * P, (t + 1) * P)
+            nc.tensor.matmul_mx(
+                out=banks[t, half][:],
+                lhsT=w_words[g][:, cols].bitcast(FP8X4),
+                lhsT_scale=w_scales[g][:, cols],
+                rhs=got_words[g, half][:].bitcast(FP8X4),
+                rhs_scale=got_scales[half][4 * g :, :],
+                start=(g == 0),
+                stop=(g == PASSES - 1),
+            )
+
+        for half in range(2):
+            for t in range(PACK):
+                product(0, t, half)
+
+        h = [keep.tile([P, PACK, HALF], F32, name="h_%d" % half) for half in range(2)]
+        mean_part = [keep.tile([P, PACK], F32, name="mean_part_%d" % half) for half in range(2)]
+        for half in range(2):
+            for t in range(PACK):
+                product(1, t, half)
+                if half == 0 or t == PACK - 1:
+                    nc.scalar.activation(
+                        out=h[half][:, t, :], in_=banks[t, half][:], func=ACT.Relu, scale=1.0 / S,
+                        accum_out=mean_part[half][:, t : t + 1],
+                    )
+                else:
+                    nc.vector.scalar_tensor_tensor(
+                        out=h[half][:, t, :], in0=banks[t, half][:], scalar=0.0, in1=inv_count[:], op0=ALU.max, op1=ALU.mult,
+                        accum_out=mean_part[half][:, t : t + 1],
+                    )
+        neg_mean = keep.tile([P, PACK], F32, name="neg_mean")
+        nc.vector.scalar_tensor_tensor(
+            out=neg_mean[:], in0=mean_part[0][:], scalar=-1.0, in1=mean_part[1][:], op0=ALU.mult, op1=ALU.subtract
+        )
+
+        def center(engine, c0, width):
+            half, h0 = divmod(c0, HALF)
+            planes = keep.tile([P, PACK, width], BF16, name="z_planes_%d" % c0)
+            for t in range(PACK):
+                src = h[half][:, t, h0 : h0 + width]
+                if engine == "vector":
+                    nc.vector.tensor_scalar(
+                        out=planes[:, t, :], in0=src, scalar1=float(S), scalar2=neg_mean[:, t : t + 1], op0=ALU.mult, op1=ALU.add
+                    )
+                else:
+                    nc.scalar.activation(
+                        out=planes[:, t, :], in_=src, func=ACT.Identity, bias=neg_mean[:, t : t + 1], scale=float(S)
+                    )
+            return planes
+
+        def weave(engine, c0, width, planes):
+            grouped = keep.tile([P, width, PACK], BF16, name="z_bf_%d" % c0, align_bytes=64)
+            interleave(engine, grouped[:], planes)
+            return grouped
+
+        def finish(engine, c0, width, grouped):
+            z_words = keep.tile([P, width], U32, name="z_words_%d" % c0, align_bytes=64)
+            z_scales = keep.tile([P, width], U8, name="z_scales_%d" % c0, align_bytes=64)
+            nc.vector.quantize_mx(
+                out=z_words[:].bitcast(FP8X4), scales=z_scales[:], in_=grouped[:].rearrange("p c j -> p (c j)")
+            )
+            acc = psum.tile([P, width], F32, name="bank_%d" % (c0 // P))
+            nc.tensor.matmul_mx(
+                out=acc[:],
+                lhsT=w2_codes[:].bitcast(FP4X4),
+                lhsT_scale=w2_plane[:],
+                rhs=z_words[:].bitcast(FP8X4),
+                rhs_scale=z_scales[:],
+                start=True,
+                stop=True,
+            )
+            return acc
+
+        def store(engine, c0, width, acc):
+            result = keep.tile([P, width], F32, name="result_%d" % c0)
+            if engine == "vector":
+                nc.vector.tensor_copy(out=result[:], in_=acc[:])
+            else:
+                nc.scalar.activation(out=result[:], in_=acc[:], func=ACT.Copy)
+            nc.sync.dma_start(out=out[:, c0 : c0 + width], in_=result[:])
+
+        own = center("vector", 640, 384)
+        first = center("scalar", 0, 256)
+        second = center("scalar", 256, 256)
+        third = center("scalar", 512, 128)
+        third_bf = weave("scalar", 512, 128, third[:])
+        a_bf = weave("vector", 640, 128, own[:, :, 0:128])
+        b_bf = weave("vector", 768, 256, own[:, :, 128:384])
+        first_bf = weave("vector", 0, 256, first[:])
+        acc_a = finish("vector", 640, 128, a_bf)
+        acc_b = finish("vector", 768, 256, b_bf)
+        acc_first = finish("vector", 0, 256, first_bf)
+        second_bf = weave("vector", 256, 256, second[:])
+        acc_third = finish("vector", 512, 128, third_bf)
+        acc_second = finish("vector", 256, 256, second_bf)
+        store("scalar", 640, 128, acc_a)
+        store("scalar", 768, 256, acc_b)
+        store("scalar", 0, 256, acc_first)
+        store("vector", 512, 128, acc_third)
+        store("scalar", 256, 256, acc_second)

@@ -21,9 +21,12 @@ PACK = 4
 K_PASS = P * PACK
 PASSES = K // K_PASS
 HALF = S // 2
-X_CHUNKS = (((512, 192),) * 4, ((512, 128), (512, 128), (512, 256), (256, 96), (256, 96)))
-W_PARTS = 2
-Z_WIDTH = 256
+X_CHUNKS = (
+    ((640, (512, 512, 256)), (384, (256, 256, 256))),
+    ((512, (512, 256, 256, 128)), (384, (256, 256, 128)), (128, (256,))),
+)
+W_SHARE = (0, 24)
+WARM_PASSES = 8
 
 
 def tile_picked_deepset_relu_e_kernel(tc, xT, w1, w2_words, w2_scales, offs, out):
@@ -38,14 +41,18 @@ def tile_picked_deepset_relu_e_kernel(tc, xT, w1, w2_words, w2_scales, offs, out
         w2_plane = keep.tile([P, N], U8, name="w2_plane", align_bytes=64)
         w2_codes = keep.tile([P, 2 * N], U8, name="w2_codes", align_bytes=64)
         nc.vector.memset(w2_plane[:].bitcast(I32), 0)
-        inv_count = keep.tile([P, HALF], F32, name="inv_count")
-        nc.vector.memset(inv_count[:], 1.0 / S)
+
+        table_in = keep.tile([P, 1], F32, name="table_in")
+        table_out = keep.tile([P, 1], F32, name="table_out")
+        nc.vector.memset(table_in[:], 0.0)
+        nc.scalar.activation(out=table_out[:], in_=table_in[:], func=ACT.Relu)
 
         x_raw = {}
         for g in range(PASSES):
             rows = xT[g * K_PASS : (g + 1) * K_PASS, :].rearrange("(p j) c -> p j c", j=PACK)
             c0 = 0
-            for width, share in X_CHUNKS[g]:
+            for share, slices in X_CHUNKS[g]:
+                width = sum(slices)
                 raw = keep.tile([P, PACK, width], F32, name="x_raw_%d_%d" % (g, c0))
                 nc.sync.dma_start(out=raw[:], in_=rows[:, :, c0 : c0 + width])
                 x_raw[g, c0] = raw
@@ -53,13 +60,11 @@ def tile_picked_deepset_relu_e_kernel(tc, xT, w1, w2_words, w2_scales, offs, out
                     nc.sync.dma_start(offsets[:], offs)
                 c0 = c0 + width
         w_raw = {}
-        part = H // W_PARTS
         for g in range(PASSES):
             rows = w1[g * K_PASS : (g + 1) * K_PASS, :].rearrange("(p j) c -> p j c", j=PACK)
-            for a in range(W_PARTS):
-                raw = keep.tile([P, PACK, part], F32, name="w_raw_%d_%d" % (g, a))
-                nc.sync.dma_start(out=raw[:], in_=rows[:, :, a * part : (a + 1) * part])
-                w_raw[g, a] = raw
+            raw = keep.tile([P, PACK, H], F32, name="w_raw_%d" % g)
+            nc.sync.dma_start(out=raw[:], in_=rows)
+            w_raw[g] = raw
         nc.sync.dma_start(out=w2_codes[:].bitcast(I32), in_=w2_words[0].bitcast(I32))
         for q in range(4):
             nc.sync.dma_start(out=w2_plane[32 * q : 32 * q + 4, :].bitcast(I32), in_=w2_scales[0, 4 * q : 4 * q + 4, :].bitcast(I32))
@@ -81,27 +86,37 @@ def tile_picked_deepset_relu_e_kernel(tc, xT, w1, w2_words, w2_scales, offs, out
             nc.vector.tensor_copy(got[:], x_words[g][:].indirect(offsets[:, half * 32 : (half + 1) * 32]))
             got_words[g, half] = got
 
-        def gather_scales(half):
+        def gather_scales(half, pieces):
             got = keep.tile([P, HALF], U8, name="got_scales_%d" % half, align_bytes=64)
-            nc.vector.tensor_copy(got[:], x_scales[:].indirect(offsets[:, half * 32 : (half + 1) * 32]))
+            step = HALF // pieces
+            for s0 in range(0, HALF, step):
+                entry = half * HALF + s0
+                nc.vector.tensor_copy(got[:, s0 : s0 + step], x_scales[:].indirect(offsets[:, entry // 16 : (entry + step) // 16]))
             got_scales[half] = got
 
         for g in range(PASSES):
             c0 = 0
-            for width, share in X_CHUNKS[g]:
+            for share, slices in X_CHUNKS[g]:
                 raw = x_raw[g, c0]
-                grouped = keep.tile([P, width, PACK], BF16, name="x_bf_%d_%d" % (g, c0), align_bytes=64)
-                interleave("vector", grouped[:, :share, :], raw[:, :, :share])
-                interleave("scalar", grouped[:, share:, :], raw[:, :, share:])
-                step = min(width, 512)
-                for s0 in range(0, width, step):
-                    cols = slice(c0 + s0, c0 + s0 + step)
+                s0 = 0
+                rounded = []
+                for step in slices:
+                    grouped = keep.tile([P, step, PACK], BF16, name="x_bf_%d_%d" % (g, c0 + s0), align_bytes=64)
+                    mine = min(max(share - s0, 0), step)
+                    if mine > 0:
+                        interleave("vector", grouped[:, :mine, :], raw[:, :, s0 : s0 + mine])
+                    if mine < step:
+                        interleave("scalar", grouped[:, mine:, :], raw[:, :, s0 + mine : s0 + step])
+                    rounded.append((c0 + s0, step, grouped))
+                    s0 = s0 + step
+                for first, step, grouped in rounded:
+                    cols = slice(first, first + step)
                     nc.vector.quantize_mx(
                         out=x_words[g][:, cols].bitcast(FP8X4),
                         scales=x_scales[4 * g :, cols],
-                        in_=grouped[:, s0 : s0 + step, :].rearrange("p c j -> p (c j)"),
+                        in_=grouped[:].rearrange("p c j -> p (c j)"),
                     )
-                c0 = c0 + width
+                c0 = c0 + s0
             if g == 0:
                 gather_words(0, 0, "got_0_0")
                 gather_words(0, 1, "got_0_1")
@@ -109,16 +124,15 @@ def tile_picked_deepset_relu_e_kernel(tc, xT, w1, w2_words, w2_scales, offs, out
         w_words = {}
         w_scales = {}
 
-        def round_w(g):
-            grouped = keep.tile([P, PACK, P, PACK], BF16, name="w_bf_%d" % g, tag="w_bf_%d" % g, align_bytes=64)
-            m_part = P // W_PARTS
-            for a in range(W_PARTS):
-                nc.scalar.activation(
-                    out=grouped[:, :, a * m_part : (a + 1) * m_part, :].rearrange("p t m j -> p m j t"),
-                    in_=w_raw[g, a][:].rearrange("p j (m t) -> p m j t", t=PACK),
-                    func=ACT.Copy,
-                )
-            return grouped
+        w_bf = [keep.tile([P, PACK, P, PACK], BF16, name="w_bf_%d" % g, tag="w_bf_%d" % g, align_bytes=64) for g in range(PASSES)]
+
+        def round_w(engine, g, m0, m1):
+            dst = w_bf[g][:, :, m0:m1, :].rearrange("p t m j -> p m j t")
+            src = w_raw[g][:, :, PACK * m0 : PACK * m1].rearrange("p j (m t) -> p m j t", t=PACK)
+            if engine == "vector":
+                nc.vector.tensor_copy(out=dst, in_=src)
+            else:
+                nc.scalar.activation(out=dst, in_=src, func=ACT.Copy)
 
         def quantize_w(g, grouped):
             w_words[g] = keep.tile([P, H], U32, name="w_words_%d" % g, align_bytes=64)
@@ -131,13 +145,26 @@ def tile_picked_deepset_relu_e_kernel(tc, xT, w1, w2_words, w2_scales, offs, out
                     in_=grouped[:, t, :, :].rearrange("p m j -> p (m j)"),
                 )
 
-        w_bf = [round_w(g) for g in range(PASSES)]
-        gather_scales(0)
-        gather_scales(1)
+        round_w("scalar", 0, 0, P)
+        round_w("scalar", 1, W_SHARE[1], P)
+        gather_scales(0, 2)
+        warm = psum.tile([P, 256], F32, name="bank_7")
+        for n in range(WARM_PASSES):
+            nc.tensor.matmul_mx(
+                out=warm[:],
+                lhsT=got_words[0, 0][:, 0:P].bitcast(FP8X4),
+                lhsT_scale=got_scales[0][:, 0:P],
+                rhs=got_words[0, 0][:, 0:256].bitcast(FP8X4),
+                rhs_scale=got_scales[0][:, 0:256],
+                start=True,
+                stop=True,
+            )
+        gather_scales(1, 1)
+        gather_words(1, 0, "got_1_0")
         quantize_w(0, w_bf[0])
-        gather_words(1, 0, "w_bf_0")
+        gather_words(1, 1, "w_bf_0")
+        round_w("vector", 1, 0, W_SHARE[1])
         quantize_w(1, w_bf[1])
-        gather_words(1, 1, "w_bf_1")
 
         banks = {}
         for half in range(2):
@@ -156,28 +183,28 @@ def tile_picked_deepset_relu_e_kernel(tc, xT, w1, w2_words, w2_scales, offs, out
                 stop=(g == PASSES - 1),
             )
 
-        for half in range(2):
-            for t in range(PACK):
+        for t in range(PACK):
+            for half in range(2):
                 product(0, t, half)
 
         h = [keep.tile([P, PACK, HALF], F32, name="h_%d" % half) for half in range(2)]
         mean_part = [keep.tile([P, PACK], F32, name="mean_part_%d" % half) for half in range(2)]
-        for half in range(2):
-            for t in range(PACK):
+        for t in range(PACK):
+            for half in range(2):
                 product(1, t, half)
-                if half == 0 or t == PACK - 1:
+                if half == 0:
                     nc.scalar.activation(
                         out=h[half][:, t, :], in_=banks[t, half][:], func=ACT.Relu, scale=1.0 / S,
                         accum_out=mean_part[half][:, t : t + 1],
                     )
                 else:
-                    nc.vector.scalar_tensor_tensor(
-                        out=h[half][:, t, :], in0=banks[t, half][:], scalar=0.0, in1=inv_count[:], op0=ALU.max, op1=ALU.mult,
+                    nc.vector.tensor_scalar(
+                        out=h[half][:, t, :], in0=banks[t, half][:], scalar1=0.0, scalar2=None, op0=ALU.max, op1=ALU.add,
                         accum_out=mean_part[half][:, t : t + 1],
                     )
         neg_mean = keep.tile([P, PACK], F32, name="neg_mean")
         nc.vector.scalar_tensor_tensor(
-            out=neg_mean[:], in0=mean_part[0][:], scalar=-1.0, in1=mean_part[1][:], op0=ALU.mult, op1=ALU.subtract
+            out=neg_mean[:], in0=mean_part[1][:], scalar=-1.0 / S, in1=mean_part[0][:], op0=ALU.mult, op1=ALU.subtract
         )
 
         def center(engine, c0, width):
@@ -187,11 +214,12 @@ def tile_picked_deepset_relu_e_kernel(tc, xT, w1, w2_words, w2_scales, offs, out
                 src = h[half][:, t, h0 : h0 + width]
                 if engine == "vector":
                     nc.vector.tensor_scalar(
-                        out=planes[:, t, :], in0=src, scalar1=float(S), scalar2=neg_mean[:, t : t + 1], op0=ALU.mult, op1=ALU.add
+                        out=planes[:, t, :], in0=src, scalar1=neg_mean[:, t : t + 1], scalar2=None, op0=ALU.add
                     )
                 else:
                     nc.scalar.activation(
-                        out=planes[:, t, :], in_=src, func=ACT.Identity, bias=neg_mean[:, t : t + 1], scale=float(S)
+                        out=planes[:, t, :], in_=src, func=ACT.Identity, bias=neg_mean[:, t : t + 1],
+                        scale=float(S) if half == 0 else 1.0,
                     )
             return planes
 
@@ -218,13 +246,13 @@ def tile_picked_deepset_relu_e_kernel(tc, xT, w1, w2_words, w2_scales, offs, out
             )
             return acc
 
-        def store(engine, c0, width, acc):
+        def store(engine, queue, c0, width, acc):
             result = keep.tile([P, width], F32, name="result_%d" % c0)
             if engine == "vector":
                 nc.vector.tensor_copy(out=result[:], in_=acc[:])
             else:
                 nc.scalar.activation(out=result[:], in_=acc[:], func=ACT.Copy)
-            nc.sync.dma_start(out=out[:, c0 : c0 + width], in_=result[:])
+            queue.dma_start(out=out[:, c0 : c0 + width], in_=result[:])
 
         own = center("vector", 640, 384)
         first = center("scalar", 0, 256)
@@ -234,14 +262,14 @@ def tile_picked_deepset_relu_e_kernel(tc, xT, w1, w2_words, w2_scales, offs, out
         a_bf = weave("vector", 640, 128, own[:, :, 0:128])
         b_bf = weave("vector", 768, 256, own[:, :, 128:384])
         first_bf = weave("vector", 0, 256, first[:])
+        second_bf = weave("vector", 256, 256, second[:])
         acc_a = finish("vector", 640, 128, a_bf)
         acc_b = finish("vector", 768, 256, b_bf)
         acc_first = finish("vector", 0, 256, first_bf)
-        second_bf = weave("vector", 256, 256, second[:])
-        acc_third = finish("vector", 512, 128, third_bf)
         acc_second = finish("vector", 256, 256, second_bf)
-        store("scalar", 640, 128, acc_a)
-        store("scalar", 768, 256, acc_b)
-        store("scalar", 0, 256, acc_first)
-        store("vector", 512, 128, acc_third)
-        store("scalar", 256, 256, acc_second)
+        acc_third = finish("vector", 512, 128, third_bf)
+        store("scalar", nc.sync, 640, 128, acc_a)
+        store("scalar", nc.sync, 768, 256, acc_b)
+        store("scalar", nc.sync, 0, 256, acc_first)
+        store("scalar", nc.scalar, 256, 256, acc_second)
+        store("vector", nc.sync, 512, 128, acc_third)

@@ -25,7 +25,7 @@ X_CHUNKS = (
     ((640, (512, 512, 256)), (384, (256, 256, 256))),
     ((512, (512, 256, 256, 128)), (384, (256, 256, 128)), (128, (256,))),
 )
-W_SHARE = (0, 24)
+W_SHARE = (0, 40)
 WARM_PASSES = 8
 
 
@@ -127,8 +127,8 @@ def tile_picked_deepset_relu_e_kernel(tc, xT, w1, w2_words, w2_scales, offs, out
         w_bf = [keep.tile([P, PACK, P, PACK], BF16, name="w_bf_%d" % g, tag="w_bf_%d" % g, align_bytes=64) for g in range(PASSES)]
 
         def round_w(engine, g, m0, m1):
-            dst = w_bf[g][:, :, m0:m1, :].rearrange("p t m j -> p m j t")
-            src = w_raw[g][:, :, PACK * m0 : PACK * m1].rearrange("p j (m t) -> p m j t", t=PACK)
+            dst = w_bf[g][:, :, m0:m1, :].rearrange("p t m j -> p m t j")
+            src = w_raw[g][:, :, PACK * m0 : PACK * m1].rearrange("p j (m t) -> p m t j", t=PACK)
             if engine == "vector":
                 nc.vector.tensor_copy(out=dst, in_=src)
             else:
@@ -271,5 +271,5 @@ def tile_picked_deepset_relu_e_kernel(tc, xT, w1, w2_words, w2_scales, offs, out
         store("scalar", nc.sync, 640, 128, acc_a)
         store("scalar", nc.sync, 768, 256, acc_b)
         store("scalar", nc.sync, 0, 256, acc_first)
-        store("scalar", nc.scalar, 256, 256, acc_second)
+        store("scalar", nc.sync, 256, 256, acc_second)
         store("vector", nc.sync, 512, 128, acc_third)

@@ -21,12 +21,15 @@ PACK = 4
 K_PASS = P * PACK
 PASSES = K // K_PASS
 HALF = S // 2
-X_CHUNKS = (
-    ((640, (512, 512, 256)), (384, (256, 256, 256))),
-    ((512, (512, 256, 256, 128)), (384, (256, 256, 128)), (128, (256,))),
-)
-W_SHARE = (0, 40)
-WARM_PASSES = 8
+PAIRS = 2
+X_RUNS = {
+    (0, 0): ((2048, 1376),),
+    (0, 1): ((1024, 480), (1024, 688)),
+    (1, 0): ((1024, 688), (1024, 688)),
+    (1, 1): ((768, 0), (960, 528), (320, 208)),
+}
+W_SHARE = 24
+WARM_PASSES = 2
 
 
 def tile_picked_deepset_relu_e_kernel(tc, xT, w1, w2_words, w2_scales, offs, out):
@@ -36,8 +39,6 @@ def tile_picked_deepset_relu_e_kernel(tc, xT, w1, w2_words, w2_scales, offs, out
         psum = ctx.enter_context(tc.psum_pool(name="psum", bufs=1))
 
         offsets = keep.tile([P, S // 16], U16, name="offsets")
-        x_scales = keep.tile([P, T], U8, name="x_scales", align_bytes=64)
-        nc.vector.memset(x_scales[:].bitcast(I32), 0)
         w2_plane = keep.tile([P, N], U8, name="w2_plane", align_bytes=64)
         w2_codes = keep.tile([P, 2 * N], U8, name="w2_codes", align_bytes=64)
         nc.vector.memset(w2_plane[:].bitcast(I32), 0)
@@ -47,24 +48,36 @@ def tile_picked_deepset_relu_e_kernel(tc, xT, w1, w2_words, w2_scales, offs, out
         nc.vector.memset(table_in[:], 0.0)
         nc.scalar.activation(out=table_out[:], in_=table_in[:], func=ACT.Relu)
 
+        def load_w(g):
+            rows = w1[g * K_PASS : (g + 1) * K_PASS, :].rearrange("(p j) c -> p j c", j=PACK)
+            raw = keep.tile([P, PACK, H], F32, name="w_raw_%d" % g, tag="w_raw_%d" % g, align_bytes=64)
+            nc.sync.dma_start(out=raw[:], in_=rows)
+            return raw
+
         x_raw = {}
-        for g in range(PASSES):
-            rows = xT[g * K_PASS : (g + 1) * K_PASS, :].rearrange("(p j) c -> p j c", j=PACK)
-            c0 = 0
-            for share, slices in X_CHUNKS[g]:
-                width = sum(slices)
-                raw = keep.tile([P, PACK, width], F32, name="x_raw_%d_%d" % (g, c0))
-                nc.sync.dma_start(out=raw[:], in_=rows[:, :, c0 : c0 + width])
-                x_raw[g, c0] = raw
-                if g == 0 and c0 == 0:
-                    nc.sync.dma_start(offsets[:], offs)
-                c0 = c0 + width
         w_raw = {}
         for g in range(PASSES):
-            rows = w1[g * K_PASS : (g + 1) * K_PASS, :].rearrange("(p j) c -> p j c", j=PACK)
-            raw = keep.tile([P, PACK, H], F32, name="w_raw_%d" % g)
-            nc.sync.dma_start(out=raw[:], in_=rows)
-            w_raw[g] = raw
+            rows = xT[g * K_PASS : (g + 1) * K_PASS, :].rearrange("(p j) c -> p j c", j=PACK)
+            for u in range(PAIRS):
+                runs = X_RUNS[g, u]
+                c0 = 0
+                if len(runs) == 2:
+                    raw = keep.tile([P, 2, T], F32, name="x_raw_%d_%d" % (g, u), tag="x_raw_%d_%d" % (g, u), align_bytes=64)
+                    nc.sync.dma_start(out=raw[:, 0, :], in_=rows[:, 2 * u, :])
+                    for width, share in runs:
+                        nc.sync.dma_start(out=raw[:, 1, c0 : c0 + width], in_=rows[:, 2 * u + 1, c0 : c0 + width])
+                        x_raw[g, u, c0] = raw[:, :, c0 : c0 + width]
+                        c0 = c0 + width
+                else:
+                    for width, share in runs:
+                        raw = keep.tile([P, 2, width], F32, name="x_raw_%d_%d_%d" % (g, u, c0), tag="x_raw_%d_%d_%d" % (g, u, c0), align_bytes=64)
+                        nc.sync.dma_start(out=raw[:], in_=rows[:, 2 * u : 2 * u + 2, c0 : c0 + width])
+                        x_raw[g, u, c0] = raw[:]
+                        c0 = c0 + width
+                if g == 0 and u == 0:
+                    nc.sync.dma_start(offsets[:], offs)
+        for g in range(PASSES):
+            w_raw[g] = load_w(g)
         nc.sync.dma_start(out=w2_codes[:].bitcast(I32), in_=w2_words[0].bitcast(I32))
         for q in range(4):
             nc.sync.dma_start(out=w2_plane[32 * q : 32 * q + 4, :].bitcast(I32), in_=w2_scales[0, 4 * q : 4 * q + 4, :].bitcast(I32))
@@ -77,53 +90,44 @@ def tile_picked_deepset_relu_e_kernel(tc, xT, w1, w2_words, w2_scales, offs, out
             else:
                 nc.scalar.activation(out=dst, in_=src, func=ACT.Copy)
 
-        x_words = [keep.tile([P, T], U32, name="x_words_%d" % g, align_bytes=64) for g in range(PASSES)]
-        got_words = {}
-        got_scales = {}
+        x_pairs = {}
+        got = [keep.tile([P, PAIRS, S], U32, name="got_%d" % g) for g in range(PASSES)]
+        x_words = {}
+        x_scales = {}
+        x_bf = {}
 
-        def gather_words(g, half, tag):
-            got = keep.tile([P, HALF], U32, name="got_words_%d_%d" % (g, half), tag=tag, align_bytes=64)
-            nc.vector.tensor_copy(got[:], x_words[g][:].indirect(offsets[:, half * 32 : (half + 1) * 32]))
-            got_words[g, half] = got
-
-        def gather_scales(half, pieces):
-            got = keep.tile([P, HALF], U8, name="got_scales_%d" % half, align_bytes=64)
-            step = HALF // pieces
-            for s0 in range(0, HALF, step):
-                entry = half * HALF + s0
-                nc.vector.tensor_copy(got[:, s0 : s0 + step], x_scales[:].indirect(offsets[:, entry // 16 : (entry + step) // 16]))
-            got_scales[half] = got
-
-        for g in range(PASSES):
+        def round_x(g, u):
+            x_pairs[g, u] = keep.tile([P, T], U32, name="x_pairs_%d_%d" % (g, u), tag="x_pairs_%d_%d" % (g, u), align_bytes=64)
+            pairs = x_pairs[g, u][:].bitcast(BF16).rearrange("p (c j) -> p c j", j=2)
             c0 = 0
-            for share, slices in X_CHUNKS[g]:
-                raw = x_raw[g, c0]
-                s0 = 0
-                rounded = []
-                for step in slices:
-                    grouped = keep.tile([P, step, PACK], BF16, name="x_bf_%d_%d" % (g, c0 + s0), align_bytes=64)
-                    mine = min(max(share - s0, 0), step)
-                    if mine > 0:
-                        interleave("vector", grouped[:, :mine, :], raw[:, :, s0 : s0 + mine])
-                    if mine < step:
-                        interleave("scalar", grouped[:, mine:, :], raw[:, :, s0 + mine : s0 + step])
-                    rounded.append((c0 + s0, step, grouped))
-                    s0 = s0 + step
-                for first, step, grouped in rounded:
-                    cols = slice(first, first + step)
-                    nc.vector.quantize_mx(
-                        out=x_words[g][:, cols].bitcast(FP8X4),
-                        scales=x_scales[4 * g :, cols],
-                        in_=grouped[:].rearrange("p c j -> p (c j)"),
-                    )
-                c0 = c0 + s0
-            if g == 0:
-                gather_words(0, 0, "got_0_0")
-                gather_words(0, 1, "got_0_1")
+            for width, share in X_RUNS[g, u]:
+                dst = pairs[:, c0 : c0 + width, :]
+                src = x_raw[g, u, c0].rearrange("p j c -> p c j")
+                nc.scalar.activation(out=dst[:, share:, :], in_=src[:, share:, :], func=ACT.Copy)
+                if share > 0:
+                    nc.vector.tensor_copy(out=dst[:, :share, :], in_=src[:, :share, :])
+                c0 = c0 + width
+
+        def gather(g, u, e0, e1):
+            nc.vector.tensor_copy(got[g][:, u, e0:e1], x_pairs[g, u][:].indirect(offsets[:, e0 // 16 : e1 // 16]))
+
+        def join(engine, g, half, tag):
+            x_bf[g, half] = keep.tile([P, HALF * PACK], BF16, name="x_bf_%d_%d" % (g, half), tag=tag, align_bytes=64)
+            cols = slice(half * HALF, (half + 1) * HALF)
+            if engine == "vector":
+                dst = x_bf[g, half][:].bitcast(I32).rearrange("p (c u) -> p c u", u=PAIRS)
+                nc.vector.tensor_copy(out=dst, in_=got[g][:].bitcast(I32)[:, :, cols].rearrange("p u c -> p c u"))
+            else:
+                dst = x_bf[g, half][:].bitcast(U32).rearrange("p (c u) -> p c u", u=PAIRS)
+                nc.scalar.copy(out=dst, in_=got[g][:, :, cols].rearrange("p u c -> p c u"))
+
+        def quantize_x(g, half, tag):
+            x_words[g, half] = keep.tile([P, HALF], U32, name="x_words_%d_%d" % (g, half), tag=tag, align_bytes=64)
+            x_scales[g, half] = keep.tile([P, HALF], U8, name="x_scales_%d_%d" % (g, half), align_bytes=64)
+            nc.vector.quantize_mx(out=x_words[g, half][:].bitcast(FP8X4), scales=x_scales[g, half][:], in_=x_bf[g, half][:])
 
         w_words = {}
         w_scales = {}
-
         w_bf = [keep.tile([P, PACK, P, PACK], BF16, name="w_bf_%d" % g, tag="w_bf_%d" % g, align_bytes=64) for g in range(PASSES)]
 
         def round_w(engine, g, m0, m1):
@@ -134,42 +138,18 @@ def tile_picked_deepset_relu_e_kernel(tc, xT, w1, w2_words, w2_scales, offs, out
             else:
                 nc.scalar.activation(out=dst, in_=src, func=ACT.Copy)
 
-        def quantize_w(g, grouped):
+        def quantize_w(g, step):
             w_words[g] = keep.tile([P, H], U32, name="w_words_%d" % g, align_bytes=64)
             w_scales[g] = keep.tile([P, H], U8, name="w_scales_%d" % g, align_bytes=64)
-            for t in range(PACK):
-                cols = slice(t * P, (t + 1) * P)
+            for t in range(0, PACK, step):
+                cols = slice(t * P, (t + step) * P)
                 nc.vector.quantize_mx(
                     out=w_words[g][:, cols].bitcast(FP8X4),
                     scales=w_scales[g][:, cols],
-                    in_=grouped[:, t, :, :].rearrange("p m j -> p (m j)"),
+                    in_=w_bf[g][:, t : t + step, :, :].rearrange("p t m j -> p (t m j)"),
                 )
 
-        round_w("scalar", 0, 0, P)
-        round_w("scalar", 1, W_SHARE[1], P)
-        gather_scales(0, 2)
-        warm = psum.tile([P, 256], F32, name="bank_7")
-        for n in range(WARM_PASSES):
-            nc.tensor.matmul_mx(
-                out=warm[:],
-                lhsT=got_words[0, 0][:, 0:P].bitcast(FP8X4),
-                lhsT_scale=got_scales[0][:, 0:P],
-                rhs=got_words[0, 0][:, 0:256].bitcast(FP8X4),
-                rhs_scale=got_scales[0][:, 0:256],
-                start=True,
-                stop=True,
-            )
-        gather_scales(1, 1)
-        gather_words(1, 0, "got_1_0")
-        quantize_w(0, w_bf[0])
-        gather_words(1, 1, "w_bf_0")
-        round_w("vector", 1, 0, W_SHARE[1])
-        quantize_w(1, w_bf[1])
-
         banks = {}
-        for half in range(2):
-            for t in range(PACK):
-                banks[t, half] = psum.tile([P, HALF], F32, name="bank_%d" % (2 * t + half))
 
         def product(g, t, half):
             cols = slice(t * P, (t + 1) * P)
@@ -177,15 +157,52 @@ def tile_picked_deepset_relu_e_kernel(tc, xT, w1, w2_words, w2_scales, offs, out
                 out=banks[t, half][:],
                 lhsT=w_words[g][:, cols].bitcast(FP8X4),
                 lhsT_scale=w_scales[g][:, cols],
-                rhs=got_words[g, half][:].bitcast(FP8X4),
-                rhs_scale=got_scales[half][4 * g :, :],
+                rhs=x_words[g, half][:].bitcast(FP8X4),
+                rhs_scale=x_scales[g, half][:],
                 start=(g == 0),
                 stop=(g == PASSES - 1),
             )
 
+        round_x(0, 0)
+        gather(0, 0, 0, S)
+        round_x(0, 1)
+        gather(0, 1, 0, HALF)
+        join("scalar", 0, 0, "x_bf_0_0")
+        gather(0, 1, HALF, S)
+        round_x(1, 0)
+        gather(1, 0, 0, S)
+        quantize_x(0, 0, "x_pairs_1_0")
+        join("scalar", 0, 1, "x_raw_1_0")
+        round_x(1, 1)
+        gather(1, 1, 0, HALF)
+        quantize_x(0, 1, "x_raw_1_1_1728")
+        gather(1, 1, HALF, S)
+        warm = psum.tile([P, HALF], F32, name="bank_7")
+        for n in range(WARM_PASSES):
+            nc.tensor.matmul_mx(
+                out=warm[:],
+                lhsT=x_words[0, 1][:, 0:P].bitcast(FP8X4),
+                lhsT_scale=x_scales[0, 1][:, 0:P],
+                rhs=x_words[0, 1][:].bitcast(FP8X4),
+                rhs_scale=x_scales[0, 1][:],
+                start=True,
+                stop=True,
+            )
+        for half in range(2):
+            for t in range(PACK):
+                banks[t, half] = psum.tile([P, HALF], F32, name="bank_%d" % (2 * t + half))
+        round_w("scalar", 0, 0, P)
+        quantize_w(0, 2)
         for t in range(PACK):
             for half in range(2):
                 product(0, t, half)
+        join("scalar", 1, 0, "w_raw_0")
+        join("vector", 1, 1, "w_bf_0")
+        quantize_x(1, 1, "x_words_1_1")
+        quantize_x(1, 0, "x_words_1_0")
+        round_w("scalar", 1, W_SHARE, P)
+        round_w("vector", 1, 0, W_SHARE)
+        quantize_w(1, 1)
 
         h = [keep.tile([P, PACK, HALF], F32, name="h_%d" % half) for half in range(2)]
         mean_part = [keep.tile([P, PACK], F32, name="mean_part_%d" % half) for half in range(2)]

@@ -25,11 +25,10 @@ PAIRS = 2
 X_RUNS = {
     (0, 0): ((2048, 1376),),
     (0, 1): ((1024, 480), (1024, 688)),
-    (1, 0): ((1024, 688), (1024, 688)),
-    (1, 1): ((768, 0), (960, 528), (320, 208)),
+    (1, 0): ((1024, 480), (1024, 688)),
+    (1, 1): ((768, 0), (896, 592), (384, 256)),
 }
-W_SHARE = 24
-WARM_PASSES = 2
+W_SHARE = 92
 
 
 def tile_picked_deepset_relu_e_kernel(tc, xT, w1, w2_words, w2_scales, offs, out):
@@ -61,6 +60,8 @@ def tile_picked_deepset_relu_e_kernel(tc, xT, w1, w2_words, w2_scales, offs, out
             for u in range(PAIRS):
                 runs = X_RUNS[g, u]
                 c0 = 0
+                if (g, u) == (1, 0):
+                    w_raw[0] = load_w(0)
                 if len(runs) == 2:
                     raw = keep.tile([P, 2, T], F32, name="x_raw_%d_%d" % (g, u), tag="x_raw_%d_%d" % (g, u), align_bytes=64)
                     nc.sync.dma_start(out=raw[:, 0, :], in_=rows[:, 2 * u, :])
@@ -76,8 +77,7 @@ def tile_picked_deepset_relu_e_kernel(tc, xT, w1, w2_words, w2_scales, offs, out
                         c0 = c0 + width
                 if g == 0 and u == 0:
                     nc.sync.dma_start(offsets[:], offs)
-        for g in range(PASSES):
-            w_raw[g] = load_w(g)
+        w_raw[1] = load_w(1)
         nc.sync.dma_start(out=w2_codes[:].bitcast(I32), in_=w2_words[0].bitcast(I32))
         for q in range(4):
             nc.sync.dma_start(out=w2_plane[32 * q : 32 * q + 4, :].bitcast(I32), in_=w2_scales[0, 4 * q : 4 * q + 4, :].bitcast(I32))
@@ -138,80 +138,71 @@ def tile_picked_deepset_relu_e_kernel(tc, xT, w1, w2_words, w2_scales, offs, out
             else:
                 nc.scalar.activation(out=dst, in_=src, func=ACT.Copy)
 
-        def quantize_w(g, step):
-            w_words[g] = keep.tile([P, H], U32, name="w_words_%d" % g, align_bytes=64)
-            w_scales[g] = keep.tile([P, H], U8, name="w_scales_%d" % g, align_bytes=64)
-            for t in range(0, PACK, step):
-                cols = slice(t * P, (t + step) * P)
-                nc.vector.quantize_mx(
-                    out=w_words[g][:, cols].bitcast(FP8X4),
-                    scales=w_scales[g][:, cols],
-                    in_=w_bf[g][:, t : t + step, :, :].rearrange("p t m j -> p (t m j)"),
-                )
+        def quantize_w(g, t, tag):
+            w_words[g, t] = keep.tile([P, P], U32, name="w_words_%d_%d" % (g, t), tag=tag, align_bytes=64)
+            w_scales[g, t] = keep.tile([P, P], U8, name="w_scales_%d_%d" % (g, t), align_bytes=64)
+            nc.vector.quantize_mx(
+                out=w_words[g, t][:].bitcast(FP8X4),
+                scales=w_scales[g, t][:],
+                in_=w_bf[g][:, t, :, :].rearrange("p m j -> p (m j)"),
+            )
 
         banks = {}
+        for half in range(2):
+            for t in range(PACK):
+                banks[t, half] = psum.tile([P, HALF], F32, name="bank_%d" % (2 * t + half))
 
         def product(g, t, half):
-            cols = slice(t * P, (t + 1) * P)
             nc.tensor.matmul_mx(
                 out=banks[t, half][:],
-                lhsT=w_words[g][:, cols].bitcast(FP8X4),
-                lhsT_scale=w_scales[g][:, cols],
+                lhsT=w_words[g, t][:].bitcast(FP8X4),
+                lhsT_scale=w_scales[g, t][:],
                 rhs=x_words[g, half][:].bitcast(FP8X4),
                 rhs_scale=x_scales[g, half][:],
                 start=(g == 0),
                 stop=(g == PASSES - 1),
             )
 
+        def first_pass(t, tag):
+            quantize_w(0, t, tag)
+            for half in range(2):
+                product(0, t, half)
+
         round_x(0, 0)
         gather(0, 0, 0, S)
         round_x(0, 1)
-        gather(0, 1, 0, HALF)
-        join("scalar", 0, 0, "x_bf_0_0")
-        gather(0, 1, HALF, S)
+        gather(0, 1, 0, S)
+        round_w("scalar", 0, 0, P)
+        join("vector", 0, 0, "x_bf_0_0")
+        join("vector", 0, 1, "x_bf_0_1")
+        quantize_x(0, 0, "x_words_0_0")
+        quantize_x(0, 1, "x_words_0_1")
         round_x(1, 0)
         gather(1, 0, 0, S)
-        quantize_x(0, 0, "x_pairs_1_0")
-        join("scalar", 0, 1, "x_raw_1_0")
+        first_pass(0, "x_pairs_1_0")
+        first_pass(1, "x_raw_1_0")
         round_x(1, 1)
         gather(1, 1, 0, HALF)
-        quantize_x(0, 1, "x_raw_1_1_1728")
+        join("scalar", 1, 0, "x_bf_1_0")
+        first_pass(2, "x_raw_1_1_1664")
         gather(1, 1, HALF, S)
-        warm = psum.tile([P, HALF], F32, name="bank_7")
-        for n in range(WARM_PASSES):
-            nc.tensor.matmul_mx(
-                out=warm[:],
-                lhsT=x_words[0, 1][:, 0:P].bitcast(FP8X4),
-                lhsT_scale=x_scales[0, 1][:, 0:P],
-                rhs=x_words[0, 1][:].bitcast(FP8X4),
-                rhs_scale=x_scales[0, 1][:],
-                start=True,
-                stop=True,
-            )
-        for half in range(2):
-            for t in range(PACK):
-                banks[t, half] = psum.tile([P, HALF], F32, name="bank_%d" % (2 * t + half))
-        round_w("scalar", 0, 0, P)
-        quantize_w(0, 2)
-        for t in range(PACK):
-            for half in range(2):
-                product(0, t, half)
-        join("scalar", 1, 0, "w_raw_0")
-        join("vector", 1, 1, "w_bf_0")
-        quantize_x(1, 1, "x_words_1_1")
+        join("scalar", 1, 1, "x_bf_1_1")
+        first_pass(3, "x_pairs_1_1")
         quantize_x(1, 0, "x_words_1_0")
         round_w("scalar", 1, W_SHARE, P)
         round_w("vector", 1, 0, W_SHARE)
-        quantize_w(1, 1)
+        for t in range(PACK):
+            quantize_w(1, t, "w_words_1_%d" % t)
+        quantize_x(1, 1, "w_bf_1")
 
         h = [keep.tile([P, PACK, HALF], F32, name="h_%d" % half) for half in range(2)]
         mean_part = [keep.tile([P, PACK], F32, name="mean_part_%d" % half) for half in range(2)]
-        for t in range(PACK):
-            for half in range(2):
+        for half in range(2):
+            for t in range(PACK):
                 product(1, t, half)
-                if half == 0:
+                if half == 0 or t == PACK - 1:
                     nc.scalar.activation(
-                        out=h[half][:, t, :], in_=banks[t, half][:], func=ACT.Relu, scale=1.0 / S,
+                        out=h[half][:, t, :], in_=banks[t, half][:], func=ACT.Relu, scale=1.0 / S if half == 0 else 1.0,
                         accum_out=mean_part[half][:, t : t + 1],
                     )
                 else:
@@ -271,22 +262,32 @@ def tile_picked_deepset_relu_e_kernel(tc, xT, w1, w2_words, w2_scales, offs, out
                 nc.scalar.activation(out=result[:], in_=acc[:], func=ACT.Copy)
             queue.dma_start(out=out[:, c0 : c0 + width], in_=result[:])
 
-        own = center("vector", 640, 384)
+        def center_woven(c0, width):
+            half, h0 = divmod(c0, HALF)
+            grouped = keep.tile([P, width, PACK], BF16, name="z_bf_%d" % c0, align_bytes=64)
+            nc.vector.tensor_tensor(
+                out=grouped[:].rearrange("p (c i) t -> p c t i", i=4),
+                in0=h[half][:, :, h0 : h0 + width].rearrange("p t (c i) -> p c t i", i=4),
+                in1=neg_mean[:].unsqueeze(1).unsqueeze(3).to_broadcast([P, width // 4, PACK, 4]),
+                op=ALU.add,
+            )
+            return grouped
+
+        b_bf = center_woven(768, 256)
+        a_bf = center_woven(640, 128)
         first = center("scalar", 0, 256)
         second = center("scalar", 256, 256)
         third = center("scalar", 512, 128)
         third_bf = weave("scalar", 512, 128, third[:])
-        a_bf = weave("vector", 640, 128, own[:, :, 0:128])
-        b_bf = weave("vector", 768, 256, own[:, :, 128:384])
+        acc_b = finish("vector", 768, 256, b_bf)
+        acc_a = finish("vector", 640, 128, a_bf)
         first_bf = weave("vector", 0, 256, first[:])
         second_bf = weave("vector", 256, 256, second[:])
-        acc_a = finish("vector", 640, 128, a_bf)
-        acc_b = finish("vector", 768, 256, b_bf)
         acc_first = finish("vector", 0, 256, first_bf)
         acc_second = finish("vector", 256, 256, second_bf)
         acc_third = finish("vector", 512, 128, third_bf)
-        store("scalar", nc.sync, 640, 128, acc_a)
         store("scalar", nc.sync, 768, 256, acc_b)
+        store("scalar", nc.sync, 640, 128, acc_a)
         store("scalar", nc.sync, 0, 256, acc_first)
         store("scalar", nc.sync, 256, 256, acc_second)
         store("vector", nc.sync, 512, 128, acc_third)

@@ -25,10 +25,11 @@ PAIRS = 2
 X_RUNS = {
     (0, 0): ((2048, 1376),),
     (0, 1): ((1024, 480), (1024, 688)),
-    (1, 0): ((1024, 480), (1024, 688)),
-    (1, 1): ((768, 0), (896, 592), (384, 256)),
+    (1, 0): ((1024, 512), (1024, 576)),
+    (1, 1): ((768, 0), (1024, 688), (256, 176)),
 }
 W_SHARE = 92
+LATE = 128
 
 
 def tile_picked_deepset_relu_e_kernel(tc, xT, w1, w2_words, w2_scales, offs, out):
@@ -94,7 +95,6 @@ def tile_picked_deepset_relu_e_kernel(tc, xT, w1, w2_words, w2_scales, offs, out
         got = [keep.tile([P, PAIRS, S], U32, name="got_%d" % g) for g in range(PASSES)]
         x_words = {}
         x_scales = {}
-        x_bf = {}
 
         def round_x(g, u):
             x_pairs[g, u] = keep.tile([P, T], U32, name="x_pairs_%d_%d" % (g, u), tag="x_pairs_%d_%d" % (g, u), align_bytes=64)
@@ -111,20 +111,24 @@ def tile_picked_deepset_relu_e_kernel(tc, xT, w1, w2_words, w2_scales, offs, out
         def gather(g, u, e0, e1):
             nc.vector.tensor_copy(got[g][:, u, e0:e1], x_pairs[g, u][:].indirect(offsets[:, e0 // 16 : e1 // 16]))
 
-        def join(engine, g, half, tag):
-            x_bf[g, half] = keep.tile([P, HALF * PACK], BF16, name="x_bf_%d_%d" % (g, half), tag=tag, align_bytes=64)
-            cols = slice(half * HALF, (half + 1) * HALF)
+        def join(engine, g, e0, width, tag):
+            grouped = keep.tile([P, width * PACK], BF16, name="x_bf_%d_%d" % (g, e0), tag=tag, align_bytes=64)
+            cols = slice(e0, e0 + width)
             if engine == "vector":
-                dst = x_bf[g, half][:].bitcast(I32).rearrange("p (c u) -> p c u", u=PAIRS)
+                dst = grouped[:].bitcast(I32).rearrange("p (c u) -> p c u", u=PAIRS)
                 nc.vector.tensor_copy(out=dst, in_=got[g][:].bitcast(I32)[:, :, cols].rearrange("p u c -> p c u"))
             else:
-                dst = x_bf[g, half][:].bitcast(U32).rearrange("p (c u) -> p c u", u=PAIRS)
+                dst = grouped[:].bitcast(U32).rearrange("p (c u) -> p c u", u=PAIRS)
                 nc.scalar.copy(out=dst, in_=got[g][:, :, cols].rearrange("p u c -> p c u"))
+            return grouped
 
-        def quantize_x(g, half, tag):
+        def codes(g, half, tag):
             x_words[g, half] = keep.tile([P, HALF], U32, name="x_words_%d_%d" % (g, half), tag=tag, align_bytes=64)
             x_scales[g, half] = keep.tile([P, HALF], U8, name="x_scales_%d_%d" % (g, half), align_bytes=64)
-            nc.vector.quantize_mx(out=x_words[g, half][:].bitcast(FP8X4), scales=x_scales[g, half][:], in_=x_bf[g, half][:])
+
+        def quantize_x(g, half, c0, width, grouped):
+            cols = slice(c0, c0 + width)
+            nc.vector.quantize_mx(out=x_words[g, half][:, cols].bitcast(FP8X4), scales=x_scales[g, half][:, cols], in_=grouped)
 
         w_words = {}
         w_scales = {}
@@ -138,14 +142,17 @@ def tile_picked_deepset_relu_e_kernel(tc, xT, w1, w2_words, w2_scales, offs, out
             else:
                 nc.scalar.activation(out=dst, in_=src, func=ACT.Copy)
 
-        def quantize_w(g, t, tag):
-            w_words[g, t] = keep.tile([P, P], U32, name="w_words_%d_%d" % (g, t), tag=tag, align_bytes=64)
-            w_scales[g, t] = keep.tile([P, P], U8, name="w_scales_%d_%d" % (g, t), align_bytes=64)
+        def quantize_w(g, t0, count, tag):
+            words = keep.tile([P, count * P], U32, name="w_words_%d_%d" % (g, t0), tag=tag, align_bytes=64)
+            scales = keep.tile([P, count * P], U8, name="w_scales_%d_%d" % (g, t0), align_bytes=64)
             nc.vector.quantize_mx(
-                out=w_words[g, t][:].bitcast(FP8X4),
-                scales=w_scales[g, t][:],
-                in_=w_bf[g][:, t, :, :].rearrange("p m j -> p (m j)"),
+                out=words[:].bitcast(FP8X4),
+                scales=scales[:],
+                in_=w_bf[g][:, t0 : t0 + count, :, :].rearrange("p t m j -> p (t m j)"),
             )
+            for t in range(count):
+                w_words[g, t0 + t] = words[:, t * P : (t + 1) * P]
+                w_scales[g, t0 + t] = scales[:, t * P : (t + 1) * P]
 
         banks = {}
         for half in range(2):
@@ -155,45 +162,48 @@ def tile_picked_deepset_relu_e_kernel(tc, xT, w1, w2_words, w2_scales, offs, out
         def product(g, t, half):
             nc.tensor.matmul_mx(
                 out=banks[t, half][:],
-                lhsT=w_words[g, t][:].bitcast(FP8X4),
-                lhsT_scale=w_scales[g, t][:],
+                lhsT=w_words[g, t].bitcast(FP8X4),
+                lhsT_scale=w_scales[g, t],
                 rhs=x_words[g, half][:].bitcast(FP8X4),
                 rhs_scale=x_scales[g, half][:],
                 start=(g == 0),
                 stop=(g == PASSES - 1),
             )
 
-        def first_pass(t, tag):
-            quantize_w(0, t, tag)
-            for half in range(2):
-                product(0, t, half)
-
         round_x(0, 0)
         gather(0, 0, 0, S)
         round_x(0, 1)
         gather(0, 1, 0, S)
         round_w("scalar", 0, 0, P)
-        join("vector", 0, 0, "x_bf_0_0")
-        join("vector", 0, 1, "x_bf_0_1")
-        quantize_x(0, 0, "x_words_0_0")
-        quantize_x(0, 1, "x_words_0_1")
+        early = join("vector", 0, 0, HALF, "x_bf_0_0")
+        middle = join("scalar", 0, HALF, HALF - LATE, "w_raw_0")
+        codes(0, 0, "x_words_0_0")
+        quantize_x(0, 0, 0, HALF, early[:])
+        quantize_w(0, 0, PACK, "w_words_0")
+        for t in range(PACK):
+            product(0, t, 0)
         round_x(1, 0)
+        codes(0, 1, "x_words_0_1")
+        quantize_x(0, 1, 0, 256, middle[:, : 256 * PACK])
+        quantize_x(0, 1, 256, 128, middle[:, 256 * PACK :])
         gather(1, 0, 0, S)
-        first_pass(0, "x_pairs_1_0")
-        first_pass(1, "x_raw_1_0")
         round_x(1, 1)
+        late = join("scalar", 0, S - LATE, LATE, "x_raw_1_1_1792")
         gather(1, 1, 0, HALF)
-        join("scalar", 1, 0, "x_bf_1_0")
-        first_pass(2, "x_raw_1_1_1664")
+        first_half = join("scalar", 1, 0, HALF, "x_bf_1_0")
+        quantize_x(0, 1, HALF - LATE, LATE, late[:])
+        for t in range(PACK):
+            product(0, t, 1)
         gather(1, 1, HALF, S)
-        join("scalar", 1, 1, "x_bf_1_1")
-        first_pass(3, "x_pairs_1_1")
-        quantize_x(1, 0, "x_words_1_0")
+        second_half = join("scalar", 1, HALF, HALF, "x_bf_1_1")
+        codes(1, 0, "x_words_1_0")
+        quantize_x(1, 0, 0, HALF, first_half[:])
         round_w("scalar", 1, W_SHARE, P)
         round_w("vector", 1, 0, W_SHARE)
         for t in range(PACK):
-            quantize_w(1, t, "w_words_1_%d" % t)
-        quantize_x(1, 1, "w_bf_1")
+            quantize_w(1, t, 1, "w_words_1_%d" % t)
+        codes(1, 1, "w_bf_1")
+        quantize_x(1, 1, 0, HALF, second_half[:])
 
         h = [keep.tile([P, PACK, HALF], F32, name="h_%d" % half) for half in range(2)]
         mean_part = [keep.tile([P, PACK], F32, name="mean_part_%d" % half) for half in range(2)]

@@ -135,8 +135,8 @@ def tile_picked_deepset_relu_e_kernel(tc, xT, w1, w2_words, w2_scales, offs, out
         w_bf = [keep.tile([P, PACK, P, PACK], BF16, name="w_bf_%d" % g, tag="w_bf_%d" % g, align_bytes=64) for g in range(PASSES)]
 
         def round_w(engine, g, m0, m1):
-            dst = w_bf[g][:, :, m0:m1, :].rearrange("p t m j -> p m t j")
-            src = w_raw[g][:, :, PACK * m0 : PACK * m1].rearrange("p j (m t) -> p m t j", t=PACK)
+            dst = w_bf[g][:, :, m0:m1, :].rearrange("p t m j -> p m j t")
+            src = w_raw[g][:, :, PACK * m0 : PACK * m1].rearrange("p j (m t) -> p m j t", t=PACK)
             if engine == "vector":
                 nc.vector.tensor_copy(out=dst, in_=src)
             else:

@@ -24,12 +24,14 @@ HALF = S // 2
 PAIRS = 2
 X_RUNS = {
     (0, 0): ((2048, 1376),),
-    (0, 1): ((1024, 480), (1024, 688)),
-    (1, 0): ((1024, 512), (1024, 576)),
-    (1, 1): ((768, 0), (1024, 688), (256, 176)),
+    (0, 1): ((1024, 0), (1024, 688)),
+    (1, 0): ((1024, 256), (1024, 688)),
+    (1, 1): ((768, 0), (928, 608), (352, 352)),
 }
-W_SHARE = 92
-LATE = 128
+W_SHARE = 64
+W_LAST = 96
+LATE = 256
+QUARTER = 256
 
 
 def tile_picked_deepset_relu_e_kernel(tc, xT, w1, w2_words, w2_scales, offs, out):
@@ -63,22 +65,19 @@ def tile_picked_deepset_relu_e_kernel(tc, xT, w1, w2_words, w2_scales, offs, out
                 c0 = 0
                 if (g, u) == (1, 0):
                     w_raw[0] = load_w(0)
-                if len(runs) == 2:
-                    raw = keep.tile([P, 2, T], F32, name="x_raw_%d_%d" % (g, u), tag="x_raw_%d_%d" % (g, u), align_bytes=64)
-                    nc.sync.dma_start(out=raw[:, 0, :], in_=rows[:, 2 * u, :])
-                    for width, share in runs:
-                        nc.sync.dma_start(out=raw[:, 1, c0 : c0 + width], in_=rows[:, 2 * u + 1, c0 : c0 + width])
-                        x_raw[g, u, c0] = raw[:, :, c0 : c0 + width]
-                        c0 = c0 + width
-                else:
-                    for width, share in runs:
-                        raw = keep.tile([P, 2, width], F32, name="x_raw_%d_%d_%d" % (g, u, c0), tag="x_raw_%d_%d_%d" % (g, u, c0), align_bytes=64)
-                        nc.sync.dma_start(out=raw[:], in_=rows[:, 2 * u : 2 * u + 2, c0 : c0 + width])
-                        x_raw[g, u, c0] = raw[:]
-                        c0 = c0 + width
+                for width, share in runs:
+                    raw = keep.tile([P, 2, width], F32, name="x_raw_%d_%d_%d" % (g, u, c0), tag="x_raw_%d_%d_%d" % (g, u, c0), align_bytes=64)
+                    nc.sync.dma_start(out=raw[:], in_=rows[:, 2 * u : 2 * u + 2, c0 : c0 + width])
+                    x_raw[g, u, c0] = raw[:]
+                    c0 = c0 + width
                 if g == 0 and u == 0:
                     nc.sync.dma_start(offsets[:], offs)
-        w_raw[1] = load_w(1)
+        w_rows = w1[K_PASS:, :].rearrange("(p j) c -> p j c", j=PACK)
+        w_part = []
+        for c0, c1 in ((0, PACK * W_SHARE), (PACK * W_SHARE, H)):
+            raw = keep.tile([P, PACK, c1 - c0], F32, name="w_part_%d" % c0, tag="w_part_%d" % c0, align_bytes=64)
+            nc.sync.dma_start(out=raw[:], in_=w_rows[:, :, c0:c1])
+            w_part.append(raw)
         nc.sync.dma_start(out=w2_codes[:].bitcast(I32), in_=w2_words[0].bitcast(I32))
         for q in range(4):
             nc.sync.dma_start(out=w2_plane[32 * q : 32 * q + 4, :].bitcast(I32), in_=w2_scales[0, 4 * q : 4 * q + 4, :].bitcast(I32))
@@ -96,14 +95,16 @@ def tile_picked_deepset_relu_e_kernel(tc, xT, w1, w2_words, w2_scales, offs, out
         x_words = {}
         x_scales = {}
 
-        def round_x(g, u):
-            x_pairs[g, u] = keep.tile([P, T], U32, name="x_pairs_%d_%d" % (g, u), tag="x_pairs_%d_%d" % (g, u), align_bytes=64)
+        def round_x(g, u, r0=0, r1=2):
+            if r0 == 0:
+                x_pairs[g, u] = keep.tile([P, T], U32, name="x_pairs_%d_%d" % (g, u), tag="x_pairs_%d_%d" % (g, u), align_bytes=64)
             pairs = x_pairs[g, u][:].bitcast(BF16).rearrange("p (c j) -> p c j", j=2)
-            c0 = 0
-            for width, share in X_RUNS[g, u]:
+            c0 = sum(width for width, share in X_RUNS[g, u][:r0])
+            for width, share in X_RUNS[g, u][r0:r1]:
                 dst = pairs[:, c0 : c0 + width, :]
                 src = x_raw[g, u, c0].rearrange("p j c -> p c j")
-                nc.scalar.activation(out=dst[:, share:, :], in_=src[:, share:, :], func=ACT.Copy)
+                if share < width:
+                    nc.scalar.activation(out=dst[:, share:, :], in_=src[:, share:, :], func=ACT.Copy)
                 if share > 0:
                     nc.vector.tensor_copy(out=dst[:, :share, :], in_=src[:, :share, :])
                 c0 = c0 + width
@@ -134,9 +135,9 @@ def tile_picked_deepset_relu_e_kernel(tc, xT, w1, w2_words, w2_scales, offs, out
         w_scales = {}
         w_bf = [keep.tile([P, PACK, P, PACK], BF16, name="w_bf_%d" % g, tag="w_bf_%d" % g, align_bytes=64) for g in range(PASSES)]
 
-        def round_w(engine, g, m0, m1):
+        def round_w(engine, g, m0, m1, raw):
             dst = w_bf[g][:, :, m0:m1, :].rearrange("p t m j -> p m j t")
-            src = w_raw[g][:, :, PACK * m0 : PACK * m1].rearrange("p j (m t) -> p m j t", t=PACK)
+            src = raw.rearrange("p j (m t) -> p m j t", t=PACK)
             if engine == "vector":
                 nc.vector.tensor_copy(out=dst, in_=src)
             else:
@@ -174,9 +175,9 @@ def tile_picked_deepset_relu_e_kernel(tc, xT, w1, w2_words, w2_scales, offs, out
         gather(0, 0, 0, S)
         round_x(0, 1)
         gather(0, 1, 0, S)
-        round_w("scalar", 0, 0, P)
+        round_w("scalar", 0, 0, P, w_raw[0][:])
         early = join("vector", 0, 0, HALF, "x_bf_0_0")
-        middle = join("scalar", 0, HALF, HALF - LATE, "w_raw_0")
+        middle = join("vector", 0, HALF, HALF - LATE, "x_bf_0_1")
         codes(0, 0, "x_words_0_0")
         quantize_x(0, 0, 0, HALF, early[:])
         quantize_w(0, 0, PACK, "w_words_0")
@@ -184,46 +185,52 @@ def tile_picked_deepset_relu_e_kernel(tc, xT, w1, w2_words, w2_scales, offs, out
             product(0, t, 0)
         round_x(1, 0)
         codes(0, 1, "x_words_0_1")
-        quantize_x(0, 1, 0, 256, middle[:, : 256 * PACK])
-        quantize_x(0, 1, 256, 128, middle[:, 256 * PACK :])
+        quantize_x(0, 1, 0, HALF - LATE, middle[:])
         gather(1, 0, 0, S)
         round_x(1, 1)
-        late = join("scalar", 0, S - LATE, LATE, "x_raw_1_1_1792")
-        gather(1, 1, 0, HALF)
-        first_half = join("scalar", 1, 0, HALF, "x_bf_1_0")
+        late = join("scalar", 0, S - LATE, LATE, "x_raw_1_1_768")
+        round_x(1, 1, 2, 3)
         quantize_x(0, 1, HALF - LATE, LATE, late[:])
         for t in range(PACK):
             product(0, t, 1)
+        round_w("scalar", 1, 0, W_SHARE, w_part[0][:])
+        gather(1, 1, 0, HALF)
+        first_half = join("scalar", 1, 0, HALF, "w_part_0")
         gather(1, 1, HALF, S)
-        second_half = join("scalar", 1, HALF, HALF, "x_bf_1_1")
+        round_w("vector", 1, W_SHARE, W_LAST, w_part[1][:, :, : PACK * (W_LAST - W_SHARE)])
+        round_w("scalar", 1, W_LAST, P, w_part[1][:, :, PACK * (W_LAST - W_SHARE) :])
+        second_half = join("scalar", 1, HALF, HALF, "w_part_%d" % (PACK * W_SHARE))
         codes(1, 0, "x_words_1_0")
         quantize_x(1, 0, 0, HALF, first_half[:])
-        round_w("scalar", 1, W_SHARE, P)
-        round_w("vector", 1, 0, W_SHARE)
         for t in range(PACK):
             quantize_w(1, t, 1, "w_words_1_%d" % t)
         codes(1, 1, "w_bf_1")
         quantize_x(1, 1, 0, HALF, second_half[:])
 
         h = [keep.tile([P, PACK, HALF], F32, name="h_%d" % half) for half in range(2)]
-        mean_part = [keep.tile([P, PACK], F32, name="mean_part_%d" % half) for half in range(2)]
-        for half in range(2):
-            for t in range(PACK):
-                product(1, t, half)
-                if half == 0 or t == PACK - 1:
-                    nc.scalar.activation(
-                        out=h[half][:, t, :], in_=banks[t, half][:], func=ACT.Relu, scale=1.0 / S if half == 0 else 1.0,
-                        accum_out=mean_part[half][:, t : t + 1],
-                    )
-                else:
-                    nc.vector.tensor_scalar(
-                        out=h[half][:, t, :], in0=banks[t, half][:], scalar1=0.0, scalar2=None, op0=ALU.max, op1=ALU.add,
-                        accum_out=mean_part[half][:, t : t + 1],
-                    )
-        neg_mean = keep.tile([P, PACK], F32, name="neg_mean")
-        nc.vector.scalar_tensor_tensor(
-            out=neg_mean[:], in0=mean_part[1][:], scalar=-1.0 / S, in1=mean_part[0][:], op0=ALU.mult, op1=ALU.subtract
-        )
+        part = [keep.tile([P, PACK], F32, name="part_%d" % half) for half in range(2)]
+        total = keep.tile([P, PACK], F32, name="total")
+
+        def empty(engine, t, half, sums, start):
+            product(1, t, half)
+            if engine == "scalar":
+                nc.scalar.activation(out=h[half][:, t, :], in_=banks[t, half][:], func=ACT.Relu, accum_out=sums[:, t : t + 1])
+            else:
+                nc.vector.tensor_scalar(
+                    out=h[half][:, t, :], in0=banks[t, half][:], scalar1=0.0, scalar2=start, op0=ALU.max, op1=ALU.add,
+                    accum_out=sums[:, t : t + 1],
+                )
+
+        empty("scalar", 0, 0, part[0], None)
+        empty("scalar", 1, 0, part[0], None)
+        empty("vector", 2, 0, part[0], None)
+        empty("vector", 3, 0, part[0], None)
+        empty("scalar", 1, 1, part[1], None)
+        empty("vector", 0, 1, total, part[0][:, 0:1])
+        empty("scalar", 2, 1, part[1], None)
+        empty("scalar", 3, 1, part[1], None)
+        nc.vector.tensor_tensor(out=total[:, 1:3], in0=part[0][:, 1:3], in1=part[1][:, 1:3], op=ALU.add)
+        nc.scalar.activation(out=total[:, 3:4], in_=part[1][:, 3:4], func=ACT.Identity, bias=part[0][:, 3:4])
 
         def center(engine, c0, width):
             half, h0 = divmod(c0, HALF)
@@ -232,13 +239,10 @@ def tile_picked_deepset_relu_e_kernel(tc, xT, w1, w2_words, w2_scales, offs, out
                 src = h[half][:, t, h0 : h0 + width]
                 if engine == "vector":
                     nc.vector.tensor_scalar(
-                        out=planes[:, t, :], in0=src, scalar1=neg_mean[:, t : t + 1], scalar2=None, op0=ALU.add
+                        out=planes[:, t, :], in0=src, scalar1=-float(S), scalar2=total[:, t : t + 1], op0=ALU.mult, op1=ALU.add
                     )
                 else:
-                    nc.scalar.activation(
-                        out=planes[:, t, :], in_=src, func=ACT.Identity, bias=neg_mean[:, t : t + 1],
-                        scale=float(S) if half == 0 else 1.0,
-                    )
+                    nc.scalar.activation(out=planes[:, t, :], in_=src, func=ACT.Identity, bias=total[:, t : t + 1], scale=-float(S))
             return planes
 
         def weave(engine, c0, width, planes):
@@ -267,24 +271,14 @@ def tile_picked_deepset_relu_e_kernel(tc, xT, w1, w2_words, w2_scales, offs, out
         def store(engine, queue, c0, width, acc):
             result = keep.tile([P, width], F32, name="result_%d" % c0)
             if engine == "vector":
-                nc.vector.tensor_copy(out=result[:], in_=acc[:])
+                nc.vector.tensor_scalar(out=result[:], in0=acc[:], scalar1=-1.0 / S, scalar2=None, op0=ALU.mult)
             else:
-                nc.scalar.activation(out=result[:], in_=acc[:], func=ACT.Copy)
+                nc.scalar.activation(out=result[:], in_=acc[:], func=ACT.Copy, scale=-1.0 / S)
             queue.dma_start(out=out[:, c0 : c0 + width], in_=result[:])
 
-        def center_woven(c0, width):
-            half, h0 = divmod(c0, HALF)
-            grouped = keep.tile([P, width, PACK], BF16, name="z_bf_%d" % c0, align_bytes=64)
-            nc.vector.tensor_tensor(
-                out=grouped[:].rearrange("p (c i) t -> p c t i", i=4),
-                in0=h[half][:, :, h0 : h0 + width].rearrange("p t (c i) -> p c t i", i=4),
-                in1=neg_mean[:].unsqueeze(1).unsqueeze(3).to_broadcast([P, width // 4, PACK, 4]),
-                op=ALU.add,
-            )
-            return grouped
-
-        b_bf = center_woven(768, 256)
-        a_bf = center_woven(640, 128)
+        own = center("vector", 640, 384)
+        b_bf = weave("vector", 768, 256, own[:, :, 128:])
+        a_bf = weave("vector", 640, 128, own[:, :, :128])
         first = center("scalar", 0, 256)
         second = center("scalar", 256, 256)
         third = center("scalar", 512, 128)

@@ -23,21 +23,20 @@ PASSES = K // K_PASS
 HALF = S // 2
 PAIRS = 2
 X_RUNS = {
-    (0, 0): ((2048, 1376),),
-    (0, 1): ((1024, 0), (1024, 688)),
-    (1, 0): ((1024, 256), (1024, 688)),
-    (1, 1): ((768, 0), (928, 608), (352, 352)),
+    (0, 0): ((1024, 688), (1024, 688)),
+    (0, 1): ((1024, 640), (1024, 688)),
+    (1, 0): ((1024, 0), (1024, 512)),
+    (1, 1): ((640, 0), (640, 0), (384, 384), (384, 256)),
 }
-W_SHARE = 64
-W_LAST = 96
-LATE = 256
-QUARTER = 256
+W_PARTS = (0, 48, 128)
+W_LAST = 80
 
 
 def tile_picked_deepset_relu_e_kernel(tc, xT, w1, w2_words, w2_scales, offs, out):
     nc = tc.nc
     with ExitStack() as ctx:
         keep = ctx.enter_context(tc.tile_pool(name="keep", bufs=1))
+        held = ctx.enter_context(tc.tile_pool(name="held", bufs=1))
         psum = ctx.enter_context(tc.psum_pool(name="psum", bufs=1))
 
         offsets = keep.tile([P, S // 16], U16, name="offsets")
@@ -65,6 +64,16 @@ def tile_picked_deepset_relu_e_kernel(tc, xT, w1, w2_words, w2_scales, offs, out
                 c0 = 0
                 if (g, u) == (1, 0):
                     w_raw[0] = load_w(0)
+                if g == 0:
+                    raw = keep.tile([P, 2 * T], F32, name="x_raw_%d_%d" % (g, u), align_bytes=64)
+                    stream = rows[:, 2 * u : 2 * u + 2, :].rearrange("p j c -> p (j c)")
+                    done = 0
+                    for width, share in runs:
+                        nc.sync.dma_start(out=raw[:, done : T + c0 + width], in_=stream[:, done : T + c0 + width])
+                        x_raw[g, u, c0] = raw[:].rearrange("p (j c) -> p j c", j=2)[:, :, c0 : c0 + width]
+                        c0 = c0 + width
+                        done = T + c0
+                    runs = ()
                 for width, share in runs:
                     raw = keep.tile([P, 2, width], F32, name="x_raw_%d_%d_%d" % (g, u, c0), tag="x_raw_%d_%d_%d" % (g, u, c0), align_bytes=64)
                     nc.sync.dma_start(out=raw[:], in_=rows[:, 2 * u : 2 * u + 2, c0 : c0 + width])
@@ -74,8 +83,12 @@ def tile_picked_deepset_relu_e_kernel(tc, xT, w1, w2_words, w2_scales, offs, out
                     nc.sync.dma_start(offsets[:], offs)
         w_rows = w1[K_PASS:, :].rearrange("(p j) c -> p j c", j=PACK)
         w_part = []
-        for c0, c1 in ((0, PACK * W_SHARE), (PACK * W_SHARE, H)):
-            raw = keep.tile([P, PACK, c1 - c0], F32, name="w_part_%d" % c0, tag="w_part_%d" % c0, align_bytes=64)
+        for i in range(2):
+            c0, c1 = PACK * W_PARTS[i], PACK * W_PARTS[i + 1]
+            if i == 0:
+                raw = held.tile([P, PACK, c1 - c0], F32, name="w_part_%d" % c0, offset=2560, align_bytes=64)
+            else:
+                raw = keep.tile([P, PACK, c1 - c0], F32, name="w_part_%d" % c0, align_bytes=64)
             nc.sync.dma_start(out=raw[:], in_=w_rows[:, :, c0:c1])
             w_part.append(raw)
         nc.sync.dma_start(out=w2_codes[:].bitcast(I32), in_=w2_words[0].bitcast(I32))
@@ -88,14 +101,17 @@ def tile_picked_deepset_relu_e_kernel(tc, xT, w1, w2_words, w2_scales, offs, out
             if engine == "vector":
                 nc.vector.tensor_copy(out=dst, in_=src)
             else:
-                nc.scalar.activation(out=dst, in_=src, func=ACT.Copy)
+                nc.scalar.copy(out=dst, in_=src)
 
         x_pairs = {}
-        got = [keep.tile([P, PAIRS, S], U32, name="got_%d" % g) for g in range(PASSES)]
+        got = {}
+        for g in range(PASSES):
+            for half in range(2):
+                got[g, half] = keep.tile([P, PAIRS, HALF], U32, name="got_%d_%d" % (g, half), tag="got_%d_%d" % (g, half), align_bytes=64)
         x_words = {}
         x_scales = {}
 
-        def round_x(g, u, r0=0, r1=2):
+        def round_x(g, u, r0=0, r1=4):
             if r0 == 0:
                 x_pairs[g, u] = keep.tile([P, T], U32, name="x_pairs_%d_%d" % (g, u), tag="x_pairs_%d_%d" % (g, u), align_bytes=64)
             pairs = x_pairs[g, u][:].bitcast(BF16).rearrange("p (c j) -> p c j", j=2)
@@ -109,18 +125,22 @@ def tile_picked_deepset_relu_e_kernel(tc, xT, w1, w2_words, w2_scales, offs, out
                     nc.vector.tensor_copy(out=dst[:, :share, :], in_=src[:, :share, :])
                 c0 = c0 + width
 
-        def gather(g, u, e0, e1):
-            nc.vector.tensor_copy(got[g][:, u, e0:e1], x_pairs[g, u][:].indirect(offsets[:, e0 // 16 : e1 // 16]))
+        def gather(g, u, half):
+            e0 = half * HALF
+            nc.vector.tensor_copy(got[g, half][:, u, :], x_pairs[g, u][:].indirect(offsets[:, e0 // 16 : (e0 + HALF) // 16]))
 
-        def join(engine, g, e0, width, tag):
-            grouped = keep.tile([P, width * PACK], BF16, name="x_bf_%d_%d" % (g, e0), tag=tag, align_bytes=64)
-            cols = slice(e0, e0 + width)
+        def join(engine, g, e0, width, offset):
+            if offset is None:
+                grouped = keep.tile([P, width * PACK], BF16, name="x_bf_%d_%d" % (g, e0), align_bytes=64)
+            else:
+                grouped = held.tile([P, width * PACK], BF16, name="x_bf_%d_%d" % (g, e0), offset=offset, align_bytes=64)
+            src = got[g, e0 // HALF]
             if engine == "vector":
                 dst = grouped[:].bitcast(I32).rearrange("p (c u) -> p c u", u=PAIRS)
-                nc.vector.tensor_copy(out=dst, in_=got[g][:].bitcast(I32)[:, :, cols].rearrange("p u c -> p c u"))
+                nc.vector.tensor_copy(out=dst, in_=src[:].bitcast(I32).rearrange("p u c -> p c u"))
             else:
                 dst = grouped[:].bitcast(U32).rearrange("p (c u) -> p c u", u=PAIRS)
-                nc.scalar.copy(out=dst, in_=got[g][:, :, cols].rearrange("p u c -> p c u"))
+                nc.scalar.copy(out=dst, in_=src[:].rearrange("p u c -> p c u"))
             return grouped
 
         def codes(g, half, tag):
@@ -143,14 +163,19 @@ def tile_picked_deepset_relu_e_kernel(tc, xT, w1, w2_words, w2_scales, offs, out
             else:
                 nc.scalar.activation(out=dst, in_=src, func=ACT.Copy)
 
-        def quantize_w(g, t0, count, tag):
+        def quantize_w(g, t0, steps, tag):
+            count = sum(steps)
             words = keep.tile([P, count * P], U32, name="w_words_%d_%d" % (g, t0), tag=tag, align_bytes=64)
             scales = keep.tile([P, count * P], U8, name="w_scales_%d_%d" % (g, t0), align_bytes=64)
-            nc.vector.quantize_mx(
-                out=words[:].bitcast(FP8X4),
-                scales=scales[:],
-                in_=w_bf[g][:, t0 : t0 + count, :, :].rearrange("p t m j -> p (t m j)"),
-            )
+            t = 0
+            for step in steps:
+                cols = slice(t * P, (t + step) * P)
+                nc.vector.quantize_mx(
+                    out=words[:, cols].bitcast(FP8X4),
+                    scales=scales[:, cols],
+                    in_=w_bf[g][:, t0 + t : t0 + t + step, :, :].rearrange("p t m j -> p (t m j)"),
+                )
+                t = t + step
             for t in range(count):
                 w_words[g, t0 + t] = words[:, t * P : (t + 1) * P]
                 w_scales[g, t0 + t] = scales[:, t * P : (t + 1) * P]
@@ -172,78 +197,87 @@ def tile_picked_deepset_relu_e_kernel(tc, xT, w1, w2_words, w2_scales, offs, out
             )
 
         round_x(0, 0)
-        gather(0, 0, 0, S)
+        gather(0, 0, 0)
+        gather(0, 0, 1)
         round_x(0, 1)
-        gather(0, 1, 0, S)
+        gather(0, 1, 0)
+        gather(0, 1, 1)
         round_w("scalar", 0, 0, P, w_raw[0][:])
-        early = join("vector", 0, 0, HALF, "x_bf_0_0")
-        middle = join("vector", 0, HALF, HALF - LATE, "x_bf_0_1")
+        early = join("vector", 0, 0, HALF, None)
+        middle = join("vector", 0, HALF, HALF, None)
+        quantize_w(0, 0, (2,), "w_words_0")
         codes(0, 0, "x_words_0_0")
         quantize_x(0, 0, 0, HALF, early[:])
-        quantize_w(0, 0, PACK, "w_words_0")
-        for t in range(PACK):
-            product(0, t, 0)
         round_x(1, 0)
         codes(0, 1, "x_words_0_1")
-        quantize_x(0, 1, 0, HALF - LATE, middle[:])
-        gather(1, 0, 0, S)
+        quantize_x(0, 1, 0, HALF, middle[:])
+        for half in range(2):
+            for t in range(2):
+                product(0, t, half)
+        gather(1, 0, 0)
+        gather(1, 0, 1)
         round_x(1, 1)
-        late = join("scalar", 0, S - LATE, LATE, "x_raw_1_1_768")
-        round_x(1, 1, 2, 3)
-        quantize_x(0, 1, HALF - LATE, LATE, late[:])
-        for t in range(PACK):
-            product(0, t, 1)
-        round_w("scalar", 1, 0, W_SHARE, w_part[0][:])
-        gather(1, 1, 0, HALF)
-        first_half = join("scalar", 1, 0, HALF, "w_part_0")
-        gather(1, 1, HALF, S)
-        round_w("vector", 1, W_SHARE, W_LAST, w_part[1][:, :, : PACK * (W_LAST - W_SHARE)])
-        round_w("scalar", 1, W_LAST, P, w_part[1][:, :, PACK * (W_LAST - W_SHARE) :])
-        second_half = join("scalar", 1, HALF, HALF, "w_part_%d" % (PACK * W_SHARE))
+        round_w("scalar", 1, W_PARTS[0], W_PARTS[1], w_part[0][:])
+        gather(1, 1, 0)
+        quantize_w(0, 2, (2,), "x_raw_1_1_1664")
+        for half in range(2):
+            for t in range(2, PACK):
+                product(0, t, half)
+        first_half = join("scalar", 1, 0, HALF, 0)
+        gather(1, 1, 1)
+        cut = PACK * (W_LAST - W_PARTS[1])
+        round_w("scalar", 1, W_PARTS[1], W_LAST, w_part[1][:, :, :cut])
+        second_half = join("scalar", 1, HALF, HALF, 4096)
+        round_w("vector", 1, W_LAST, P, w_part[1][:, :, cut:])
         codes(1, 0, "x_words_1_0")
         quantize_x(1, 0, 0, HALF, first_half[:])
-        for t in range(PACK):
-            quantize_w(1, t, 1, "w_words_1_%d" % t)
-        codes(1, 1, "w_bf_1")
+        quantize_w(1, 0, (1, 1, 2), "got_1_0")
+        codes(1, 1, "x_words_1_1")
         quantize_x(1, 1, 0, HALF, second_half[:])
 
-        h = [keep.tile([P, PACK, HALF], F32, name="h_%d" % half) for half in range(2)]
-        part = [keep.tile([P, PACK], F32, name="part_%d" % half) for half in range(2)]
-        total = keep.tile([P, PACK], F32, name="total")
+        h = [keep.tile([P, S], F32, name="h_%d" % t) for t in range(PACK)]
+        part = keep.tile([P, PACK], F32, name="part")
+        total = [keep.tile([P, 1], F32, name="total_%d" % t) for t in range(PACK)]
+        planes = keep.tile([P, PACK, S], BF16, name="z_planes")
 
         def empty(engine, t, half, sums, start):
-            product(1, t, half)
+            dst = h[t][:, half * HALF : (half + 1) * HALF]
             if engine == "scalar":
-                nc.scalar.activation(out=h[half][:, t, :], in_=banks[t, half][:], func=ACT.Relu, accum_out=sums[:, t : t + 1])
+                nc.scalar.activation(out=dst, in_=banks[t, half][:], func=ACT.Relu, accum_out=sums)
             else:
                 nc.vector.tensor_scalar(
-                    out=h[half][:, t, :], in0=banks[t, half][:], scalar1=0.0, scalar2=start, op0=ALU.max, op1=ALU.add,
-                    accum_out=sums[:, t : t + 1],
+                    out=dst, in0=banks[t, half][:], scalar1=0.0, scalar2=start, op0=ALU.max, op1=ALU.add, accum_out=sums
                 )
 
-        empty("scalar", 0, 0, part[0], None)
-        empty("scalar", 1, 0, part[0], None)
-        empty("vector", 2, 0, part[0], None)
-        empty("vector", 3, 0, part[0], None)
-        empty("scalar", 1, 1, part[1], None)
-        empty("vector", 0, 1, total, part[0][:, 0:1])
-        empty("scalar", 2, 1, part[1], None)
-        empty("scalar", 3, 1, part[1], None)
-        nc.vector.tensor_tensor(out=total[:, 1:3], in0=part[0][:, 1:3], in1=part[1][:, 1:3], op=ALU.add)
-        nc.scalar.activation(out=total[:, 3:4], in_=part[1][:, 3:4], func=ACT.Identity, bias=part[0][:, 3:4])
+        def center(engine, t, c0, c1):
+            if engine == "vector":
+                nc.vector.tensor_scalar(
+                    out=planes[:, t, c0:c1], in0=h[t][:, c0:c1], scalar1=-float(S), scalar2=total[t][:], op0=ALU.mult, op1=ALU.add
+                )
+            else:
+                nc.scalar.activation(out=planes[:, t, c0:c1], in_=h[t][:, c0:c1], func=ACT.Identity, bias=total[t][:], scale=-float(S))
 
-        def center(engine, c0, width):
-            half, h0 = divmod(c0, HALF)
-            planes = keep.tile([P, PACK, width], BF16, name="z_planes_%d" % c0)
-            for t in range(PACK):
-                src = h[half][:, t, h0 : h0 + width]
-                if engine == "vector":
-                    nc.vector.tensor_scalar(
-                        out=planes[:, t, :], in0=src, scalar1=-float(S), scalar2=total[:, t : t + 1], op0=ALU.mult, op1=ALU.add
-                    )
-                else:
-                    nc.scalar.activation(out=planes[:, t, :], in_=src, func=ACT.Identity, bias=total[:, t : t + 1], scale=-float(S))
-            return planes
+        for t in range(PACK):
+            product(1, t, 0)
+        for t in (0, 2, 1, 3):
+            product(1, t, 1)
+        other = keep.tile([P, 1], F32, name="other")
+        for t in range(3):
+            empty("scalar", t, 0, part[:, t : t + 1], None)
+        empty("vector", 3, 0, part[:, 3:4], None)
+        empty("vector", 0, 1, total[0][:], part[:, 0:1])
+        empty("scalar", 2, 1, other[:], None)
+        empty("vector", 1, 1, total[1][:], part[:, 1:2])
+        empty("vector", 3, 1, total[3][:], part[:, 3:4])
+        nc.vector.tensor_tensor(out=total[2][:], in0=part[:, 2:3], in1=other[:], op=ALU.add)
+        center("scalar", 0, 0, S)
+        center("vector", 1, 0, HALF)
+        center("scalar", 1, HALF, S)
+        center("vector", 3, 0, HALF)
+        center("vector", 2, 0, HALF)
+        center("scalar", 2, 768, S)
+        center("scalar", 2, HALF, 768)
+        center("vector", 3, HALF, S)
 
         def weave(engine, c0, width, planes):
             grouped = keep.tile([P, width, PACK], BF16, name="z_bf_%d" % c0, align_bytes=64)
@@ -276,22 +310,17 @@ def tile_picked_deepset_relu_e_kernel(tc, xT, w1, w2_words, w2_scales, offs, out
                 nc.scalar.activation(out=result[:], in_=acc[:], func=ACT.Copy, scale=-1.0 / S)
             queue.dma_start(out=out[:, c0 : c0 + width], in_=result[:])
 
-        own = center("vector", 640, 384)
-        b_bf = weave("vector", 768, 256, own[:, :, 128:])
-        a_bf = weave("vector", 640, 128, own[:, :, :128])
-        first = center("scalar", 0, 256)
-        second = center("scalar", 256, 256)
-        third = center("scalar", 512, 128)
-        third_bf = weave("scalar", 512, 128, third[:])
-        acc_b = finish("vector", 768, 256, b_bf)
-        acc_a = finish("vector", 640, 128, a_bf)
-        first_bf = weave("vector", 0, 256, first[:])
-        second_bf = weave("vector", 256, 256, second[:])
-        acc_first = finish("vector", 0, 256, first_bf)
-        acc_second = finish("vector", 256, 256, second_bf)
-        acc_third = finish("vector", 512, 128, third_bf)
-        store("scalar", nc.sync, 768, 256, acc_b)
-        store("scalar", nc.sync, 640, 128, acc_a)
-        store("scalar", nc.sync, 0, 256, acc_first)
-        store("scalar", nc.sync, 256, 256, acc_second)
-        store("vector", nc.sync, 512, 128, acc_third)
+        z_bf = {}
+        acc = {}
+        z_bf[768] = weave("scalar", 768, 256, planes[:, :, 768:1024])
+        z_bf[512] = weave("scalar", 512, 128, planes[:, :, 512:640])
+        z_bf[640] = weave("scalar", 640, 128, planes[:, :, 640:768])
+        z_bf[0] = weave("vector", 0, 256, planes[:, :, 0:256])
+        z_bf[256] = weave("vector", 256, 256, planes[:, :, 256:512])
+        for c0, width in ((0, 256), (256, 256), (768, 256), (512, 128), (640, 128)):
+            acc[c0] = finish("vector", c0, width, z_bf[c0])
+        store("scalar", nc.sync, 0, 256, acc[0])
+        store("scalar", nc.sync, 256, 256, acc[256])
+        store("scalar", nc.sync, 768, 256, acc[768])
+        store("scalar", nc.sync, 512, 128, acc[512])
+        store("vector", nc.sync, 640, 128, acc[640])

@@ -25,8 +25,8 @@ PAIRS = 2
 X_RUNS = {
     (0, 0): ((1024, 688), (1024, 688)),
     (0, 1): ((1024, 640), (1024, 688)),
-    (1, 0): ((1024, 0), (1024, 512)),
-    (1, 1): ((640, 0), (640, 0), (384, 384), (384, 256)),
+    (1, 0): ((512, 0), (768, 0), (768, 768)),
+    (1, 1): ((512, 0), (1024, 640), (512, 400)),
 }
 W_PARTS = (0, 48, 128)
 W_LAST = 80
@@ -64,21 +64,14 @@ def tile_picked_deepset_relu_e_kernel(tc, xT, w1, w2_words, w2_scales, offs, out
                 c0 = 0
                 if (g, u) == (1, 0):
                     w_raw[0] = load_w(0)
-                if g == 0:
-                    raw = keep.tile([P, 2 * T], F32, name="x_raw_%d_%d" % (g, u), align_bytes=64)
-                    stream = rows[:, 2 * u : 2 * u + 2, :].rearrange("p j c -> p (j c)")
-                    done = 0
-                    for width, share in runs:
-                        nc.sync.dma_start(out=raw[:, done : T + c0 + width], in_=stream[:, done : T + c0 + width])
-                        x_raw[g, u, c0] = raw[:].rearrange("p (j c) -> p j c", j=2)[:, :, c0 : c0 + width]
-                        c0 = c0 + width
-                        done = T + c0
-                    runs = ()
+                raw = keep.tile([P, 2 * T], F32, name="x_raw_%d_%d" % (g, u), tag="x_raw_%d_%d" % (g, u), align_bytes=64)
+                stream = rows[:, 2 * u : 2 * u + 2, :].rearrange("p j c -> p (j c)")
+                done = 0
                 for width, share in runs:
-                    raw = keep.tile([P, 2, width], F32, name="x_raw_%d_%d_%d" % (g, u, c0), tag="x_raw_%d_%d_%d" % (g, u, c0), align_bytes=64)
-                    nc.sync.dma_start(out=raw[:], in_=rows[:, 2 * u : 2 * u + 2, c0 : c0 + width])
-                    x_raw[g, u, c0] = raw[:]
+                    nc.sync.dma_start(out=raw[:, done : T + c0 + width], in_=stream[:, done : T + c0 + width])
+                    x_raw[g, u, c0] = raw[:].rearrange("p (j c) -> p j c", j=2)[:, :, c0 : c0 + width]
                     c0 = c0 + width
+                    done = T + c0
                 if g == 0 and u == 0:
                     nc.sync.dma_start(offsets[:], offs)
         w_rows = w1[K_PASS:, :].rearrange("(p j) c -> p j c", j=PACK)
@@ -130,8 +123,8 @@ def tile_picked_deepset_relu_e_kernel(tc, xT, w1, w2_words, w2_scales, offs, out
             nc.vector.tensor_copy(got[g, half][:, u, :], x_pairs[g, u][:].indirect(offsets[:, e0 // 16 : (e0 + HALF) // 16]))
 
         def join(engine, g, e0, width, offset):
-            if offset is None:
-                grouped = keep.tile([P, width * PACK], BF16, name="x_bf_%d_%d" % (g, e0), align_bytes=64)
+            if g == 0:
+                grouped = keep.tile([P, width * PACK], BF16, name="x_bf_%d_%d" % (g, e0), tag=offset, align_bytes=64)
             else:
                 grouped = held.tile([P, width * PACK], BF16, name="x_bf_%d_%d" % (g, e0), offset=offset, align_bytes=64)
             src = got[g, e0 // HALF]
@@ -203,8 +196,8 @@ def tile_picked_deepset_relu_e_kernel(tc, xT, w1, w2_words, w2_scales, offs, out
         gather(0, 1, 0)
         gather(0, 1, 1)
         round_w("scalar", 0, 0, P, w_raw[0][:])
-        early = join("vector", 0, 0, HALF, None)
-        middle = join("vector", 0, HALF, HALF, None)
+        early = join("vector", 0, 0, HALF, "x_bf_0_0")
+        middle = join("vector", 0, HALF, HALF, "x_bf_0_1")
         quantize_w(0, 0, (2,), "w_words_0")
         codes(0, 0, "x_words_0_0")
         quantize_x(0, 0, 0, HALF, early[:])
@@ -219,7 +212,7 @@ def tile_picked_deepset_relu_e_kernel(tc, xT, w1, w2_words, w2_scales, offs, out
         round_x(1, 1)
         round_w("scalar", 1, W_PARTS[0], W_PARTS[1], w_part[0][:])
         gather(1, 1, 0)
-        quantize_w(0, 2, (2,), "x_raw_1_1_1664")
+        quantize_w(0, 2, (2,), "x_raw_1_1")
         for half in range(2):
             for t in range(2, PACK):
                 product(0, t, half)

@@ -22,21 +22,13 @@ K_PASS = P * PACK
 PASSES = K // K_PASS
 HALF = S // 2
 PAIRS = 2
-X_RUNS = {
-    (0, 0): ((1024, 688), (1024, 688)),
-    (0, 1): ((1024, 640), (1024, 688)),
-    (1, 0): ((512, 0), (768, 0), (768, 768)),
-    (1, 1): ((512, 0), (1024, 640), (512, 400)),
-}
-W_PARTS = (0, 48, 128)
-W_LAST = 80
+DIRECT = (256, 256, 256, 256, 256, 256, 512, 512)
 
 
 def tile_picked_deepset_relu_e_kernel(tc, xT, w1, w2_words, w2_scales, offs, out):
     nc = tc.nc
     with ExitStack() as ctx:
         keep = ctx.enter_context(tc.tile_pool(name="keep", bufs=1))
-        held = ctx.enter_context(tc.tile_pool(name="held", bufs=1))
         psum = ctx.enter_context(tc.psum_pool(name="psum", bufs=1))
 
         offsets = keep.tile([P, S // 16], U16, name="offsets")
@@ -44,46 +36,24 @@ def tile_picked_deepset_relu_e_kernel(tc, xT, w1, w2_words, w2_scales, offs, out
         w2_codes = keep.tile([P, 2 * N], U8, name="w2_codes", align_bytes=64)
         nc.vector.memset(w2_plane[:].bitcast(I32), 0)
 
-        table_in = keep.tile([P, 1], F32, name="table_in")
-        table_out = keep.tile([P, 1], F32, name="table_out")
-        nc.vector.memset(table_in[:], 0.0)
-        nc.scalar.activation(out=table_out[:], in_=table_in[:], func=ACT.Relu)
-
-        def load_w(g):
-            rows = w1[g * K_PASS : (g + 1) * K_PASS, :].rearrange("(p j) c -> p j c", j=PACK)
-            raw = keep.tile([P, PACK, H], F32, name="w_raw_%d" % g, tag="w_raw_%d" % g, align_bytes=64)
-            nc.sync.dma_start(out=raw[:], in_=rows)
-            return raw
-
-        x_raw = {}
-        w_raw = {}
-        for g in range(PASSES):
+        x_raw = []
+        for plane in range(PASSES * PACK):
+            g, j = divmod(plane, PACK)
+            if plane == PASSES * PACK - 1:
+                w_first = keep.tile([P, PACK * H], F32, name="w_first", align_bytes=64)
+                nc.sync.dma_start(out=w_first[:], in_=w1[:K_PASS, :].rearrange("(p j) c -> p (j c)", j=PACK))
             rows = xT[g * K_PASS : (g + 1) * K_PASS, :].rearrange("(p j) c -> p j c", j=PACK)
-            for u in range(PAIRS):
-                runs = X_RUNS[g, u]
-                c0 = 0
-                if (g, u) == (1, 0):
-                    w_raw[0] = load_w(0)
-                raw = keep.tile([P, 2 * T], F32, name="x_raw_%d_%d" % (g, u), tag="x_raw_%d_%d" % (g, u), align_bytes=64)
-                stream = rows[:, 2 * u : 2 * u + 2, :].rearrange("p j c -> p (j c)")
-                done = 0
-                for width, share in runs:
-                    nc.sync.dma_start(out=raw[:, done : T + c0 + width], in_=stream[:, done : T + c0 + width])
-                    x_raw[g, u, c0] = raw[:].rearrange("p (j c) -> p j c", j=2)[:, :, c0 : c0 + width]
-                    c0 = c0 + width
-                    done = T + c0
-                if g == 0 and u == 0:
-                    nc.sync.dma_start(offsets[:], offs)
-        w_rows = w1[K_PASS:, :].rearrange("(p j) c -> p j c", j=PACK)
-        w_part = []
-        for i in range(2):
-            c0, c1 = PACK * W_PARTS[i], PACK * W_PARTS[i + 1]
-            if i == 0:
-                raw = held.tile([P, PACK, c1 - c0], F32, name="w_part_%d" % c0, offset=2560, align_bytes=64)
-            else:
-                raw = keep.tile([P, PACK, c1 - c0], F32, name="w_part_%d" % c0, align_bytes=64)
-            nc.sync.dma_start(out=raw[:], in_=w_rows[:, :, c0:c1])
-            w_part.append(raw)
+            raw = keep.tile([P, T], F32, name="x_raw_%d" % plane, align_bytes=64)
+            nc.sync.dma_start(out=raw[:], in_=rows[:, j, :])
+            x_raw.append(raw)
+            if plane == 0:
+                nc.sync.dma_start(offsets[:], offs)
+        w_rows = w1[K_PASS:, :].rearrange("(p j) c -> p (j c)", j=PACK)
+        w_pair = []
+        for u in range(PAIRS):
+            raw = keep.tile([P, 2 * H], F32, name="w_pair_%d" % u, tag="w_pair_%d" % u, align_bytes=64)
+            nc.sync.dma_start(out=raw[:], in_=w_rows[:, 2 * u * H : 2 * (u + 1) * H])
+            w_pair.append(raw)
         nc.sync.dma_start(out=w2_codes[:].bitcast(I32), in_=w2_words[0].bitcast(I32))
         for q in range(4):
             nc.sync.dma_start(out=w2_plane[32 * q : 32 * q + 4, :].bitcast(I32), in_=w2_scales[0, 4 * q : 4 * q + 4, :].bitcast(I32))
@@ -96,80 +66,59 @@ def tile_picked_deepset_relu_e_kernel(tc, xT, w1, w2_words, w2_scales, offs, out
             else:
                 nc.scalar.copy(out=dst, in_=src)
 
-        x_pairs = {}
-        got = {}
-        for g in range(PASSES):
-            for half in range(2):
-                got[g, half] = keep.tile([P, PAIRS, HALF], U32, name="got_%d_%d" % (g, half), tag="got_%d_%d" % (g, half), align_bytes=64)
+        woven = {}
         x_words = {}
         x_scales = {}
+        for g in range(PASSES):
+            for half in range(2):
+                woven[g, half] = keep.tile([P, HALF, PACK], BF16, name="x_bf_%d_%d" % (g, half), align_bytes=64)
+                x_scales[g, half] = keep.tile([P, HALF], U8, name="x_scales_%d_%d" % (g, half), align_bytes=64)
+        picked = [keep.tile([P, PACK, S], BF16, name="picked_%d" % g, align_bytes=64) for g in range(PASSES)]
 
-        def round_x(g, u, r0=0, r1=4):
-            if r0 == 0:
-                x_pairs[g, u] = keep.tile([P, T], U32, name="x_pairs_%d_%d" % (g, u), tag="x_pairs_%d_%d" % (g, u), align_bytes=64)
-            pairs = x_pairs[g, u][:].bitcast(BF16).rearrange("p (c j) -> p c j", j=2)
-            c0 = sum(width for width, share in X_RUNS[g, u][:r0])
-            for width, share in X_RUNS[g, u][r0:r1]:
-                dst = pairs[:, c0 : c0 + width, :]
-                src = x_raw[g, u, c0].rearrange("p j c -> p c j")
-                if share < width:
-                    nc.scalar.activation(out=dst[:, share:, :], in_=src[:, share:, :], func=ACT.Copy)
-                if share > 0:
-                    nc.vector.tensor_copy(out=dst[:, :share, :], in_=src[:, :share, :])
-                c0 = c0 + width
+        def gather(plane):
+            g, j = divmod(plane, PACK)
+            direct = DIRECT[plane]
+            nc.vector.tensor_copy(out=woven[g, 0][:, :direct, j], in_=x_raw[plane][:].indirect(offsets[:, : direct // 16]))
+            nc.scalar.activation(out=picked[g][:, j, direct:], in_=x_raw[plane][:].indirect(offsets[:, direct // 16 :]), func=ACT.Copy)
 
-        def gather(g, u, half):
-            e0 = half * HALF
-            nc.vector.tensor_copy(got[g, half][:, u, :], x_pairs[g, u][:].indirect(offsets[:, e0 // 16 : (e0 + HALF) // 16]))
+        def weave_x(g, e0, e1, j0, j1):
+            half = e0 // HALF
+            interleave("vector", woven[g, half][:, e0 - half * HALF : e1 - half * HALF, j0:j1], picked[g][:, j0:j1, e0:e1])
 
-        def join(engine, g, e0, width, offset):
-            if g == 0:
-                grouped = keep.tile([P, width * PACK], BF16, name="x_bf_%d_%d" % (g, e0), tag=offset, align_bytes=64)
-            else:
-                grouped = held.tile([P, width * PACK], BF16, name="x_bf_%d_%d" % (g, e0), offset=offset, align_bytes=64)
-            src = got[g, e0 // HALF]
-            if engine == "vector":
-                dst = grouped[:].bitcast(I32).rearrange("p (c u) -> p c u", u=PAIRS)
-                nc.vector.tensor_copy(out=dst, in_=src[:].bitcast(I32).rearrange("p u c -> p c u"))
-            else:
-                dst = grouped[:].bitcast(U32).rearrange("p (c u) -> p c u", u=PAIRS)
-                nc.scalar.copy(out=dst, in_=src[:].rearrange("p u c -> p c u"))
-            return grouped
-
-        def codes(g, half, tag):
+        def quantize_x(g, half, tag):
             x_words[g, half] = keep.tile([P, HALF], U32, name="x_words_%d_%d" % (g, half), tag=tag, align_bytes=64)
-            x_scales[g, half] = keep.tile([P, HALF], U8, name="x_scales_%d_%d" % (g, half), align_bytes=64)
-
-        def quantize_x(g, half, c0, width, grouped):
-            cols = slice(c0, c0 + width)
-            nc.vector.quantize_mx(out=x_words[g, half][:, cols].bitcast(FP8X4), scales=x_scales[g, half][:, cols], in_=grouped)
+            nc.vector.quantize_mx(
+                out=x_words[g, half][:].bitcast(FP8X4), scales=x_scales[g, half][:], in_=woven[g, half][:].rearrange("p c j -> p (c j)")
+            )
 
         w_words = {}
         w_scales = {}
-        w_bf = [keep.tile([P, PACK, P, PACK], BF16, name="w_bf_%d" % g, tag="w_bf_%d" % g, align_bytes=64) for g in range(PASSES)]
+        w_bf = {}
+        for g in range(PASSES):
+            for t0 in (0, 2):
+                w_bf[g, t0] = keep.tile([P, 2, P, PACK], BF16, name="w_bf_%d_%d" % (g, t0), align_bytes=64)
 
-        def round_w(engine, g, m0, m1, raw):
-            dst = w_bf[g][:, :, m0:m1, :].rearrange("p t m j -> p m j t")
-            src = raw.rearrange("p j (m t) -> p m j t", t=PACK)
+        def round_w(engine, g, t0, j0, j1, raw):
+            dst = w_bf[g, t0][:, :, :, j0:j1].rearrange("p t m j -> p m j t")
+            src = raw[:].rearrange("p (j m t) -> p m j t", m=P, t=PACK)[:, :, :, t0 : t0 + 2]
             if engine == "vector":
                 nc.vector.tensor_copy(out=dst, in_=src)
             else:
                 nc.scalar.activation(out=dst, in_=src, func=ACT.Copy)
 
-        def quantize_w(g, t0, steps, tag):
-            count = sum(steps)
-            words = keep.tile([P, count * P], U32, name="w_words_%d_%d" % (g, t0), tag=tag, align_bytes=64)
-            scales = keep.tile([P, count * P], U8, name="w_scales_%d_%d" % (g, t0), align_bytes=64)
+        def quantize_w(g, t0, steps):
+            words = keep.tile([P, 2 * P], U32, name="w_words_%d_%d" % (g, t0), align_bytes=64)
+            scales = keep.tile([P, 2 * P], U8, name="w_scales_%d_%d" % (g, t0), align_bytes=64)
             t = 0
             for step in steps:
                 cols = slice(t * P, (t + step) * P)
                 nc.vector.quantize_mx(
                     out=words[:, cols].bitcast(FP8X4),
                     scales=scales[:, cols],
-                    in_=w_bf[g][:, t0 + t : t0 + t + step, :, :].rearrange("p t m j -> p (t m j)"),
+                    in_=w_bf[g, t0][:, t : t + step, :, :].rearrange("p t m j -> p (t m j)"),
                 )
                 t = t + step
-            for t in range(count):
+            for t in range(2):
                 w_words[g, t0 + t] = words[:, t * P : (t + 1) * P]
                 w_scales[g, t0 + t] = scales[:, t * P : (t + 1) * P]
 
@@ -189,44 +138,34 @@ def tile_picked_deepset_relu_e_kernel(tc, xT, w1, w2_words, w2_scales, offs, out
                 stop=(g == PASSES - 1),
             )
 
-        round_x(0, 0)
-        gather(0, 0, 0)
-        gather(0, 0, 1)
-        round_x(0, 1)
-        gather(0, 1, 0)
-        gather(0, 1, 1)
-        round_w("scalar", 0, 0, P, w_raw[0][:])
-        early = join("vector", 0, 0, HALF, "x_bf_0_0")
-        middle = join("vector", 0, HALF, HALF, "x_bf_0_1")
-        quantize_w(0, 0, (2,), "w_words_0")
-        codes(0, 0, "x_words_0_0")
-        quantize_x(0, 0, 0, HALF, early[:])
-        round_x(1, 0)
-        codes(0, 1, "x_words_0_1")
-        quantize_x(0, 1, 0, HALF, middle[:])
+        for plane in range(PACK):
+            gather(plane)
+        weave_x(0, DIRECT[0], HALF, 0, PACK)
+        weave_x(0, HALF, S, 0, PACK)
+        gather(4)
+        quantize_x(0, 0, "x_words_0_0")
+        quantize_x(0, 1, "x_words_0_1")
+        gather(5)
+        weave_x(1, DIRECT[4], HALF, 0, 2)
+        weave_x(1, HALF, S, 0, 2)
+        gather(6)
+        round_w("vector", 0, 0, 0, PACK, w_first)
+        round_w("scalar", 0, 2, 0, PACK, w_first)
+        quantize_w(0, 0, (2,))
+        quantize_w(0, 2, (2,))
         for half in range(2):
-            for t in range(2):
+            for t in range(PACK):
                 product(0, t, half)
-        gather(1, 0, 0)
-        gather(1, 0, 1)
-        round_x(1, 1)
-        round_w("scalar", 1, W_PARTS[0], W_PARTS[1], w_part[0][:])
-        gather(1, 1, 0)
-        quantize_w(0, 2, (2,), "x_raw_1_1")
-        for half in range(2):
-            for t in range(2, PACK):
-                product(0, t, half)
-        first_half = join("scalar", 1, 0, HALF, 0)
-        gather(1, 1, 1)
-        cut = PACK * (W_LAST - W_PARTS[1])
-        round_w("scalar", 1, W_PARTS[1], W_LAST, w_part[1][:, :, :cut])
-        second_half = join("scalar", 1, HALF, HALF, 4096)
-        round_w("vector", 1, W_LAST, P, w_part[1][:, :, cut:])
-        codes(1, 0, "x_words_1_0")
-        quantize_x(1, 0, 0, HALF, first_half[:])
-        quantize_w(1, 0, (1, 1, 2), "got_1_0")
-        codes(1, 1, "x_words_1_1")
-        quantize_x(1, 1, 0, HALF, second_half[:])
+        gather(7)
+        round_w("scalar", 1, 0, 0, 2, w_pair[0])
+        round_w("scalar", 1, 2, 0, 2, w_pair[0])
+        weave_x(1, HALF, S, 2, PACK)
+        round_w("vector", 1, 0, 2, PACK, w_pair[1])
+        round_w("scalar", 1, 2, 2, PACK, w_pair[1])
+        quantize_x(1, 0, "w_pair_0")
+        quantize_w(1, 0, (1, 1))
+        quantize_w(1, 2, (2,))
+        quantize_x(1, 1, "w_pair_1")
 
         h = [keep.tile([P, S], F32, name="h_%d" % t) for t in range(PACK)]
         part = keep.tile([P, PACK], F32, name="part")

@@ -160,9 +160,9 @@ def tile_picked_deepset_relu_e_kernel(tc, xT, w1, w2_words, w2_scales, offs, out
         round_w("scalar", 1, 0, 0, 2, w_pair[0])
         round_w("scalar", 1, 2, 0, 2, w_pair[0])
         weave_x(1, HALF, S, 2, PACK)
+        quantize_x(1, 0, "x_words_1_0")
         round_w("vector", 1, 0, 2, PACK, w_pair[1])
         round_w("scalar", 1, 2, 2, PACK, w_pair[1])
-        quantize_x(1, 0, "w_pair_0")
         quantize_w(1, 0, (1, 1))
         quantize_w(1, 2, (2,))
         quantize_x(1, 1, "w_pair_1")
@@ -186,6 +186,10 @@ def tile_picked_deepset_relu_e_kernel(tc, xT, w1, w2_words, w2_scales, offs, out
                 nc.vector.tensor_scalar(
                     out=planes[:, t, c0:c1], in0=h[t][:, c0:c1], scalar1=-float(S), scalar2=total[t][:], op0=ALU.mult, op1=ALU.add
                 )
+            elif engine == "gpsimd":
+                nc.gpsimd.tensor_scalar(
+                    out=planes[:, t, c0:c1], in0=h[t][:, c0:c1], scalar1=-float(S), scalar2=total[t][:], op0=ALU.mult, op1=ALU.add
+                )
             else:
                 nc.scalar.activation(out=planes[:, t, c0:c1], in_=h[t][:, c0:c1], func=ACT.Identity, bias=total[t][:], scale=-float(S))
 
@@ -194,22 +198,24 @@ def tile_picked_deepset_relu_e_kernel(tc, xT, w1, w2_words, w2_scales, offs, out
         for t in (0, 2, 1, 3):
             product(1, t, 1)
         other = keep.tile([P, 1], F32, name="other")
-        for t in range(3):
-            empty("scalar", t, 0, part[:, t : t + 1], None)
-        empty("vector", 3, 0, part[:, 3:4], None)
+        empty("scalar", 0, 0, part[:, 0:1], None)
+        empty("vector", 1, 0, part[:, 1:2], None)
+        empty("scalar", 2, 0, part[:, 2:3], None)
+        empty("scalar", 3, 0, part[:, 3:4], None)
         empty("vector", 0, 1, total[0][:], part[:, 0:1])
         empty("scalar", 2, 1, other[:], None)
         empty("vector", 1, 1, total[1][:], part[:, 1:2])
         empty("vector", 3, 1, total[3][:], part[:, 3:4])
-        nc.vector.tensor_tensor(out=total[2][:], in0=part[:, 2:3], in1=other[:], op=ALU.add)
-        center("scalar", 0, 0, S)
-        center("vector", 1, 0, HALF)
+        center("gpsimd", 0, 0, 704)
+        center("scalar", 0, 704, S)
+        nc.scalar.activation(out=total[2][:], in_=part[:, 2:3], func=ACT.Identity, bias=other[:])
         center("scalar", 1, HALF, S)
-        center("vector", 3, 0, HALF)
-        center("vector", 2, 0, HALF)
-        center("scalar", 2, 768, S)
-        center("scalar", 2, HALF, 768)
+        center("scalar", 2, HALF, S)
+        center("vector", 1, 0, HALF)
         center("vector", 3, HALF, S)
+        center("vector", 2, 0, HALF)
+        center("vector", 3, 0, 256)
+        center("vector", 3, 256, HALF)
 
         def weave(engine, c0, width, planes):
             grouped = keep.tile([P, width, PACK], BF16, name="z_bf_%d" % c0, align_bytes=64)

@@ -20,9 +20,15 @@ P = 128
 PACK = 4
 K_PASS = P * PACK
 PASSES = K // K_PASS
+PLANES = PASSES * PACK
+LIST_ROWS = 16
+SCALE_ROWS = 4
 HALF = S // 2
-PAIRS = 2
-DIRECT = (256, 256, 256, 256, 256, 256, 512, 512)
+QUARTER = S // 4
+EIGHTH = S // 8
+LINE = 4
+
+DIRECT = (3 * EIGHTH,) * PACK + (QUARTER, QUARTER, HALF, HALF)
 
 
 def tile_picked_deepset_relu_e_kernel(tc, xT, w1, w2_words, w2_scales, offs, out):
@@ -31,15 +37,15 @@ def tile_picked_deepset_relu_e_kernel(tc, xT, w1, w2_words, w2_scales, offs, out
         keep = ctx.enter_context(tc.tile_pool(name="keep", bufs=1))
         psum = ctx.enter_context(tc.psum_pool(name="psum", bufs=1))
 
-        offsets = keep.tile([P, S // 16], U16, name="offsets")
-        w2_plane = keep.tile([P, N], U8, name="w2_plane", align_bytes=64)
+        offsets = keep.tile([P, S // LIST_ROWS], U16, name="offsets")
+        w2_scale = keep.tile([P, N], U8, name="w2_scale", align_bytes=64)
         w2_codes = keep.tile([P, 2 * N], U8, name="w2_codes", align_bytes=64)
-        nc.vector.memset(w2_plane[:].bitcast(I32), 0)
+        nc.vector.memset(w2_scale[:].bitcast(I32), 0)
 
         x_raw = []
-        for plane in range(PASSES * PACK):
+        for plane in range(PLANES):
             g, j = divmod(plane, PACK)
-            if plane == PASSES * PACK - 1:
+            if plane == PLANES - 1:
                 w_first = keep.tile([P, PACK * H], F32, name="w_first", align_bytes=64)
                 nc.sync.dma_start(out=w_first[:], in_=w1[:K_PASS, :].rearrange("(p j) c -> p (j c)", j=PACK))
             rows = xT[g * K_PASS : (g + 1) * K_PASS, :].rearrange("(p j) c -> p j c", j=PACK)
@@ -50,17 +56,20 @@ def tile_picked_deepset_relu_e_kernel(tc, xT, w1, w2_words, w2_scales, offs, out
                 nc.sync.dma_start(offsets[:], offs)
         w_rows = w1[K_PASS:, :].rearrange("(p j) c -> p (j c)", j=PACK)
         w_pair = []
-        for u in range(PAIRS):
+        for u in range(PACK // 2):
             raw = keep.tile([P, 2 * H], F32, name="w_pair_%d" % u, tag="w_pair_%d" % u, align_bytes=64)
             nc.sync.dma_start(out=raw[:], in_=w_rows[:, 2 * u * H : 2 * (u + 1) * H])
             w_pair.append(raw)
         nc.sync.dma_start(out=w2_codes[:].bitcast(I32), in_=w2_words[0].bitcast(I32))
-        for q in range(4):
-            nc.sync.dma_start(out=w2_plane[32 * q : 32 * q + 4, :].bitcast(I32), in_=w2_scales[0, 4 * q : 4 * q + 4, :].bitcast(I32))
+        for q in range(P // 32):
+            nc.sync.dma_start(
+                out=w2_scale[32 * q : 32 * q + SCALE_ROWS, :].bitcast(I32),
+                in_=w2_scales[0, SCALE_ROWS * q : SCALE_ROWS * (q + 1), :].bitcast(I32),
+            )
 
         def interleave(engine, dst, src):
-            dst = dst.rearrange("p (c i) j -> p c j i", i=4)
-            src = src.rearrange("p j (c i) -> p c j i", i=4)
+            dst = dst.rearrange("p (c i) j -> p c j i", i=LINE)
+            src = src.rearrange("p j (c i) -> p c j i", i=LINE)
             if engine == "vector":
                 nc.vector.tensor_copy(out=dst, in_=src)
             else:
@@ -75,20 +84,27 @@ def tile_picked_deepset_relu_e_kernel(tc, xT, w1, w2_words, w2_scales, offs, out
                 x_scales[g, half] = keep.tile([P, HALF], U8, name="x_scales_%d_%d" % (g, half), align_bytes=64)
         picked = [keep.tile([P, PACK, S], BF16, name="picked_%d" % g, align_bytes=64) for g in range(PASSES)]
 
-        def gather(plane):
+        def window(plane, e0, e1):
+            return x_raw[plane][:].indirect(offsets[:, e0 // LIST_ROWS : e1 // LIST_ROWS])
+
+        def gather(plane, cuts=()):
             g, j = divmod(plane, PACK)
             direct = DIRECT[plane]
-            nc.vector.tensor_copy(out=woven[g, 0][:, :direct, j], in_=x_raw[plane][:].indirect(offsets[:, : direct // 16]))
-            nc.scalar.activation(out=picked[g][:, j, direct:], in_=x_raw[plane][:].indirect(offsets[:, direct // 16 :]), func=ACT.Copy)
+            nc.vector.tensor_copy(out=woven[g, 0][:, :direct, j], in_=window(plane, 0, direct))
+            edges = (direct,) + cuts + (S,)
+            for e0, e1 in zip(edges, edges[1:]):
+                nc.scalar.activation(out=picked[g][:, j, e0:e1], in_=window(plane, e0, e1), func=ACT.Copy)
 
-        def weave_x(g, e0, e1, j0, j1):
+        def weave_x(engine, g, e0, e1, j0, j1):
             half = e0 // HALF
-            interleave("vector", woven[g, half][:, e0 - half * HALF : e1 - half * HALF, j0:j1], picked[g][:, j0:j1, e0:e1])
+            interleave(engine, woven[g, half][:, e0 - half * HALF : e1 - half * HALF, j0:j1], picked[g][:, j0:j1, e0:e1])
 
         def quantize_x(g, half, tag):
             x_words[g, half] = keep.tile([P, HALF], U32, name="x_words_%d_%d" % (g, half), tag=tag, align_bytes=64)
             nc.vector.quantize_mx(
-                out=x_words[g, half][:].bitcast(FP8X4), scales=x_scales[g, half][:], in_=woven[g, half][:].rearrange("p c j -> p (c j)")
+                out=x_words[g, half][:].bitcast(FP8X4),
+                scales=x_scales[g, half][:],
+                in_=woven[g, half][:].rearrange("p c j -> p (c j)"),
             )
 
         w_words = {}
@@ -106,18 +122,16 @@ def tile_picked_deepset_relu_e_kernel(tc, xT, w1, w2_words, w2_scales, offs, out
             else:
                 nc.scalar.activation(out=dst, in_=src, func=ACT.Copy)
 
-        def quantize_w(g, t0, steps):
+        def quantize_w(g, t0, step):
             words = keep.tile([P, 2 * P], U32, name="w_words_%d_%d" % (g, t0), align_bytes=64)
             scales = keep.tile([P, 2 * P], U8, name="w_scales_%d_%d" % (g, t0), align_bytes=64)
-            t = 0
-            for step in steps:
+            for t in range(0, 2, step):
                 cols = slice(t * P, (t + step) * P)
                 nc.vector.quantize_mx(
                     out=words[:, cols].bitcast(FP8X4),
                     scales=scales[:, cols],
                     in_=w_bf[g, t0][:, t : t + step, :, :].rearrange("p t m j -> p (t m j)"),
                 )
-                t = t + step
             for t in range(2):
                 w_words[g, t0 + t] = words[:, t * P : (t + 1) * P]
                 w_scales[g, t0 + t] = scales[:, t * P : (t + 1) * P]
@@ -127,52 +141,53 @@ def tile_picked_deepset_relu_e_kernel(tc, xT, w1, w2_words, w2_scales, offs, out
             for t in range(PACK):
                 banks[t, half] = psum.tile([P, HALF], F32, name="bank_%d" % (2 * t + half))
 
-        def product(g, t, half):
-            nc.tensor.matmul_mx(
-                out=banks[t, half][:],
-                lhsT=w_words[g, t].bitcast(FP8X4),
-                lhsT_scale=w_scales[g, t],
-                rhs=x_words[g, half][:].bitcast(FP8X4),
-                rhs_scale=x_scales[g, half][:],
-                start=(g == 0),
-                stop=(g == PASSES - 1),
-            )
+        def products(g):
+            for half in range(2):
+                for t in range(PACK):
+                    nc.tensor.matmul_mx(
+                        out=banks[t, half][:],
+                        lhsT=w_words[g, t].bitcast(FP8X4),
+                        lhsT_scale=w_scales[g, t],
+                        rhs=x_words[g, half][:].bitcast(FP8X4),
+                        rhs_scale=x_scales[g, half][:],
+                        start=(g == 0),
+                        stop=(g == PASSES - 1),
+                    )
 
         for plane in range(PACK):
             gather(plane)
-        weave_x(0, DIRECT[0], HALF, 0, PACK)
-        weave_x(0, HALF, S, 0, PACK)
+        weave_x("vector", 0, DIRECT[0], HALF, 0, PACK)
+        weave_x("vector", 0, HALF, S - QUARTER, 0, PACK)
+        weave_x("scalar", 0, S - QUARTER, S, 0, PACK)
         gather(4)
         quantize_x(0, 0, "x_words_0_0")
         quantize_x(0, 1, "x_words_0_1")
-        gather(5)
-        weave_x(1, DIRECT[4], HALF, 0, 2)
-        weave_x(1, HALF, S, 0, 2)
+        gather(5, (HALF,))
+        weave_x("vector", 1, DIRECT[4], HALF, 0, 2)
+        weave_x("vector", 1, HALF, S, 0, 2)
         gather(6)
         round_w("vector", 0, 0, 0, PACK, w_first)
         round_w("scalar", 0, 2, 0, PACK, w_first)
-        quantize_w(0, 0, (2,))
-        quantize_w(0, 2, (2,))
-        for half in range(2):
-            for t in range(PACK):
-                product(0, t, half)
+        quantize_w(0, 0, 2)
+        quantize_w(0, 2, 2)
+        products(0)
         gather(7)
         round_w("scalar", 1, 0, 0, 2, w_pair[0])
         round_w("scalar", 1, 2, 0, 2, w_pair[0])
-        weave_x(1, HALF, S, 2, PACK)
-        quantize_x(1, 0, "x_words_1_0")
+        weave_x("vector", 1, HALF, S, 2, PACK)
         round_w("vector", 1, 0, 2, PACK, w_pair[1])
         round_w("scalar", 1, 2, 2, PACK, w_pair[1])
-        quantize_w(1, 0, (1, 1))
-        quantize_w(1, 2, (2,))
+        quantize_x(1, 0, "w_pair_0")
+        quantize_w(1, 0, 1)
+        quantize_w(1, 2, 2)
         quantize_x(1, 1, "w_pair_1")
 
         h = [keep.tile([P, S], F32, name="h_%d" % t) for t in range(PACK)]
-        part = keep.tile([P, PACK], F32, name="part")
+        first_sum = keep.tile([P, PACK], F32, name="first_sum")
         total = [keep.tile([P, 1], F32, name="total_%d" % t) for t in range(PACK)]
-        planes = keep.tile([P, PACK, S], BF16, name="z_planes")
+        z_planes = keep.tile([P, PACK, S], BF16, name="z_planes")
 
-        def empty(engine, t, half, sums, start):
+        def empty(engine, t, half, sums, start=None):
             dst = h[t][:, half * HALF : (half + 1) * HALF]
             if engine == "scalar":
                 nc.scalar.activation(out=dst, in_=banks[t, half][:], func=ACT.Relu, accum_out=sums)
@@ -184,55 +199,50 @@ def tile_picked_deepset_relu_e_kernel(tc, xT, w1, w2_words, w2_scales, offs, out
         def center(engine, t, c0, c1):
             if engine == "vector":
                 nc.vector.tensor_scalar(
-                    out=planes[:, t, c0:c1], in0=h[t][:, c0:c1], scalar1=-float(S), scalar2=total[t][:], op0=ALU.mult, op1=ALU.add
-                )
-            elif engine == "gpsimd":
-                nc.gpsimd.tensor_scalar(
-                    out=planes[:, t, c0:c1], in0=h[t][:, c0:c1], scalar1=-float(S), scalar2=total[t][:], op0=ALU.mult, op1=ALU.add
+                    out=z_planes[:, t, c0:c1], in0=h[t][:, c0:c1], scalar1=-float(S), scalar2=total[t][:], op0=ALU.mult, op1=ALU.add
                 )
             else:
-                nc.scalar.activation(out=planes[:, t, c0:c1], in_=h[t][:, c0:c1], func=ACT.Identity, bias=total[t][:], scale=-float(S))
+                nc.scalar.activation(out=z_planes[:, t, c0:c1], in_=h[t][:, c0:c1], func=ACT.Identity, bias=total[t][:], scale=-float(S))
 
-        for t in range(PACK):
-            product(1, t, 0)
-        for t in (0, 2, 1, 3):
-            product(1, t, 1)
-        other = keep.tile([P, 1], F32, name="other")
-        empty("scalar", 0, 0, part[:, 0:1], None)
-        empty("vector", 1, 0, part[:, 1:2], None)
-        empty("scalar", 2, 0, part[:, 2:3], None)
-        empty("scalar", 3, 0, part[:, 3:4], None)
-        empty("vector", 0, 1, total[0][:], part[:, 0:1])
-        empty("scalar", 2, 1, other[:], None)
-        empty("vector", 1, 1, total[1][:], part[:, 1:2])
-        empty("vector", 3, 1, total[3][:], part[:, 3:4])
-        center("gpsimd", 0, 0, 704)
-        center("scalar", 0, 704, S)
-        nc.scalar.activation(out=total[2][:], in_=part[:, 2:3], func=ACT.Identity, bias=other[:])
-        center("scalar", 1, HALF, S)
-        center("scalar", 2, HALF, S)
-        center("vector", 1, 0, HALF)
-        center("vector", 3, HALF, S)
-        center("vector", 2, 0, HALF)
-        center("vector", 3, 0, 256)
-        center("vector", 3, 256, HALF)
+        products(1)
+        second_sum = keep.tile([P, 2], F32, name="second_sum")
+        empty("scalar", 0, 0, first_sum[:, 0:1])
+        empty("vector", 1, 0, first_sum[:, 1:2])
+        empty("scalar", 2, 0, first_sum[:, 2:3])
+        empty("scalar", 3, 0, first_sum[:, 3:4])
+        for t in (0, 1):
+            empty("vector", t, 1, total[t][:], first_sum[:, t : t + 1])
+        for t in (2, 3):
+            empty("scalar", t, 1, second_sum[:, t - 2 : t - 1])
+        for t in (0, 1):
+            center("vector", t, 0, S)
+            nc.vector.tensor_tensor(out=total[t + 2][:], in0=first_sum[:, t + 2 : t + 3], in1=second_sum[:, t : t + 1], op=ALU.add)
+        center("scalar", 2, S - QUARTER, S)
+        center("vector", 2, 0, S - QUARTER)
+        center("scalar", 3, S - QUARTER, S)
+        center("scalar", 3, HALF, S - QUARTER)
+        center("vector", 3, 0, QUARTER)
+        center("vector", 3, QUARTER, HALF)
 
-        def weave(engine, c0, width, planes):
+        vector_runs = ((0, QUARTER), (QUARTER, QUARTER))
+        scalar_runs = ((S - QUARTER, QUARTER), (HALF, EIGHTH), (HALF + EIGHTH, EIGHTH))
+
+        def weave_z(engine, c0, width):
             grouped = keep.tile([P, width, PACK], BF16, name="z_bf_%d" % c0, align_bytes=64)
-            interleave(engine, grouped[:], planes)
+            interleave(engine, grouped[:], z_planes[:, :, c0 : c0 + width])
             return grouped
 
-        def finish(engine, c0, width, grouped):
+        def second_product(c0, width, grouped):
             z_words = keep.tile([P, width], U32, name="z_words_%d" % c0, align_bytes=64)
             z_scales = keep.tile([P, width], U8, name="z_scales_%d" % c0, align_bytes=64)
             nc.vector.quantize_mx(
                 out=z_words[:].bitcast(FP8X4), scales=z_scales[:], in_=grouped[:].rearrange("p c j -> p (c j)")
             )
-            acc = psum.tile([P, width], F32, name="bank_%d" % (c0 // P))
+            acc = psum.tile([P, width], F32, name="bank_%d" % (c0 // EIGHTH))
             nc.tensor.matmul_mx(
                 out=acc[:],
                 lhsT=w2_codes[:].bitcast(FP4X4),
-                lhsT_scale=w2_plane[:],
+                lhsT_scale=w2_scale[:],
                 rhs=z_words[:].bitcast(FP8X4),
                 rhs_scale=z_scales[:],
                 start=True,
@@ -240,25 +250,24 @@ def tile_picked_deepset_relu_e_kernel(tc, xT, w1, w2_words, w2_scales, offs, out
             )
             return acc
 
-        def store(engine, queue, c0, width, acc):
+        def store(engine, c0, width, acc):
             result = keep.tile([P, width], F32, name="result_%d" % c0)
             if engine == "vector":
                 nc.vector.tensor_scalar(out=result[:], in0=acc[:], scalar1=-1.0 / S, scalar2=None, op0=ALU.mult)
             else:
                 nc.scalar.activation(out=result[:], in_=acc[:], func=ACT.Copy, scale=-1.0 / S)
-            queue.dma_start(out=out[:, c0 : c0 + width], in_=result[:])
+            nc.sync.dma_start(out=out[:, c0 : c0 + width], in_=result[:])
 
         z_bf = {}
+        for c0, width in scalar_runs:
+            z_bf[c0] = weave_z("scalar", c0, width)
+        for c0, width in vector_runs:
+            z_bf[c0] = weave_z("vector", c0, width)
+        runs = vector_runs + scalar_runs
         acc = {}
-        z_bf[768] = weave("scalar", 768, 256, planes[:, :, 768:1024])
-        z_bf[512] = weave("scalar", 512, 128, planes[:, :, 512:640])
-        z_bf[640] = weave("scalar", 640, 128, planes[:, :, 640:768])
-        z_bf[0] = weave("vector", 0, 256, planes[:, :, 0:256])
-        z_bf[256] = weave("vector", 256, 256, planes[:, :, 256:512])
-        for c0, width in ((0, 256), (256, 256), (768, 256), (512, 128), (640, 128)):
-            acc[c0] = finish("vector", c0, width, z_bf[c0])
-        store("scalar", nc.sync, 0, 256, acc[0])
-        store("scalar", nc.sync, 256, 256, acc[256])
-        store("scalar", nc.sync, 768, 256, acc[768])
-        store("scalar", nc.sync, 512, 128, acc[512])
-        store("vector", nc.sync, 640, 128, acc[640])
+        for c0, width in runs:
+            acc[c0] = second_product(c0, width, z_bf[c0])
+        for c0, width in runs[:-1]:
+            store("scalar", c0, width, acc[c0])
+        c0, width = runs[-1]
+        store("vector", c0, width, acc[c0])

@@ -28,7 +28,7 @@ QUARTER = S // 4
 EIGHTH = S // 8
 LINE = 4
 
-DIRECT = (3 * EIGHTH,) * PACK + (QUARTER, QUARTER, HALF, HALF)
+DIRECT = (3 * EIGHTH,) * PACK + (QUARTER, QUARTER, HALF + EIGHTH, HALF + EIGHTH)
 
 
 def tile_picked_deepset_relu_e_kernel(tc, xT, w1, w2_words, w2_scales, offs, out):
@@ -75,13 +75,12 @@ def tile_picked_deepset_relu_e_kernel(tc, xT, w1, w2_words, w2_scales, offs, out
             else:
                 nc.scalar.copy(out=dst, in_=src)
 
-        woven = {}
         x_words = {}
         x_scales = {}
         for g in range(PASSES):
             for half in range(2):
-                woven[g, half] = keep.tile([P, HALF, PACK], BF16, name="x_bf_%d_%d" % (g, half), align_bytes=64)
                 x_scales[g, half] = keep.tile([P, HALF], U8, name="x_scales_%d_%d" % (g, half), align_bytes=64)
+        woven = [keep.tile([P, S, PACK], BF16, name="x_bf_%d" % g, align_bytes=64) for g in range(PASSES)]
         picked = [keep.tile([P, PACK, S], BF16, name="picked_%d" % g, align_bytes=64) for g in range(PASSES)]
 
         def window(plane, e0, e1):
@@ -90,21 +89,20 @@ def tile_picked_deepset_relu_e_kernel(tc, xT, w1, w2_words, w2_scales, offs, out
         def gather(plane, cuts=()):
             g, j = divmod(plane, PACK)
             direct = DIRECT[plane]
-            nc.vector.tensor_copy(out=woven[g, 0][:, :direct, j], in_=window(plane, 0, direct))
+            nc.vector.tensor_copy(out=woven[g][:, :direct, j], in_=window(plane, 0, direct))
             edges = (direct,) + cuts + (S,)
             for e0, e1 in zip(edges, edges[1:]):
                 nc.scalar.activation(out=picked[g][:, j, e0:e1], in_=window(plane, e0, e1), func=ACT.Copy)
 
         def weave_x(engine, g, e0, e1, j0, j1):
-            half = e0 // HALF
-            interleave(engine, woven[g, half][:, e0 - half * HALF : e1 - half * HALF, j0:j1], picked[g][:, j0:j1, e0:e1])
+            interleave(engine, woven[g][:, e0:e1, j0:j1], picked[g][:, j0:j1, e0:e1])
 
         def quantize_x(g, half, tag):
             x_words[g, half] = keep.tile([P, HALF], U32, name="x_words_%d_%d" % (g, half), tag=tag, align_bytes=64)
             nc.vector.quantize_mx(
                 out=x_words[g, half][:].bitcast(FP8X4),
                 scales=x_scales[g, half][:],
-                in_=woven[g, half][:].rearrange("p c j -> p (c j)"),
+                in_=woven[g][:, half * HALF : (half + 1) * HALF, :].rearrange("p c j -> p (c j)"),
             )
 
         w_words = {}
@@ -156,15 +154,14 @@ def tile_picked_deepset_relu_e_kernel(tc, xT, w1, w2_words, w2_scales, offs, out
 
         for plane in range(PACK):
             gather(plane)
-        weave_x("vector", 0, DIRECT[0], HALF, 0, PACK)
-        weave_x("vector", 0, HALF, S - QUARTER, 0, PACK)
+        weave_x("vector", 0, DIRECT[0], S - QUARTER, 0, PACK)
         weave_x("scalar", 0, S - QUARTER, S, 0, PACK)
         gather(4)
         quantize_x(0, 0, "x_words_0_0")
         quantize_x(0, 1, "x_words_0_1")
-        gather(5, (HALF,))
-        weave_x("vector", 1, DIRECT[4], HALF, 0, 2)
-        weave_x("vector", 1, HALF, S, 0, 2)
+        gather(5, (DIRECT[6],))
+        weave_x("vector", 1, DIRECT[4], DIRECT[6], 0, 2)
+        weave_x("vector", 1, DIRECT[6], S, 0, 2)
         gather(6)
         round_w("vector", 0, 0, 0, PACK, w_first)
         round_w("scalar", 0, 2, 0, PACK, w_first)
@@ -174,7 +171,7 @@ def tile_picked_deepset_relu_e_kernel(tc, xT, w1, w2_words, w2_scales, offs, out
         gather(7)
         round_w("scalar", 1, 0, 0, 2, w_pair[0])
         round_w("scalar", 1, 2, 0, 2, w_pair[0])
-        weave_x("vector", 1, HALF, S, 2, PACK)
+        weave_x("vector", 1, DIRECT[7], S, 2, PACK)
         round_w("vector", 1, 0, 2, PACK, w_pair[1])
         round_w("scalar", 1, 2, 2, PACK, w_pair[1])
         quantize_x(1, 0, "w_pair_0")
@@ -214,9 +211,10 @@ def tile_picked_deepset_relu_e_kernel(tc, xT, w1, w2_words, w2_scales, offs, out
             empty("vector", t, 1, total[t][:], first_sum[:, t : t + 1])
         for t in (2, 3):
             empty("scalar", t, 1, second_sum[:, t - 2 : t - 1])
+        for t in (2, 3):
+            nc.scalar.activation(out=total[t][:], in_=first_sum[:, t : t + 1], func=ACT.Identity, bias=second_sum[:, t - 2 : t - 1])
         for t in (0, 1):
             center("vector", t, 0, S)
-            nc.vector.tensor_tensor(out=total[t + 2][:], in0=first_sum[:, t + 2 : t + 3], in1=second_sum[:, t : t + 1], op=ALU.add)
         center("scalar", 2, S - QUARTER, S)
         center("vector", 2, 0, S - QUARTER)
         center("scalar", 3, S - QUARTER, S)

@@ -28,7 +28,7 @@ QUARTER = S // 4
 EIGHTH = S // 8
 LINE = 4
 
-DIRECT = (3 * EIGHTH,) * PACK + (QUARTER, QUARTER, HALF + EIGHTH, HALF + EIGHTH)
+DIRECT = (3 * EIGHTH,) * PACK + (QUARTER, QUARTER, 3 * EIGHTH, HALF + EIGHTH)
 
 
 def tile_picked_deepset_relu_e_kernel(tc, xT, w1, w2_words, w2_scales, offs, out):
@@ -154,15 +154,15 @@ def tile_picked_deepset_relu_e_kernel(tc, xT, w1, w2_words, w2_scales, offs, out
 
         for plane in range(PACK):
             gather(plane)
-        weave_x("vector", 0, DIRECT[0], S - QUARTER, 0, PACK)
-        weave_x("scalar", 0, S - QUARTER, S, 0, PACK)
+        weave_x("vector", 0, DIRECT[0], S, 0, PACK)
         gather(4)
         quantize_x(0, 0, "x_words_0_0")
         quantize_x(0, 1, "x_words_0_1")
         gather(5, (DIRECT[6],))
-        weave_x("vector", 1, DIRECT[4], DIRECT[6], 0, 2)
-        weave_x("vector", 1, DIRECT[6], S, 0, 2)
-        gather(6)
+        weave_x("vector", 1, DIRECT[5], DIRECT[6], 0, 2)
+        gather(6, (DIRECT[7],))
+        weave_x("vector", 1, DIRECT[6], DIRECT[7], 0, PACK - 1)
+        weave_x("vector", 1, DIRECT[7], S, 0, PACK - 1)
         round_w("vector", 0, 0, 0, PACK, w_first)
         round_w("scalar", 0, 2, 0, PACK, w_first)
         quantize_w(0, 0, 2)
@@ -171,7 +171,7 @@ def tile_picked_deepset_relu_e_kernel(tc, xT, w1, w2_words, w2_scales, offs, out
         gather(7)
         round_w("scalar", 1, 0, 0, 2, w_pair[0])
         round_w("scalar", 1, 2, 0, 2, w_pair[0])
-        weave_x("vector", 1, DIRECT[7], S, 2, PACK)
+        weave_x("vector", 1, DIRECT[7], S, PACK - 1, PACK)
         round_w("vector", 1, 0, 2, PACK, w_pair[1])
         round_w("scalar", 1, 2, 2, PACK, w_pair[1])
         quantize_x(1, 0, "w_pair_0")

@@ -28,6 +28,8 @@ QUARTER = S // 4
 EIGHTH = S // 8
 LINE = 4
 
+W_VECTOR = 72
+
 DIRECT = (3 * EIGHTH,) * PACK + (QUARTER, QUARTER, 3 * EIGHTH, HALF + EIGHTH)
 
 
@@ -108,9 +110,10 @@ def tile_picked_deepset_relu_e_kernel(tc, xT, w1, w2_words, w2_scales, offs, out
         w_words = {}
         w_scales = {}
         w_bf = {}
-        for g in range(PASSES):
-            for t0 in (0, 2):
-                w_bf[g, t0] = keep.tile([P, 2, P, PACK], BF16, name="w_bf_%d_%d" % (g, t0), align_bytes=64)
+        w_bf_first = keep.tile([P, PACK, P, PACK], BF16, name="w_bf_first", align_bytes=64)
+        for t0 in (0, 2):
+            pair = keep.tile([P, 2, P, PACK], BF16, name="w_bf_last_%d" % t0, align_bytes=64)
+            w_bf[1, t0] = pair[:]
 
         def round_w(engine, g, t0, j0, j1, raw):
             dst = w_bf[g, t0][:, :, :, j0:j1].rearrange("p t m j -> p m j t")
@@ -120,17 +123,18 @@ def tile_picked_deepset_relu_e_kernel(tc, xT, w1, w2_words, w2_scales, offs, out
             else:
                 nc.scalar.activation(out=dst, in_=src, func=ACT.Copy)
 
-        def quantize_w(g, t0, step):
-            words = keep.tile([P, 2 * P], U32, name="w_words_%d_%d" % (g, t0), align_bytes=64)
-            scales = keep.tile([P, 2 * P], U8, name="w_scales_%d_%d" % (g, t0), align_bytes=64)
-            for t in range(0, 2, step):
+        def quantize_w(g, t0, rounded, step):
+            tiles = rounded.shape[1]
+            words = keep.tile([P, tiles * P], U32, name="w_words_%d_%d" % (g, t0), align_bytes=64)
+            scales = keep.tile([P, tiles * P], U8, name="w_scales_%d_%d" % (g, t0), align_bytes=64)
+            for t in range(0, tiles, step):
                 cols = slice(t * P, (t + step) * P)
                 nc.vector.quantize_mx(
                     out=words[:, cols].bitcast(FP8X4),
                     scales=scales[:, cols],
-                    in_=w_bf[g, t0][:, t : t + step, :, :].rearrange("p t m j -> p (t m j)"),
+                    in_=rounded[:, t : t + step, :, :].rearrange("p t m j -> p (t m j)"),
                 )
-            for t in range(2):
+            for t in range(tiles):
                 w_words[g, t0 + t] = words[:, t * P : (t + 1) * P]
                 w_scales[g, t0 + t] = scales[:, t * P : (t + 1) * P]
 
@@ -163,10 +167,11 @@ def tile_picked_deepset_relu_e_kernel(tc, xT, w1, w2_words, w2_scales, offs, out
         gather(6, (DIRECT[7],))
         weave_x("vector", 1, DIRECT[6], DIRECT[7], 0, PACK - 1)
         weave_x("vector", 1, DIRECT[7], S, 0, PACK - 1)
-        round_w("vector", 0, 0, 0, PACK, w_first)
-        round_w("scalar", 0, 2, 0, PACK, w_first)
-        quantize_w(0, 0, 2)
-        quantize_w(0, 2, 2)
+        dst = w_bf_first[:].rearrange("p t m j -> p m j t")
+        src = w_first[:].rearrange("p (j m t) -> p m j t", m=P, t=PACK)
+        nc.vector.tensor_copy(out=dst[:, :W_VECTOR, :, :], in_=src[:, :W_VECTOR, :, :])
+        nc.scalar.activation(out=dst[:, W_VECTOR:, :, :], in_=src[:, W_VECTOR:, :, :], func=ACT.Copy)
+        quantize_w(0, 0, w_bf_first[:], PACK)
         products(0)
         gather(7)
         round_w("scalar", 1, 0, 0, 2, w_pair[0])
@@ -175,8 +180,8 @@ def tile_picked_deepset_relu_e_kernel(tc, xT, w1, w2_words, w2_scales, offs, out
         round_w("vector", 1, 0, 2, PACK, w_pair[1])
         round_w("scalar", 1, 2, 2, PACK, w_pair[1])
         quantize_x(1, 0, "w_pair_0")
-        quantize_w(1, 0, 1)
-        quantize_w(1, 2, 2)
+        quantize_w(1, 0, w_bf[1, 0], 1)
+        quantize_w(1, 2, w_bf[1, 2], 2)
         quantize_x(1, 1, "w_pair_1")
 
         h = [keep.tile([P, S], F32, name="h_%d" % t) for t in range(PACK)]

@@ -48,10 +48,10 @@ def tile_picked_deepset_relu_e_kernel(tc, xT, w1, w2_words, w2_scales, offs, out
         for plane in range(PLANES):
             g, j = divmod(plane, PACK)
             if plane == PLANES - 1:
-                w_first = keep.tile([P, PACK * H], F32, name="w_first", align_bytes=64)
+                w_first = keep.tile([P, PACK * H], F32, name="w_first", align_bytes=256)
                 nc.sync.dma_start(out=w_first[:], in_=w1[:K_PASS, :].rearrange("(p j) c -> p (j c)", j=PACK))
             rows = xT[g * K_PASS : (g + 1) * K_PASS, :].rearrange("(p j) c -> p j c", j=PACK)
-            raw = keep.tile([P, T], F32, name="x_raw_%d" % plane, align_bytes=64)
+            raw = keep.tile([P, T], F32, name="x_raw_%d" % plane, align_bytes=256)
             nc.sync.dma_start(out=raw[:], in_=rows[:, j, :])
             x_raw.append(raw)
             if plane == 0:
@@ -59,7 +59,7 @@ def tile_picked_deepset_relu_e_kernel(tc, xT, w1, w2_words, w2_scales, offs, out
         w_rows = w1[K_PASS:, :].rearrange("(p j) c -> p (j c)", j=PACK)
         w_pair = []
         for u in range(PACK // 2):
-            raw = keep.tile([P, 2 * H], F32, name="w_pair_%d" % u, tag="w_pair_%d" % u, align_bytes=64)
+            raw = keep.tile([P, 2 * H], F32, name="w_pair_%d" % u, tag="w_pair_%d" % u, align_bytes=256)
             nc.sync.dma_start(out=raw[:], in_=w_rows[:, 2 * u * H : 2 * (u + 1) * H])
             w_pair.append(raw)
         nc.sync.dma_start(out=w2_codes[:].bitcast(I32), in_=w2_words[0].bitcast(I32))
@@ -100,7 +100,7 @@ def tile_picked_deepset_relu_e_kernel(tc, xT, w1, w2_words, w2_scales, offs, out
             interleave(engine, woven[g][:, e0:e1, j0:j1], picked[g][:, j0:j1, e0:e1])
 
         def quantize_x(g, half, tag):
-            x_words[g, half] = keep.tile([P, HALF], U32, name="x_words_%d_%d" % (g, half), tag=tag, align_bytes=64)
+            x_words[g, half] = keep.tile([P, HALF], U32, name="x_words_%d_%d" % (g, half), tag=tag, align_bytes=256)
             nc.vector.quantize_mx(
                 out=x_words[g, half][:].bitcast(FP8X4),
                 scales=x_scales[g, half][:],
@@ -254,7 +254,7 @@ def tile_picked_deepset_relu_e_kernel(tc, xT, w1, w2_words, w2_scales, offs, out
             return acc
 
         def store(engine, c0, width, acc):
-            result = keep.tile([P, width], F32, name="result_%d" % c0)
+            result = keep.tile([P, width], F32, name="result_%d" % c0, align_bytes=256)
             if engine == "vector":
                 nc.vector.tensor_scalar(out=result[:], in0=acc[:], scalar1=-1.0 / S, scalar2=None, op0=ALU.mult)
             else:

@@ -28,9 +28,18 @@ QUARTER = S // 4
 EIGHTH = S // 8
 LINE = 4
 
-W_VECTOR = 72
+W_VECTOR = 80
 
-DIRECT = (3 * EIGHTH,) * PACK + (QUARTER, QUARTER, 3 * EIGHTH, HALF + EIGHTH)
+FIRST_PAIR_VECTOR = 88
+SECOND_PAIR_VECTOR = 48
+
+LAST = S - QUARTER
+THIRD_VECTOR = 64
+
+STRETCHES = (
+    (("vector", 0, HALF), ("scalar", HALF, S)),
+    (("vector", 0, HALF), ("scalar", HALF, S - QUARTER), ("scalar", S - QUARTER, S)),
+)
 
 
 def tile_picked_deepset_relu_e_kernel(tc, xT, w1, w2_words, w2_scales, offs, out):
@@ -45,23 +54,24 @@ def tile_picked_deepset_relu_e_kernel(tc, xT, w1, w2_words, w2_scales, offs, out
         nc.vector.memset(w2_scale[:].bitcast(I32), 0)
 
         x_raw = []
+        w_raw = []
+
+        def load_w(g):
+            raw = keep.tile([P, PACK * H], F32, name="w_raw_%d" % g, align_bytes=256)
+            nc.sync.dma_start(out=raw[:], in_=w1[g * K_PASS : (g + 1) * K_PASS, :].rearrange("(p j) c -> p (j c)", j=PACK))
+            w_raw.append(raw)
+
         for plane in range(PLANES):
             g, j = divmod(plane, PACK)
             if plane == PLANES - 1:
-                w_first = keep.tile([P, PACK * H], F32, name="w_first", align_bytes=256)
-                nc.sync.dma_start(out=w_first[:], in_=w1[:K_PASS, :].rearrange("(p j) c -> p (j c)", j=PACK))
+                load_w(0)
             rows = xT[g * K_PASS : (g + 1) * K_PASS, :].rearrange("(p j) c -> p j c", j=PACK)
             raw = keep.tile([P, T], F32, name="x_raw_%d" % plane, align_bytes=256)
             nc.sync.dma_start(out=raw[:], in_=rows[:, j, :])
             x_raw.append(raw)
             if plane == 0:
                 nc.sync.dma_start(offsets[:], offs)
-        w_rows = w1[K_PASS:, :].rearrange("(p j) c -> p (j c)", j=PACK)
-        w_pair = []
-        for u in range(PACK // 2):
-            raw = keep.tile([P, 2 * H], F32, name="w_pair_%d" % u, tag="w_pair_%d" % u, align_bytes=256)
-            nc.sync.dma_start(out=raw[:], in_=w_rows[:, 2 * u * H : 2 * (u + 1) * H])
-            w_pair.append(raw)
+        load_w(1)
         nc.sync.dma_start(out=w2_codes[:].bitcast(I32), in_=w2_words[0].bitcast(I32))
         for q in range(P // 32):
             nc.sync.dma_start(
@@ -69,59 +79,43 @@ def tile_picked_deepset_relu_e_kernel(tc, xT, w1, w2_words, w2_scales, offs, out
                 in_=w2_scales[0, SCALE_ROWS * q : SCALE_ROWS * (q + 1), :].bitcast(I32),
             )
 
-        def interleave(engine, dst, src):
-            dst = dst.rearrange("p (c i) j -> p c j i", i=LINE)
-            src = src.rearrange("p j (c i) -> p c j i", i=LINE)
-            if engine == "vector":
-                nc.vector.tensor_copy(out=dst, in_=src)
-            else:
-                nc.scalar.copy(out=dst, in_=src)
-
+        woven = {}
+        for g in range(PASSES):
+            for engine, e0, e1 in STRETCHES[g]:
+                woven[g, e0] = keep.tile([P, e1 - e0, PACK], BF16, name="x_bf_%d_%d" % (g, e0), align_bytes=64)
         x_words = {}
         x_scales = {}
-        for g in range(PASSES):
-            for half in range(2):
-                x_scales[g, half] = keep.tile([P, HALF], U8, name="x_scales_%d_%d" % (g, half), align_bytes=64)
-        woven = [keep.tile([P, S, PACK], BF16, name="x_bf_%d" % g, align_bytes=64) for g in range(PASSES)]
-        picked = [keep.tile([P, PACK, S], BF16, name="picked_%d" % g, align_bytes=64) for g in range(PASSES)]
 
-        def window(plane, e0, e1):
-            return x_raw[plane][:].indirect(offsets[:, e0 // LIST_ROWS : e1 // LIST_ROWS])
-
-        def gather(plane, cuts=()):
+        def gather(plane):
             g, j = divmod(plane, PACK)
-            direct = DIRECT[plane]
-            nc.vector.tensor_copy(out=woven[g][:, :direct, j], in_=window(plane, 0, direct))
-            edges = (direct,) + cuts + (S,)
-            for e0, e1 in zip(edges, edges[1:]):
-                nc.scalar.activation(out=picked[g][:, j, e0:e1], in_=window(plane, e0, e1), func=ACT.Copy)
+            for engine, e0, e1 in STRETCHES[g]:
+                window = x_raw[plane][:].indirect(offsets[:, e0 // LIST_ROWS : e1 // LIST_ROWS])
+                if engine == "vector":
+                    nc.vector.tensor_copy(out=woven[g, e0][:, :, j], in_=window)
+                else:
+                    nc.scalar.activation(out=woven[g, e0][:, :, j], in_=window, func=ACT.Copy)
 
-        def weave_x(engine, g, e0, e1, j0, j1):
-            interleave(engine, woven[g][:, e0:e1, j0:j1], picked[g][:, j0:j1, e0:e1])
-
-        def quantize_x(g, half, tag):
-            x_words[g, half] = keep.tile([P, HALF], U32, name="x_words_%d_%d" % (g, half), tag=tag, align_bytes=256)
+        def quantize_x(g, e0, e1, tag=None):
+            name = "x_words_%d_%d" % (g, e0)
+            x_words[g, e0] = keep.tile([P, e1 - e0], U32, name=name, tag=tag or name, align_bytes=64)
+            x_scales[g, e0] = keep.tile([P, e1 - e0], U8, name="x_scales_%d_%d" % (g, e0), align_bytes=64)
             nc.vector.quantize_mx(
-                out=x_words[g, half][:].bitcast(FP8X4),
-                scales=x_scales[g, half][:],
-                in_=woven[g][:, half * HALF : (half + 1) * HALF, :].rearrange("p c j -> p (c j)"),
+                out=x_words[g, e0][:].bitcast(FP8X4),
+                scales=x_scales[g, e0][:],
+                in_=woven[g, e0][:].rearrange("p c j -> p (c j)"),
             )
 
         w_words = {}
         w_scales = {}
-        w_bf = {}
-        w_bf_first = keep.tile([P, PACK, P, PACK], BF16, name="w_bf_first", align_bytes=64)
-        for t0 in (0, 2):
-            pair = keep.tile([P, 2, P, PACK], BF16, name="w_bf_last_%d" % t0, align_bytes=64)
-            w_bf[1, t0] = pair[:]
 
-        def round_w(engine, g, t0, j0, j1, raw):
-            dst = w_bf[g, t0][:, :, :, j0:j1].rearrange("p t m j -> p m j t")
-            src = raw[:].rearrange("p (j m t) -> p m j t", m=P, t=PACK)[:, :, :, t0 : t0 + 2]
-            if engine == "vector":
-                nc.vector.tensor_copy(out=dst, in_=src)
-            else:
-                nc.scalar.activation(out=dst, in_=src, func=ACT.Copy)
+        def round_w(g, t0, tiles, vector_columns):
+            rounded = keep.tile([P, tiles, P, PACK], BF16, name="w_bf_%d_%d" % (g, t0), tag="w_bf_%d_%d" % (g, t0), align_bytes=64)
+            dst = rounded[:].rearrange("p t m j -> p m j t")
+            src = w_raw[g][:].rearrange("p (j m t) -> p m j t", m=P, t=PACK)[:, :, :, t0 : t0 + tiles]
+            if vector_columns > 0:
+                nc.vector.tensor_copy(out=dst[:, :vector_columns, :, :], in_=src[:, :vector_columns, :, :])
+            nc.scalar.activation(out=dst[:, vector_columns:, :, :], in_=src[:, vector_columns:, :, :], func=ACT.Copy)
+            return rounded
 
         def quantize_w(g, t0, rounded, step):
             tiles = rounded.shape[1]
@@ -139,64 +133,57 @@ def tile_picked_deepset_relu_e_kernel(tc, xT, w1, w2_words, w2_scales, offs, out
                 w_scales[g, t0 + t] = scales[:, t * P : (t + 1) * P]
 
         banks = {}
-        for half in range(2):
-            for t in range(PACK):
+        for t in range(PACK):
+            for half in range(2):
                 banks[t, half] = psum.tile([P, HALF], F32, name="bank_%d" % (2 * t + half))
 
-        def products(g):
-            for half in range(2):
-                for t in range(PACK):
-                    nc.tensor.matmul_mx(
-                        out=banks[t, half][:],
-                        lhsT=w_words[g, t].bitcast(FP8X4),
-                        lhsT_scale=w_scales[g, t],
-                        rhs=x_words[g, half][:].bitcast(FP8X4),
-                        rhs_scale=x_scales[g, half][:],
-                        start=(g == 0),
-                        stop=(g == PASSES - 1),
-                    )
+        def product(g, t, half):
+            parts = [(e0, e1) for engine, e0, e1 in STRETCHES[g] if e0 // HALF == half]
+            for e0, e1 in parts:
+                nc.tensor.matmul_mx(
+                    out=banks[t, half][:, e0 - half * HALF : e1 - half * HALF],
+                    lhsT=w_words[g, t].bitcast(FP8X4),
+                    lhsT_scale=w_scales[g, t],
+                    rhs=x_words[g, e0][:].bitcast(FP8X4),
+                    rhs_scale=x_scales[g, e0][:],
+                    start=(g == 0),
+                    stop=(g == PASSES - 1 and e1 % HALF == 0),
+                )
 
         for plane in range(PACK):
             gather(plane)
-        weave_x("vector", 0, DIRECT[0], S, 0, PACK)
-        gather(4)
-        quantize_x(0, 0, "x_words_0_0")
-        quantize_x(0, 1, "x_words_0_1")
-        gather(5, (DIRECT[6],))
-        weave_x("vector", 1, DIRECT[5], DIRECT[6], 0, 2)
-        gather(6, (DIRECT[7],))
-        weave_x("vector", 1, DIRECT[6], DIRECT[7], 0, PACK - 1)
-        weave_x("vector", 1, DIRECT[7], S, 0, PACK - 1)
-        dst = w_bf_first[:].rearrange("p t m j -> p m j t")
-        src = w_first[:].rearrange("p (j m t) -> p m j t", m=P, t=PACK)
-        nc.vector.tensor_copy(out=dst[:, :W_VECTOR, :, :], in_=src[:, :W_VECTOR, :, :])
-        nc.scalar.activation(out=dst[:, W_VECTOR:, :, :], in_=src[:, W_VECTOR:, :, :], func=ACT.Copy)
-        quantize_w(0, 0, w_bf_first[:], PACK)
-        products(0)
-        gather(7)
-        round_w("scalar", 1, 0, 0, 2, w_pair[0])
-        round_w("scalar", 1, 2, 0, 2, w_pair[0])
-        weave_x("vector", 1, DIRECT[7], S, PACK - 1, PACK)
-        round_w("vector", 1, 0, 2, PACK, w_pair[1])
-        round_w("scalar", 1, 2, 2, PACK, w_pair[1])
-        quantize_x(1, 0, "w_pair_0")
-        quantize_w(1, 0, w_bf[1, 0], 1)
-        quantize_w(1, 2, w_bf[1, 2], 2)
-        quantize_x(1, 1, "w_pair_1")
+        for engine, e0, e1 in STRETCHES[0]:
+            quantize_x(0, e0, e1)
+        for plane in range(PACK, PLANES - 1):
+            gather(plane)
+        quantize_w(0, 0, round_w(0, 0, PACK, W_VECTOR)[:], 1)
+        for t in range(PACK):
+            for half in range(2):
+                product(0, t, half)
+        gather(PLANES - 1)
+        for engine, e0, e1 in (STRETCHES[1][1], STRETCHES[1][0]):
+            quantize_x(1, e0, e1)
+        first_pair = round_w(1, 0, 2, FIRST_PAIR_VECTOR)
+        second_pair = round_w(1, 2, 2, SECOND_PAIR_VECTOR)
+        quantize_w(1, 0, first_pair[:], 1)
+        quantize_x(1, S - QUARTER, S, "w_bf_1_0")
 
         h = [keep.tile([P, S], F32, name="h_%d" % t) for t in range(PACK)]
-        first_sum = keep.tile([P, PACK], F32, name="first_sum")
+        sums = [keep.tile([P, 2], F32, name="sums_%d" % t) for t in range(PACK)]
         total = [keep.tile([P, 1], F32, name="total_%d" % t) for t in range(PACK)]
         z_planes = keep.tile([P, PACK, S], BF16, name="z_planes")
 
-        def empty(engine, t, half, sums, start=None):
+        def empty(engine, t, half, into, start=None):
             dst = h[t][:, half * HALF : (half + 1) * HALF]
             if engine == "scalar":
-                nc.scalar.activation(out=dst, in_=banks[t, half][:], func=ACT.Relu, accum_out=sums)
+                nc.scalar.activation(out=dst, in_=banks[t, half][:], func=ACT.Relu, accum_out=into)
             else:
                 nc.vector.tensor_scalar(
-                    out=dst, in0=banks[t, half][:], scalar1=0.0, scalar2=start, op0=ALU.max, op1=ALU.add, accum_out=sums
+                    out=dst, in0=banks[t, half][:], scalar1=0.0, scalar2=start, op0=ALU.max, op1=ALU.add, accum_out=into
                 )
+
+        def add_sums(t):
+            nc.scalar.activation(out=total[t][:], in_=sums[t][:, 0:1], func=ACT.Identity, bias=sums[t][:, 1:2])
 
         def center(engine, t, c0, c1):
             if engine == "vector":
@@ -206,48 +193,60 @@ def tile_picked_deepset_relu_e_kernel(tc, xT, w1, w2_words, w2_scales, offs, out
             else:
                 nc.scalar.activation(out=z_planes[:, t, c0:c1], in_=h[t][:, c0:c1], func=ACT.Identity, bias=total[t][:], scale=-float(S))
 
-        products(1)
-        second_sum = keep.tile([P, 2], F32, name="second_sum")
-        empty("scalar", 0, 0, first_sum[:, 0:1])
-        empty("vector", 1, 0, first_sum[:, 1:2])
-        empty("scalar", 2, 0, first_sum[:, 2:3])
-        empty("scalar", 3, 0, first_sum[:, 3:4])
-        for t in (0, 1):
-            empty("vector", t, 1, total[t][:], first_sum[:, t : t + 1])
-        for t in (2, 3):
-            empty("scalar", t, 1, second_sum[:, t - 2 : t - 1])
-        for t in (2, 3):
-            nc.scalar.activation(out=total[t][:], in_=first_sum[:, t : t + 1], func=ACT.Identity, bias=second_sum[:, t - 2 : t - 1])
-        for t in (0, 1):
-            center("vector", t, 0, S)
-        center("scalar", 2, S - QUARTER, S)
-        center("vector", 2, 0, S - QUARTER)
-        center("scalar", 3, S - QUARTER, S)
-        center("scalar", 3, HALF, S - QUARTER)
+        quantize_w(1, 2, second_pair[:], 2)
+        for t, half in ((0, 0), (1, 0), (1, 1), (0, 1), (2, 0), (2, 1), (3, 0), (3, 1)):
+            product(1, t, half)
+        empty("scalar", 0, 0, sums[0][:, 0:1])
+        empty("vector", 1, 0, sums[1][:, 0:1])
+        empty("scalar", 1, 1, sums[1][:, 1:2])
+        empty("vector", 0, 1, total[0][:], sums[0][:, 0:1])
+        empty("scalar", 2, 0, sums[2][:, 0:1])
+        empty("vector", 2, 1, sums[2][:, 1:2])
+        add_sums(1)
+        empty("scalar", 3, 0, sums[3][:, 0:1])
+        add_sums(2)
+        empty("scalar", 3, 1, sums[3][:, 1:2])
+        center("vector", 0, 0, S)
+        center("scalar", 1, LAST, S)
+        add_sums(3)
+        center("vector", 1, 0, LAST)
+        center("scalar", 2, LAST, S)
+        center("vector", 2, 0, LAST)
+        center("scalar", 3, LAST, S)
+        center("scalar", 3, LAST - EIGHTH, LAST)
         center("vector", 3, 0, QUARTER)
-        center("vector", 3, QUARTER, HALF)
+        center("vector", 3, QUARTER, LAST - EIGHTH)
 
-        vector_runs = ((0, QUARTER), (QUARTER, QUARTER))
-        scalar_runs = ((S - QUARTER, QUARTER), (HALF, EIGHTH), (HALF + EIGHTH, EIGHTH))
+        def interleave(engine, dst, src):
+            dst = dst.rearrange("p (c i) j -> p c j i", i=LINE)
+            src = src.rearrange("p j (c i) -> p c j i", i=LINE)
+            if engine == "vector":
+                nc.vector.tensor_copy(out=dst, in_=src)
+            else:
+                nc.scalar.copy(out=dst, in_=src)
 
-        def weave_z(engine, c0, width):
-            grouped = keep.tile([P, width, PACK], BF16, name="z_bf_%d" % c0, align_bytes=64)
-            interleave(engine, grouped[:], z_planes[:, :, c0 : c0 + width])
-            return grouped
+        grouped = [keep.tile([P, QUARTER, PACK], BF16, name="z_bf_%d" % q, align_bytes=64) for q in range(4)]
 
-        def second_product(c0, width, grouped):
-            z_words = keep.tile([P, width], U32, name="z_words_%d" % c0, align_bytes=64)
-            z_scales = keep.tile([P, width], U8, name="z_scales_%d" % c0, align_bytes=64)
+        def weave_z(engine, q, c0, c1):
+            interleave(engine, grouped[q][:, c0:c1, :], z_planes[:, :, q * QUARTER + c0 : q * QUARTER + c1])
+
+        def quantize_z(q):
+            z_words = keep.tile([P, QUARTER], U32, name="z_words_%d" % q, align_bytes=64)
+            z_scales = keep.tile([P, QUARTER], U8, name="z_scales_%d" % q, align_bytes=64)
             nc.vector.quantize_mx(
-                out=z_words[:].bitcast(FP8X4), scales=z_scales[:], in_=grouped[:].rearrange("p c j -> p (c j)")
+                out=z_words[:].bitcast(FP8X4), scales=z_scales[:], in_=grouped[q][:].rearrange("p c j -> p (c j)")
             )
+            return z_words, z_scales
+
+        def second_product(c0, width, z_words, z_scales):
             acc = psum.tile([P, width], F32, name="bank_%d" % (c0 // EIGHTH))
+            cols = slice(c0 % QUARTER, c0 % QUARTER + width)
             nc.tensor.matmul_mx(
                 out=acc[:],
                 lhsT=w2_codes[:].bitcast(FP4X4),
                 lhsT_scale=w2_scale[:],
-                rhs=z_words[:].bitcast(FP8X4),
-                rhs_scale=z_scales[:],
+                rhs=z_words[:, cols].bitcast(FP8X4),
+                rhs_scale=z_scales[:, cols],
                 start=True,
                 stop=True,
             )
@@ -261,16 +260,14 @@ def tile_picked_deepset_relu_e_kernel(tc, xT, w1, w2_words, w2_scales, offs, out
                 nc.scalar.activation(out=result[:], in_=acc[:], func=ACT.Copy, scale=-1.0 / S)
             nc.sync.dma_start(out=out[:, c0 : c0 + width], in_=result[:])
 
-        z_bf = {}
-        for c0, width in scalar_runs:
-            z_bf[c0] = weave_z("scalar", c0, width)
-        for c0, width in vector_runs:
-            z_bf[c0] = weave_z("vector", c0, width)
-        runs = vector_runs + scalar_runs
-        acc = {}
-        for c0, width in runs:
-            acc[c0] = second_product(c0, width, z_bf[c0])
-        for c0, width in runs[:-1]:
-            store("scalar", c0, width, acc[c0])
-        c0, width = runs[-1]
-        store("vector", c0, width, acc[c0])
+        weave_z("scalar", 3, 0, QUARTER)
+        weave_z("scalar", 2, THIRD_VECTOR, QUARTER)
+        weave_z("vector", 0, 0, QUARTER)
+        weave_z("vector", 1, 0, QUARTER)
+        weave_z("vector", 2, 0, THIRD_VECTOR)
+        for q in (0, 3, 1):
+            acc = second_product(q * QUARTER, QUARTER, *quantize_z(q))
+            store("scalar", q * QUARTER, QUARTER, acc)
+        codes = quantize_z(2)
+        for engine, c0 in (("scalar", HALF), ("vector", HALF + EIGHTH)):
+            store(engine, c0, EIGHTH, second_product(c0, EIGHTH, *codes))

@@ -28,18 +28,14 @@ QUARTER = S // 4
 EIGHTH = S // 8
 LINE = 4
 
-W_VECTOR = 80
-
-FIRST_PAIR_VECTOR = 88
-SECOND_PAIR_VECTOR = 48
-
+FILL = 40
 LAST = S - QUARTER
-THIRD_VECTOR = 64
 
 STRETCHES = (
     (("vector", 0, HALF), ("scalar", HALF, S)),
-    (("vector", 0, HALF), ("scalar", HALF, S - QUARTER), ("scalar", S - QUARTER, S)),
+    (("vector", 0, 3 * EIGHTH), ("scalar", 3 * EIGHTH, HALF), ("scalar", HALF, LAST), ("scalar", LAST, S)),
 )
+OPERANDS = (((0, HALF), (HALF, S)), ((0, HALF), (HALF, LAST), (LAST, S)))
 
 
 def tile_picked_deepset_relu_e_kernel(tc, xT, w1, w2_words, w2_scales, offs, out):
@@ -96,25 +92,29 @@ def tile_picked_deepset_relu_e_kernel(tc, xT, w1, w2_words, w2_scales, offs, out
                     nc.scalar.activation(out=woven[g, e0][:, :, j], in_=window, func=ACT.Copy)
 
         def quantize_x(g, e0, e1, tag=None):
-            name = "x_words_%d_%d" % (g, e0)
-            x_words[g, e0] = keep.tile([P, e1 - e0], U32, name=name, tag=tag or name, align_bytes=64)
-            x_scales[g, e0] = keep.tile([P, e1 - e0], U8, name="x_scales_%d_%d" % (g, e0), align_bytes=64)
+            first, end = [run for run in OPERANDS[g] if run[0] <= e0 < run[1]][0]
+            if (g, first) not in x_words:
+                name = "x_words_%d_%d" % (g, first)
+                x_words[g, first] = keep.tile([P, end - first], U32, name=name, tag=tag or name, align_bytes=64)
+                x_scales[g, first] = keep.tile([P, end - first], U8, name="x_scales_%d_%d" % (g, first), align_bytes=64)
             nc.vector.quantize_mx(
-                out=x_words[g, e0][:].bitcast(FP8X4),
-                scales=x_scales[g, e0][:],
+                out=x_words[g, first][:, e0 - first : e1 - first].bitcast(FP8X4),
+                scales=x_scales[g, first][:, e0 - first : e1 - first],
                 in_=woven[g, e0][:].rearrange("p c j -> p (c j)"),
             )
 
         w_words = {}
         w_scales = {}
 
-        def round_w(g, t0, tiles, vector_columns):
-            rounded = keep.tile([P, tiles, P, PACK], BF16, name="w_bf_%d_%d" % (g, t0), tag="w_bf_%d_%d" % (g, t0), align_bytes=64)
+        def round_w(g, t0, vector_columns):
+            name = "w_bf_%d_%d" % (g, t0)
+            rounded = keep.tile([P, 2, P, PACK], BF16, name=name, tag=name, align_bytes=64)
             dst = rounded[:].rearrange("p t m j -> p m j t")
-            src = w_raw[g][:].rearrange("p (j m t) -> p m j t", m=P, t=PACK)[:, :, :, t0 : t0 + tiles]
+            src = w_raw[g][:].rearrange("p (j m t) -> p m j t", m=P, t=PACK)[:, :, :, t0 : t0 + 2]
             if vector_columns > 0:
                 nc.vector.tensor_copy(out=dst[:, :vector_columns, :, :], in_=src[:, :vector_columns, :, :])
-            nc.scalar.activation(out=dst[:, vector_columns:, :, :], in_=src[:, vector_columns:, :, :], func=ACT.Copy)
+            if vector_columns < P:
+                nc.scalar.activation(out=dst[:, vector_columns:, :, :], in_=src[:, vector_columns:, :, :], func=ACT.Copy)
             return rounded
 
         def quantize_w(g, t0, rounded, step):
@@ -138,7 +138,7 @@ def tile_picked_deepset_relu_e_kernel(tc, xT, w1, w2_words, w2_scales, offs, out
                 banks[t, half] = psum.tile([P, HALF], F32, name="bank_%d" % (2 * t + half))
 
         def product(g, t, half):
-            parts = [(e0, e1) for engine, e0, e1 in STRETCHES[g] if e0 // HALF == half]
+            parts = [(e0, e1) for e0, e1 in OPERANDS[g] if e0 // HALF == half]
             for e0, e1 in parts:
                 nc.tensor.matmul_mx(
                     out=banks[t, half][:, e0 - half * HALF : e1 - half * HALF],
@@ -156,15 +156,18 @@ def tile_picked_deepset_relu_e_kernel(tc, xT, w1, w2_words, w2_scales, offs, out
             quantize_x(0, e0, e1)
         for plane in range(PACK, PLANES - 1):
             gather(plane)
-        quantize_w(0, 0, round_w(0, 0, PACK, W_VECTOR)[:], 1)
+        first_pair = round_w(0, 0, P)
+        second_pair = round_w(0, 2, FILL)
+        quantize_w(0, 0, first_pair[:], 1)
+        quantize_w(0, 2, second_pair[:], 2)
         for t in range(PACK):
             for half in range(2):
                 product(0, t, half)
         gather(PLANES - 1)
-        for engine, e0, e1 in (STRETCHES[1][1], STRETCHES[1][0]):
+        for engine, e0, e1 in (STRETCHES[1][1], STRETCHES[1][0], STRETCHES[1][2]):
             quantize_x(1, e0, e1)
-        first_pair = round_w(1, 0, 2, FIRST_PAIR_VECTOR)
-        second_pair = round_w(1, 2, 2, SECOND_PAIR_VECTOR)
+        first_pair = round_w(1, 0, P)
+        second_pair = round_w(1, 2, FILL)
         quantize_w(1, 0, first_pair[:], 1)
         quantize_x(1, S - QUARTER, S, "w_bf_1_0")
 
@@ -213,9 +216,9 @@ def tile_picked_deepset_relu_e_kernel(tc, xT, w1, w2_words, w2_scales, offs, out
         center("scalar", 2, LAST, S)
         center("vector", 2, 0, LAST)
         center("scalar", 3, LAST, S)
-        center("scalar", 3, LAST - EIGHTH, LAST)
+        center("scalar", 3, HALF, LAST)
         center("vector", 3, 0, QUARTER)
-        center("vector", 3, QUARTER, LAST - EIGHTH)
+        center("vector", 3, QUARTER, HALF)
 
         def interleave(engine, dst, src):
             dst = dst.rearrange("p (c i) j -> p c j i", i=LINE)
@@ -225,28 +228,27 @@ def tile_picked_deepset_relu_e_kernel(tc, xT, w1, w2_words, w2_scales, offs, out
             else:
                 nc.scalar.copy(out=dst, in_=src)
 
-        grouped = [keep.tile([P, QUARTER, PACK], BF16, name="z_bf_%d" % q, align_bytes=64) for q in range(4)]
+        vector_runs = ((0, QUARTER), (QUARTER, QUARTER))
+        scalar_runs = ((LAST, QUARTER), (HALF, EIGHTH), (HALF + EIGHTH, EIGHTH))
 
-        def weave_z(engine, q, c0, c1):
-            interleave(engine, grouped[q][:, c0:c1, :], z_planes[:, :, q * QUARTER + c0 : q * QUARTER + c1])
+        def weave_z(engine, c0, width):
+            grouped = keep.tile([P, width, PACK], BF16, name="z_bf_%d" % c0, align_bytes=64)
+            interleave(engine, grouped[:], z_planes[:, :, c0 : c0 + width])
+            return grouped
 
-        def quantize_z(q):
-            z_words = keep.tile([P, QUARTER], U32, name="z_words_%d" % q, align_bytes=64)
-            z_scales = keep.tile([P, QUARTER], U8, name="z_scales_%d" % q, align_bytes=64)
+        def second_product(c0, width, grouped):
+            z_words = keep.tile([P, width], U32, name="z_words_%d" % c0, align_bytes=64)
+            z_scales = keep.tile([P, width], U8, name="z_scales_%d" % c0, align_bytes=64)
             nc.vector.quantize_mx(
-                out=z_words[:].bitcast(FP8X4), scales=z_scales[:], in_=grouped[q][:].rearrange("p c j -> p (c j)")
+                out=z_words[:].bitcast(FP8X4), scales=z_scales[:], in_=grouped[:].rearrange("p c j -> p (c j)")
             )
-            return z_words, z_scales
-
-        def second_product(c0, width, z_words, z_scales):
             acc = psum.tile([P, width], F32, name="bank_%d" % (c0 // EIGHTH))
-            cols = slice(c0 % QUARTER, c0 % QUARTER + width)
             nc.tensor.matmul_mx(
                 out=acc[:],
                 lhsT=w2_codes[:].bitcast(FP4X4),
                 lhsT_scale=w2_scale[:],
-                rhs=z_words[:, cols].bitcast(FP8X4),
-                rhs_scale=z_scales[:, cols],
+                rhs=z_words[:].bitcast(FP8X4),
+                rhs_scale=z_scales[:],
                 start=True,
                 stop=True,
             )
@@ -260,14 +262,16 @@ def tile_picked_deepset_relu_e_kernel(tc, xT, w1, w2_words, w2_scales, offs, out
                 nc.scalar.activation(out=result[:], in_=acc[:], func=ACT.Copy, scale=-1.0 / S)
             nc.sync.dma_start(out=out[:, c0 : c0 + width], in_=result[:])
 
-        weave_z("scalar", 3, 0, QUARTER)
-        weave_z("scalar", 2, THIRD_VECTOR, QUARTER)
-        weave_z("vector", 0, 0, QUARTER)
-        weave_z("vector", 1, 0, QUARTER)
-        weave_z("vector", 2, 0, THIRD_VECTOR)
-        for q in (0, 3, 1):
-            acc = second_product(q * QUARTER, QUARTER, *quantize_z(q))
-            store("scalar", q * QUARTER, QUARTER, acc)
-        codes = quantize_z(2)
-        for engine, c0 in (("scalar", HALF), ("vector", HALF + EIGHTH)):
-            store(engine, c0, EIGHTH, second_product(c0, EIGHTH, *codes))
+        z_bf = {}
+        for c0, width in scalar_runs:
+            z_bf[c0] = weave_z("scalar", c0, width)
+        for c0, width in vector_runs:
+            z_bf[c0] = weave_z("vector", c0, width)
+        runs = vector_runs + scalar_runs
+        acc = {}
+        for c0, width in runs:
+            acc[c0] = second_product(c0, width, z_bf[c0])
+        for c0, width in runs[:-1]:
+            store("scalar", c0, width, acc[c0])
+        c0, width = runs[-1]
+        store("vector", c0, width, acc[c0])

@@ -28,7 +28,8 @@ QUARTER = S // 4
 EIGHTH = S // 8
 LINE = 4
 
-FILL = 40
+FILL = 56
+FIRST = 80
 LAST = S - QUARTER
 
 STRETCHES = (
@@ -166,7 +167,7 @@ def tile_picked_deepset_relu_e_kernel(tc, xT, w1, w2_words, w2_scales, offs, out
         gather(PLANES - 1)
         for engine, e0, e1 in (STRETCHES[1][1], STRETCHES[1][0], STRETCHES[1][2]):
             quantize_x(1, e0, e1)
-        first_pair = round_w(1, 0, P)
+        first_pair = round_w(1, 0, FIRST)
         second_pair = round_w(1, 2, FILL)
         quantize_w(1, 0, first_pair[:], 1)
         quantize_x(1, S - QUARTER, S, "w_bf_1_0")

@@ -29,7 +29,7 @@ EIGHTH = S // 8
 LINE = 4
 
 FILL = 56
-FIRST = 80
+FIRST = 76
 LAST = S - QUARTER
 
 STRETCHES = (
@@ -157,7 +157,7 @@ def tile_picked_deepset_relu_e_kernel(tc, xT, w1, w2_words, w2_scales, offs, out
             quantize_x(0, e0, e1)
         for plane in range(PACK, PLANES - 1):
             gather(plane)
-        first_pair = round_w(0, 0, P)
+        first_pair = round_w(0, 0, FIRST)
         second_pair = round_w(0, 2, FILL)
         quantize_w(0, 0, first_pair[:], 1)
         quantize_w(0, 2, second_pair[:], 2)
@@ -215,10 +215,11 @@ def tile_picked_deepset_relu_e_kernel(tc, xT, w1, w2_words, w2_scales, offs, out
         add_sums(3)
         center("vector", 1, 0, LAST)
         center("scalar", 2, LAST, S)
-        center("vector", 2, 0, LAST)
+        center("vector", 2, 0, HALF)
         center("scalar", 3, LAST, S)
         center("scalar", 3, HALF, LAST)
         center("vector", 3, 0, QUARTER)
+        center("vector", 2, HALF, LAST)
         center("vector", 3, QUARTER, HALF)
 
         def interleave(engine, dst, src):
@@ -261,7 +262,8 @@ def tile_picked_deepset_relu_e_kernel(tc, xT, w1, w2_words, w2_scales, offs, out
                 nc.vector.tensor_scalar(out=result[:], in0=acc[:], scalar1=-1.0 / S, scalar2=None, op0=ALU.mult)
             else:
                 nc.scalar.activation(out=result[:], in_=acc[:], func=ACT.Copy, scale=-1.0 / S)
-            nc.sync.dma_start(out=out[:, c0 : c0 + width], in_=result[:])
+            queue = nc.scalar if (c0, width) == scalar_runs[1] else nc.sync
+            queue.dma_start(out=out[:, c0 : c0 + width], in_=result[:])
 
         z_bf = {}
         for c0, width in scalar_runs:

from contextlib import ExitStack

import concourse.mybir as mybir

K, T, S, H, N = 1024, 2048, 1024, 512, 128
FLOPS = 2 * S * H * (K + N)

F32 = mybir.dt.float32
BF16 = mybir.dt.bfloat16
I32 = mybir.dt.int32
U32 = mybir.dt.uint32
U16 = mybir.dt.uint16
U8 = mybir.dt.uint8
FP8X4 = mybir.dt.float8_e4m3fn_x4
FP4X4 = mybir.dt.float4_e2m1fn_x4
ACT = mybir.ActivationFunctionType
ALU = mybir.AluOpType

P = 128
PACK = 4
K_PASS = P * PACK
PASSES = K // K_PASS
PLANES = PASSES * PACK
LIST_ROWS = 16
SCALE_ROWS = 4
HALF = S // 2
QUARTER = S // 4
EIGHTH = S // 8
LINE = 4

FILL = 56
FIRST = 76
LAST = S - QUARTER

STRETCHES = (
    (("vector", 0, HALF), ("scalar", HALF, S)),
    (("vector", 0, 3 * EIGHTH), ("scalar", 3 * EIGHTH, HALF), ("scalar", HALF, LAST), ("scalar", LAST, S)),
)
OPERANDS = (((0, HALF), (HALF, S)), ((0, HALF), (HALF, LAST), (LAST, S)))


def tile_picked_deepset_relu_e_kernel(tc, xT, w1, w2_words, w2_scales, offs, out):
    nc = tc.nc
    with ExitStack() as ctx:
        keep = ctx.enter_context(tc.tile_pool(name="keep", bufs=1))
        psum = ctx.enter_context(tc.psum_pool(name="psum", bufs=1))

        offsets = keep.tile([P, S // LIST_ROWS], U16, name="offsets")
        w2_scale = keep.tile([P, N], U8, name="w2_scale", align_bytes=64)
        w2_codes = keep.tile([P, 2 * N], U8, name="w2_codes", align_bytes=64)
        nc.vector.memset(w2_scale[:].bitcast(I32), 0)

        x_raw = []
        w_raw = []

        def load_w(g):
            raw = keep.tile([P, PACK * H], F32, name="w_raw_%d" % g, align_bytes=256)
            nc.sync.dma_start(out=raw[:], in_=w1[g * K_PASS : (g + 1) * K_PASS, :].rearrange("(p j) c -> p (j c)", j=PACK))
            w_raw.append(raw)

        for plane in range(PLANES):
            g, j = divmod(plane, PACK)
            if plane == PLANES - 1:
                load_w(0)
            rows = xT[g * K_PASS : (g + 1) * K_PASS, :].rearrange("(p j) c -> p j c", j=PACK)
            raw = keep.tile([P, T], F32, name="x_raw_%d" % plane, align_bytes=256)
            nc.sync.dma_start(out=raw[:], in_=rows[:, j, :])
            x_raw.append(raw)
            if plane == 0:
                nc.sync.dma_start(offsets[:], offs)
        load_w(1)
        nc.sync.dma_start(out=w2_codes[:].bitcast(I32), in_=w2_words[0].bitcast(I32))
        for q in range(P // 32):
            nc.sync.dma_start(
                out=w2_scale[32 * q : 32 * q + SCALE_ROWS, :].bitcast(I32),
                in_=w2_scales[0, SCALE_ROWS * q : SCALE_ROWS * (q + 1), :].bitcast(I32),
            )

        woven = {}
        for g in range(PASSES):
            for engine, e0, e1 in STRETCHES[g]:
                woven[g, e0] = keep.tile([P, e1 - e0, PACK], BF16, name="x_bf_%d_%d" % (g, e0), align_bytes=64)
        x_words = {}
        x_scales = {}

        def gather(plane):
            g, j = divmod(plane, PACK)
            for engine, e0, e1 in STRETCHES[g]:
                window = x_raw[plane][:].indirect(offsets[:, e0 // LIST_ROWS : e1 // LIST_ROWS])
                if engine == "vector":
                    nc.vector.tensor_copy(out=woven[g, e0][:, :, j], in_=window)
                else:
                    nc.scalar.activation(out=woven[g, e0][:, :, j], in_=window, func=ACT.Copy)

        def quantize_x(g, e0, e1, tag=None):
            first, end = [run for run in OPERANDS[g] if run[0] <= e0 < run[1]][0]
            if (g, first) not in x_words:
                name = "x_words_%d_%d" % (g, first)
                x_words[g, first] = keep.tile([P, end - first], U32, name=name, tag=tag or name, align_bytes=64)
                x_scales[g, first] = keep.tile([P, end - first], U8, name="x_scales_%d_%d" % (g, first), align_bytes=64)
            nc.vector.quantize_mx(
                out=x_words[g, first][:, e0 - first : e1 - first].bitcast(FP8X4),
                scales=x_scales[g, first][:, e0 - first : e1 - first],
                in_=woven[g, e0][:].rearrange("p c j -> p (c j)"),
            )

        w_words = {}
        w_scales = {}

        def round_w(g, t0, vector_columns):
            name = "w_bf_%d_%d" % (g, t0)
            rounded = keep.tile([P, 2, P, PACK], BF16, name=name, tag=name, align_bytes=64)
            dst = rounded[:].rearrange("p t m j -> p m j t")
            src = w_raw[g][:].rearrange("p (j m t) -> p m j t", m=P, t=PACK)[:, :, :, t0 : t0 + 2]
            if vector_columns > 0:
                nc.vector.tensor_copy(out=dst[:, :vector_columns, :, :], in_=src[:, :vector_columns, :, :])
            if vector_columns < P:
                nc.scalar.activation(out=dst[:, vector_columns:, :, :], in_=src[:, vector_columns:, :, :], func=ACT.Copy)
            return rounded

        def quantize_w(g, t0, rounded, step):
            tiles = rounded.shape[1]
            words = keep.tile([P, tiles * P], U32, name="w_words_%d_%d" % (g, t0), align_bytes=64)
            scales = keep.tile([P, tiles * P], U8, name="w_scales_%d_%d" % (g, t0), align_bytes=64)
            for t in range(0, tiles, step):
                cols = slice(t * P, (t + step) * P)
                nc.vector.quantize_mx(
                    out=words[:, cols].bitcast(FP8X4),
                    scales=scales[:, cols],
                    in_=rounded[:, t : t + step, :, :].rearrange("p t m j -> p (t m j)"),
                )
            for t in range(tiles):
                w_words[g, t0 + t] = words[:, t * P : (t + 1) * P]
                w_scales[g, t0 + t] = scales[:, t * P : (t + 1) * P]

        banks = {}
        for t in range(PACK):
            for half in range(2):
                banks[t, half] = psum.tile([P, HALF], F32, name="bank_%d" % (2 * t + half))

        def product(g, t, half):
            parts = [(e0, e1) for e0, e1 in OPERANDS[g] if e0 // HALF == half]
            for e0, e1 in parts:
                nc.tensor.matmul_mx(
                    out=banks[t, half][:, e0 - half * HALF : e1 - half * HALF],
                    lhsT=w_words[g, t].bitcast(FP8X4),
                    lhsT_scale=w_scales[g, t],
                    rhs=x_words[g, e0][:].bitcast(FP8X4),
                    rhs_scale=x_scales[g, e0][:],
                    start=(g == 0),
                    stop=(g == PASSES - 1 and e1 % HALF == 0),
                )

        for plane in range(PACK):
            gather(plane)
        for engine, e0, e1 in STRETCHES[0]:
            quantize_x(0, e0, e1)
        for plane in range(PACK, PLANES - 1):
            gather(plane)
        first_pair = round_w(0, 0, FIRST)
        second_pair = round_w(0, 2, FILL)
        quantize_w(0, 0, first_pair[:], 1)
        quantize_w(0, 2, second_pair[:], 2)
        for t in range(PACK):
            for half in range(2):
                product(0, t, half)
        gather(PLANES - 1)
        for engine, e0, e1 in (STRETCHES[1][1], STRETCHES[1][0], STRETCHES[1][2]):
            quantize_x(1, e0, e1)
        first_pair = round_w(1, 0, FIRST)
        second_pair = round_w(1, 2, FILL)
        quantize_w(1, 0, first_pair[:], 1)
        quantize_x(1, S - QUARTER, S, "w_bf_1_0")

        h = [keep.tile([P, S], F32, name="h_%d" % t) for t in range(PACK)]
        sums = [keep.tile([P, 2], F32, name="sums_%d" % t) for t in range(PACK)]
        total = [keep.tile([P, 1], F32, name="total_%d" % t) for t in range(PACK)]
        z_planes = keep.tile([P, PACK, S], BF16, name="z_planes")

        def empty(engine, t, half, into, start=None):
            dst = h[t][:, half * HALF : (half + 1) * HALF]
            if engine == "scalar":
                nc.scalar.activation(out=dst, in_=banks[t, half][:], func=ACT.Relu, accum_out=into)
            else:
                nc.vector.tensor_scalar(
                    out=dst, in0=banks[t, half][:], scalar1=0.0, scalar2=start, op0=ALU.max, op1=ALU.add, accum_out=into
                )

        def add_sums(t):
            nc.scalar.activation(out=total[t][:], in_=sums[t][:, 0:1], func=ACT.Identity, bias=sums[t][:, 1:2])

        def center(engine, t, c0, c1):
            if engine == "vector":
                nc.vector.tensor_scalar(
                    out=z_planes[:, t, c0:c1], in0=h[t][:, c0:c1], scalar1=-float(S), scalar2=total[t][:], op0=ALU.mult, op1=ALU.add
                )
            else:
                nc.scalar.activation(out=z_planes[:, t, c0:c1], in_=h[t][:, c0:c1], func=ACT.Identity, bias=total[t][:], scale=-float(S))

        quantize_w(1, 2, second_pair[:], 2)
        for t, half in ((0, 0), (1, 0), (1, 1), (0, 1), (2, 0), (2, 1), (3, 0), (3, 1)):
            product(1, t, half)
        empty("scalar", 0, 0, sums[0][:, 0:1])
        empty("vector", 1, 0, sums[1][:, 0:1])
        empty("scalar", 1, 1, sums[1][:, 1:2])
        empty("vector", 0, 1, total[0][:], sums[0][:, 0:1])
        empty("scalar", 2, 0, sums[2][:, 0:1])
        empty("vector", 2, 1, sums[2][:, 1:2])
        add_sums(1)
        empty("scalar", 3, 0, sums[3][:, 0:1])
        add_sums(2)
        empty("scalar", 3, 1, sums[3][:, 1:2])
        center("vector", 0, 0, S)
        center("scalar", 1, LAST, S)
        add_sums(3)
        center("vector", 1, 0, LAST)
        center("scalar", 2, LAST, S)
        center("vector", 2, 0, HALF)
        center("scalar", 3, LAST, S)
        center("scalar", 3, HALF, LAST)
        center("vector", 3, 0, QUARTER)
        center("vector", 2, HALF, LAST)
        center("vector", 3, QUARTER, HALF)

        def interleave(engine, dst, src):
            dst = dst.rearrange("p (c i) j -> p c j i", i=LINE)
            src = src.rearrange("p j (c i) -> p c j i", i=LINE)
            if engine == "vector":
                nc.vector.tensor_copy(out=dst, in_=src)
            else:
                nc.scalar.copy(out=dst, in_=src)

        vector_runs = ((0, QUARTER), (QUARTER, QUARTER))
        scalar_runs = ((LAST, QUARTER), (HALF, EIGHTH), (HALF + EIGHTH, EIGHTH))

        def weave_z(engine, c0, width):
            grouped = keep.tile([P, width, PACK], BF16, name="z_bf_%d" % c0, align_bytes=64)
            interleave(engine, grouped[:], z_planes[:, :, c0 : c0 + width])
            return grouped

        def second_product(c0, width, grouped):
            z_words = keep.tile([P, width], U32, name="z_words_%d" % c0, align_bytes=64)
            z_scales = keep.tile([P, width], U8, name="z_scales_%d" % c0, align_bytes=64)
            nc.vector.quantize_mx(
                out=z_words[:].bitcast(FP8X4), scales=z_scales[:], in_=grouped[:].rearrange("p c j -> p (c j)")
            )
            acc = psum.tile([P, width], F32, name="bank_%d" % (c0 // EIGHTH))
            nc.tensor.matmul_mx(
                out=acc[:],
                lhsT=w2_codes[:].bitcast(FP4X4),
                lhsT_scale=w2_scale[:],
                rhs=z_words[:].bitcast(FP8X4),
                rhs_scale=z_scales[:],
                start=True,
                stop=True,
            )
            return acc

        def store(engine, c0, width, acc):
            result = keep.tile([P, width], F32, name="result_%d" % c0, align_bytes=256)
            if engine == "vector":
                nc.vector.tensor_scalar(out=result[:], in0=acc[:], scalar1=-1.0 / S, scalar2=None, op0=ALU.mult)
            else:
                nc.scalar.activation(out=result[:], in_=acc[:], func=ACT.Copy, scale=-1.0 / S)
            queue = nc.scalar if (c0, width) == scalar_runs[1] else nc.sync
            queue.dma_start(out=out[:, c0 : c0 + width], in_=result[:])

        z_bf = {}
        for c0, width in scalar_runs:
            z_bf[c0] = weave_z("scalar", c0, width)
        for c0, width in vector_runs:
            z_bf[c0] = weave_z("vector", c0, width)
        runs = vector_runs + scalar_runs
        acc = {}
        for c0, width in runs:
            acc[c0] = second_product(c0, width, z_bf[c0])
        for c0, width in runs[:-1]:
            store("scalar", c0, width, acc[c0])
        c0, width = runs[-1]
        store("vector", c0, width, acc[c0])
